import numpy as np, ml_dtypes
CORES = [16,18,20,22]
N = 4
import mx_ref
BF = ml_dtypes.bfloat16
def cols(t, e):
    v = np.concatenate([t.reshape(128, -1, 4), np.zeros((128, 1, 4), BF)], axis=1)
    return np.ascontiguousarray(v[:, e]).reshape(128, -1)
def cut(t, i, w=512):
    return t[:, w * i:w * i + w]
def tile(rs):
    return np.stack(rs, axis=2).reshape(128, -1).astype(BF)
def pick(q, e):
    c = np.concatenate([q[0].reshape(128, -1, 4), np.zeros((128, 1, 4), np.uint8)], axis=1); s = np.concatenate([q[1], np.ones((16, 1), np.uint8)], axis=1)
    return (np.ascontiguousarray(c[:, e].reshape(128, -1)), np.ascontiguousarray(s[:, e]))
def join(*qs):
    return (np.concatenate([q[0] for q in qs], axis=1), np.concatenate([q[1] for q in qs], axis=1))
def put(q, e, v):
    c, s = q[0].reshape(128, -1, 4).copy(), q[1].copy(); c[:, e] = v[0].reshape(128, -1, 4); s[:, e] = v[1]
    return (c.reshape(128, -1), s)
def pk(c, s):
    return (np.ascontiguousarray(c), mx_ref.live(s))
def emit(q):
    return q[0], q[1]
def decode(q):
    o = []
    for b in range(4):
        e = np.zeros((128, 128, 4), np.float32); e[np.arange(128), np.arange(128), b] = 1
        o.append(mx_ref.matmul(mx_ref.quantize(e.reshape(128, 512).astype(BF)), q))
    return np.stack(o, axis=2).reshape(128, -1)
def f(rng, *shape):
    return mx_ref.flush((rng.standard_normal(shape, dtype=np.float32) * np.exp2(rng.integers(-2, 3, shape[:-1] + (1,)))).astype(BF))
def wide(rng, *shape, cols=0):
    v = rng.standard_normal(shape, dtype=np.float32) * np.exp2(rng.integers(-12, 13, shape)).astype(np.float32)
    if cols: v *= np.repeat(np.exp2(rng.integers(-cols, cols + 1, shape[:-2] + (1, shape[-1] // 4))) * (rng.random(shape[:-2] + (1, shape[-1] // 4)) > 0.0625), 4, axis=-1).astype(np.float32)
    return mx_ref.flush(v.astype(BF))
T, A, KM, CAPP, FA = 192, 32, 64, 32, 2
def big(t):
    t = np.array(t)
    t[np.abs(t.astype(np.float32)) < np.float32(2.0 ** -16)] = 0
    return t
def plain(rng):
    x = np.concatenate([f(rng, N, 128, 4 * A), f(rng, N, 128, 4 * (T - A))], axis=2)
    return {"x": big(x), "w": f(rng, N, 128, 2048), "v": f(rng, N, 128, 512)}
def pull(rng, x, at, who, n=8, bare=False):
    x = np.array(x).reshape(N, 128, T, 4)
    x[:, :n * len(at)] = 0
    for i, (q, a) in enumerate(at):
        if bare: x[q, :, a] = 0
        x[q, n * i:n * i + n, a] = (32 * (1 + rng.random((n, 4)))).astype(np.float32).astype(BF)
        r, j = np.nonzero(who == i)
        x[r, n * i:n * i + n, j] = (8 * (1 + rng.random((len(r), n, 4)))).astype(np.float32).astype(BF)
    return x.reshape(N, 128, 4 * T)
def setup_inputs(rng):
    return plain(rng)
def setup_inputs_crowd(rng):
    d, who = plain(rng), np.full((N, T), -1)
    z, q = int(rng.integers(1, N)), rng.permutation(N)[:2]
    for r in range(N):
        e = A + rng.permutation(T - A)[:KM * 5 // 6 + FA]
        who[r, e] = 0
        who[r, e[:FA]] = 1
    who[z, A:] = rng.integers(0, 2, T - A)
    d["x"] = pull(rng, d["x"], [(int(q[i]), int(rng.integers(0, A))) for i in range(2)], who)
    return d
def setup_inputs_full(rng):
    d, who, o = plain(rng), np.full((N, T), -1), rng.permutation(N)
    g = FA * A // CAPP
    e = np.tile(rng.permutation(A), FA).reshape(g, CAPP)
    for i, s in enumerate(np.sort(o[1:g + 1])):
        who[s, A:A + CAPP] = rng.permutation(e[i])
        who[s, A + CAPP:A + CAPP + 4] = e[-1, -1]
    d["x"] = pull(rng, d["x"], [(int(o[0]), a) for a in range(A)], who, 2, True)
    return d
def setup_inputs_ties(rng):
    d = plain(rng)
    x = np.array(d["x"])
    part = np.arange(128) // 8
    m = rng.permutation(N * A) % (N * A // 4)
    k = cols(np.concatenate([x[q][:, :4 * A] for q in range(N)], axis=1), rng.permutation(N * A)[m])
    k = np.abs(k.astype(np.float32)) * np.repeat(np.where(part[:, None] == m % 16, 2.0 ** -8, 1.0), 4, axis=1)
    k = big(k.astype(np.float32).astype(BF))
    for r in range(N):
        g = rng.permutation(np.arange(T - A) // 7)
        u = cols(np.ascontiguousarray(x[r][:, 4 * A:]), g)
        if r == 0:
            on = part[:, None] == (m[0] + 1 + g % 15) % 16
            u = (-np.abs(u.astype(np.float32)) * np.repeat(on, 4, axis=1)).astype(BF)
        if r == 1:
            u = np.abs(u.astype(np.float32)).reshape(128, T - A, 4)
            o = np.append(0, 1 + rng.permutation(T - A - 1)[KM // 2:])
            u[:, o[::2]] = -0.0
            u[:, o[1::2]] = 0.0
            u = u.astype(BF).reshape(128, -1)
        x[r][:, 4 * A:] = u
        x[r][:, :4 * A] = cut(k, r, 4 * A)
    d["x"] = x
    return d
def setup_inputs_own(rng):
    d = plain(rng)
    x = np.array(d["x"])
    x[:, :, 2 * A:4 * A] = -x[:, :, :2 * A]
    x[(np.arange(128) // (128 // N))[None, :] != np.arange(N)[:, None]] = 0
    d["x"] = x
    return d
def setup_inputs_spread(rng):
    return {**plain(rng), "x": big(wide(rng, N, 128, 4 * T, cols=4))}
def check_inputs(d):
    b = []
    for k in ("x", "w", "v"):
        t = np.abs(d[k].astype(np.float32))
        if not (np.isfinite(t).all() and ((t == 0) | (t >= 2.0 ** -30) & (t <= 2.0 ** 30)).all()): b.append("a value of " + k)
    return b
def choose(x):
    k = np.concatenate([x[q][:, :4 * A] for q in range(N)], axis=1)
    k = [mx_ref.quantize(np.ascontiguousarray(cut(k, i))) for i in range(N * A // 128)]
    goal, took, have = np.full((N, T), -1), np.full((N, A, FA), -1), np.zeros((N, A), int)
    for s in range(N):
        u = mx_ref.quantize(np.ascontiguousarray(x[s][:, 4 * A:]))
        z = np.concatenate([mx_ref.matmul(t, u) for t in k]) + np.float32(0.0)
        best = np.argmax(z, axis=0)
        offers = np.sort(np.argsort(-z.max(axis=0), kind="stable")[:KM])
        stand = np.zeros(N, int)
        for j in offers:
            q, a = best[j] // A, best[j] % A
            if stand[q] == CAPP: continue
            stand[q] += 1
            if have[q, a] == FA: continue
            took[q, a, have[q, a]] = s * T + A + j
            have[q, a] += 1
            goal[s, A + j] = q * T + a
    return goal, took
def reference(x, w, v):
    goal, took = choose(x)
    c = [mx_ref.quantize(np.ascontiguousarray(x[r])) for r in range(N)]
    d = np.concatenate([decode(c[r]).reshape(128, T, 4) for r in range(N)], axis=1)
    h = []
    for q in range(N):
        m = d[:, q * T:q * T + A].copy()
        for t in range(FA):
            a = np.flatnonzero(took[q, :, t] >= 0)
            m[:, a] = m[:, a] + d[:, took[q, a, t]]
        new = mx_ref.quantize(np.ascontiguousarray((m * np.float32(0.5)).reshape(128, -1).astype(BF)))
        a = np.flatnonzero(took[q, :, 0] >= 0)
        k = put(c[q], a, pick(new, a))
        rs = [np.maximum(mx_ref.matmul(mx_ref.quantize(np.ascontiguousarray(cut(w[q], i))), k), np.float32(0.0)) * np.float32(0.0625) for i in range(4)]
        h.append(mx_ref.quantize(np.ascontiguousarray(tile(rs))))
    every = join(*h)
    oc, osc = np.zeros((N, 128, 4 * T), np.uint8), np.zeros((N, 16, T), np.uint8)
    mg, y = np.zeros((N, 1, T), np.float32), np.zeros((N, 128, T), np.float32)
    for s in range(N):
        g = pick(every, np.where(goal[s] >= 0, goal[s], s * T + np.arange(T)))
        oc[s], osc[s] = emit(g)
        mg[s, 0] = goal[s]
        y[s] = mx_ref.matmul(mx_ref.quantize(np.ascontiguousarray(v[s])), g)
    return {"oc": oc, "osc": osc, "mg": mg, "y": y}

@@ -1,0 +1,450 @@
+from concourse.bass import DstId, RemoteDMATransfer
+from concourse.mybir import dt, AluOpType as Op, AxisListType, ActivationFunctionType as Act
+
+A = 32
+F, B16, I32, U16, CODE, PL = "float32", "bfloat16", "int32", "uint16", "float8_e4m3fn_x4", "uint8"
+
+SCRATCH = {}
+
+
+def _sb(dtype, **names):
+    for n, w in names.items():
+        SCRATCH[n] = ("sbuf", [128, w], dtype)
+
+
+def _mx(**names):
+    for n, w in names.items():
+        SCRATCH[n + "q"] = ("sbuf", [128, w], CODE)
+        SCRATCH[n + "p"] = ("sbuf", [128, w], PL)
+
+
+SCRATCH["psum"] = ("psum", [128, 4096], F)
+_sb(I32, pidi=1, ui=1)
+_sb(F, cst=16, row=160, kc=16, kx=16, rli=40, colw=12, colm=12, lneg=320, ones=32, zer=128, rst=160, mgt=320,
+    rmax=256, m5=8, rep=160, mrow=160, th=320, jnk=256, tiny=64, tri=256,
+    da=128, uu=128, dw=10, crow=128, prior=160, adm=160, scn=160, admt=10, fin=12, fm=2, mgr=192, yo=192)
+_sb(B16, rowb=128, k16=256, kst=256, iden=128, et=2048, trt=1024, s3t=512, zt=512, xz=512, xt=768, wt=2048, vt=512,
+    cc=320, cj=160, ot=528, mmt=640, stt=512, s2t=512, m2t=512, tmt=688, mt=512, hmt=512, hot=768,
+    lst=16, nz=16, csum=8, ll=32, lc=24, la16=16, lb16=16, lu=8, lcm=2, lf=2, lg=2, ctot=8)
+_sb(U16, rlu=40, colu=12, invu=8, off=4, gwu=10, cu=8, finu=12)
+_mx(e=512, tr=256, s3=128, a=128, x=192, k=128, r=640, w=512, v=128, ob=132, mm=160, st=128, s2=128, m2=128, tm=172,
+    sl=96, win=160, fs=128, m=128, hm=128, hw=320, fo=192)
+
+SEMAPHORES = ["qv", "qs", "qt", "qg", "dxa", "dx", "dw", "dv", "an", "so", "li", "ct", "hm", "la", "lb", "dout"]
+_TINY = {n: 2 * i for i, n in enumerate(["ab", "ab2", "cn", "sel", "gg", "gd", "gq", "gm", "gd16", "gd64", "yy", "lpv",
+                                         "key", "hia", "hib", "hi", "ylo", "lo", "thz", "thy", "thr"])}
+
+
+def rank_program(g, core, T, topo):
+    s = T.rank_of(core)
+    if s is None:
+        return
+    others = [r for r in range(4) if r != s]
+    order = others + [s]
+    Q = {"v": g.vector, "s": g.scalar, "t": g.tensor, "g": g, "y": g.sync}
+    waited, lastw, readers, total = {q: {} for q in Q}, {}, {}, {}
+
+    def wait(q, toks):
+        need = {}
+        for n, val in toks:
+            need[n] = max(need.get(n, 0), val)
+        for n in sorted(need):
+            if waited[q].get(n, 0) < need[n]:
+                Q[q].wait_ge(T.sem[n], need[n])
+                waited[q][n] = need[n]
+
+    def run(q, fn, rd=(), wr=(), sem=None, free=()):
+        toks = []
+        for k in rd:
+            toks += lastw[k]
+        for k in wr:
+            if k not in free:
+                toks += lastw.get(k, []) + readers.get(k, [])
+        wait(q, toks)
+        n, inc = (sem, 16) if sem else ("q" + q, 1)
+        fn().then_inc(T.sem[n], inc)
+        total[n] = total.get(n, 0) + inc
+        tok = (n, total[n])
+        for k in rd:
+            readers.setdefault(k, []).append(tok)
+        for k in wr:
+            lastw[k] = [tok]
+            readers[k] = []
+
+    V, S, P = g.vector, g.scalar, g.tensor
+
+    def vts(out, in0, s1, s2, op0, op1=None, rd=(), wr=()):
+        if op1 is None:
+            run("v", lambda: V.tensor_scalar(out, in0, s1, None, op0), rd, wr)
+        else:
+            run("v", lambda: V.tensor_scalar(out, in0, s1, s2, op0, op1), rd, wr)
+
+    def vtt(out, a, b, op, rd=(), wr=()):
+        run("v", lambda: V.tensor_tensor(out, a, b, op), rd, wr)
+
+    def vcp(out, in_, rd=(), wr=()):
+        run("v", lambda: V.tensor_copy(out, in_), rd, wr)
+
+    def fill(ap, c, *wr):
+        run("v", lambda: V.memset(ap, c), (), wr)
+
+    def vred(out, in_, op, rd=(), wr=()):
+        run("v", lambda: V.tensor_reduce(out, in_, AxisListType.X, op), rd, wr)
+
+    def vscan(out, d0, d1, init, op0, op1, rd=(), wr=()):
+        run("v", lambda: V.tensor_tensor_scan(out, d0, d1, init, op0, op1), rd, wr)
+
+    def act(out, in_, func, rd=(), wr=(), **kw):
+        run("s", lambda: S.activation(out, in_, func, **kw), rd, wr)
+
+    def quant(n, a, b, src, rd=(), wr=None):
+        run("v", lambda: V.quantize_mx(T[n + "q"][:, a:b], T[n + "p"][:, a:b], src), rd, wr or (n + "q", n + "p"))
+
+    def bank(i, a, b=None):
+        return T.psum[:, 512 * i:512 * i + a] if b is None else T.psum[:, 512 * i + a:512 * i + b]
+
+    def mm(i, n, ln, la, rn, ra, start=True, stop=True, rd=None):
+        b = "b%d" % i
+        run("t", lambda: P.matmul_mx(bank(i, n), T[ln + "q"][:, la:la + 128], T[ln + "p"][:, la:la + 128],
+                                     T[rn + "q"][:, ra:ra + n], T[rn + "p"][:, ra:ra + n], start, stop),
+            (ln + "q", ln + "p") + (rd or (rn + "q", rn + "p")), (b,), free=() if start else (b,))
+
+    def pickq(dn, c, d, sn, w, off, rd, wr):
+        run("v", lambda: V.tensor_copy(T[dn + "q"][:, c:d].bitcast(dt.uint32),
+                                       T[sn + "q"][:, 0:w].bitcast(dt.uint32).indirect(off)), rd, wr)
+
+    def pickp(dn, c, d, sn, w, off, rd, wr):
+        run("s", lambda: S.activation(T[dn + "p"][:, c:d], T[sn + "p"][:, 0:w].indirect(off), Act.Copy), rd, wr)
+
+    def tn(n, i=None):
+        c = _TINY[n]
+        return T.tiny[:, c:c + 2] if i is None else T.tiny[:, c + i:c + i + 1]
+
+    def addr(r):
+        rid, pid, _ = topo.addr(T.cores[r])
+        return DstId(rid=rid, pnc=pid)
+
+    def msk(es):
+        return sum(1 << e for e in es)
+
+    lsum = {"la": 0, "lb": 0}
+
+    def bcast(src, dst, sem, local, rd):
+        eng = [e for e in topo.engines(core, T.cores[others[0]])]
+        wait("g", [t for k in rd for t in lastw[k]])
+        g.remote_dma_fused([RemoteDMATransfer(dst_ids=[addr(r) for r in others], dma_engine_mask=msk(eng),
+                                              remote_sem=T.sem[sem], srcs=[src], dsts=[dst] * len(others))],
+                           local_sem=T.sem[local])
+        lsum[local] += len(eng)
+
+    def scatter(srcs, dst, dests, sem, local, rd, first=0):
+        wait("g", [t for k in rd for t in lastw[k]])
+        tr = []
+        for i, (r, src) in enumerate(zip(dests, srcs)):
+            eng = topo.engines(core, T.cores[r])
+            j = 4 * ((first + i) % 4)
+            tr.append(RemoteDMATransfer(dst_ids=[addr(r)], dma_engine_mask=msk(eng[j:j + 4]), remote_sem=T.sem[sem],
+                                        src=src, dst=dst))
+        g.remote_dma_fused(tr, local_sem=T.sem[local])
+        lsum[local] += 4 * len(tr)
+
+    u8 = dt.uint8
+    small = {"allow_small_or_imprecise_dtypes": True}
+
+    run("y", lambda: g.sync.dma_start(T.xz[:, 0:128], T.x[:, 0:128]), (), ("xza",), sem="dxa")
+    run("s", lambda: S.dma_start(T.xt[:, :], T.x[:, :]), (), ("xt",), sem="dx")
+
+    run("g", lambda: g.iota(T.pidi[:], [[0, 1]], 0, 1), (), ("pidi",))
+    run("g", lambda: g.iota(T.row[:], [[1, 160]], 0, 0, **small), (), ("row",))
+    run("g", lambda: g.iota(T.rli[:], [[32, 5], [0, 4], [16, 2]], A, 0, **small), (), ("rli",))
+    run("g", lambda: g.iota(T.colw[:], [[16, 12]], 0, 0, **small), (), ("colw",))
+    run("g", lambda: g.iota(T.k16[:], [[0, 8], [1, 16], [0, 2]], 0, 0, **small), (), ("k16",))
+    run("g", lambda: g.iota(T.kc[:], [[128, 4], [-1, 2], [64, 2]], 32, 0, **small), (), ("kc",))
+
+    def cs(j):
+        return T.cst[:, j:j + 1]
+    fill(T.xz[:, 128:512], 0.0, "xzz")
+    fill(T.zt[:], 0.0, "zt")
+    quant("win", 0, 128, T.zt[:], ("zt",), ("winqz", "winpz"))
+    quant("fs", 0, 128, T.zt[:], ("zt",))
+    fill(T.ll[:], 0.0, "ll")
+    vcp(cs(0), T.pidi[:], ("pidi",), ("c0",))
+    run("v", lambda: V.tensor_scalar(T.ui[:], T.pidi[:], 15, None, Op.bitwise_and), ("pidi",), ("ui",))
+    fill(T.trt[:], 0.0, "trA", "trB")
+    vcp(cs(1), T.ui[:], ("ui",), ("c1",))
+    vts(T.iden[:], T.row[:, 0:128], cs(0), None, Op.is_equal, rd=("row", "c0"), wr=("iden",))
+    vts(T.rlu[:], T.rli[:], cs(1), None, Op.add, rd=("rli", "c1"), wr=("rlu",))
+    vts(T.colw[:], T.colw[:], cs(1), None, Op.add, rd=("c1",), wr=("colw",))
+    vcp(T.colu[:], T.colw[:], ("colw",), ("colu",))
+
+    quant("a", 0, 128, T.xz[:], ("xza", "xzz"))
+    bcast(T.aq[:, 0:A].bitcast(u8), T.kq[:, A * s:A * s + A].bitcast(u8), "an", "la", ("aq",))
+    bcast(T.ap[:, 0:A], T.kp[:, A * s:A * s + A], "an", "la", ("ap",))
+    lastw["kq"] = lastw["kp"] = [("an", 96)]
+    run("g", lambda: g.iota(T.mgt[:, 192:320], [[192, 4], [1, 32]], 0, 0, **small), (), ("mgtb",))
+    wait("y", [("la", lsum["la"])])
+    run("y", lambda: g.sync.dma_start(T.wt[:, :], T.w[:, :]), (), ("wt",), sem="dw")
+    run("y", lambda: g.sync.dma_start(T.vt[:, :], T.v[:, :]), (), ("vt",), sem="dv")
+
+    quant("x", 0, 192, T.xt[:], ("xt",))
+    own = (A * s, A * s + A)
+    pickq("k", own[0], own[1], "a", 128, T.colu[:, 0:2], ("aq", "colu"), ("kqo",))
+    pickp("k", own[0], own[1], "a", 128, T.colu[:, 0:2], ("ap", "colu"), ("kpo",))
+    pickq("r", 0, 640, "x", 192, T.rlu[:, 0:40], ("xq", "rlu"), ("rq",))
+    pickp("r", 0, 640, "x", 192, T.rlu[:, 0:40], ("xp", "rlu"), ("rp",))
+    fill(T.ones[:], 1.0, "ones")
+    fill(T.zer[:], 0.0, "zer")
+    vts(cs(2), cs(0), 32.0, None, Op.add, rd=("c0",), wr=("c2",))
+    vts(T.lneg[:, 0:160], T.row[:], cs(0), -1.0, Op.is_lt, Op.mult, rd=("row", "c0"), wr=("lnA",))
+    vts(T.lneg[:, 160:320], T.row[:], cs(2), -1.0, Op.is_lt, Op.mult, rd=("row", "c2"), wr=("lnB",))
+    vcp(T.rowb[:], T.row[:, 0:128], ("row",), ("rowb",))
+    vts(T.tri[:, 0:128], T.row[:, 0:128], cs(0), -1.0, Op.is_gt, Op.mult, rd=("row", "c0"), wr=("tri1",))
+    vts(T.tri[:, 128:256], T.row[:, 0:128], cs(0), 32.0, Op.is_equal, Op.mult, rd=("row", "c0"), wr=("tri2",))
+    fill(T.trt[:, 896:1024:4], -1.0, "trB2")
+    vtt(T.trt[:, 0:512:4], T.tri[:, 0:128], T.tri[:, 128:256], Op.add, ("tri1", "tri2"), ("trA",))
+    fill(T.ot[:], 0.0, "otA", "otB", "otC", "otD")
+    vcp(T.trt[96:128, 897:1024:4], T.trt[96:128, 384:512:4], ("trA",), ("trB",))
+    fill(T.mmt[:], 0.0, "mm0", "mm1", "mm2", "mm3")
+    quant("tr", 0, 256, T.trt[:], ("trA", "trB", "trB2"))
+    vts(T.kst[:, 0:256:2], T.k16[:, 0:256:2], 1.0, None, Op.add, rd=("k16",), wr=("kst0",))
+    vts(T.kst[:, 1:256:2], T.k16[:, 1:256:2], 17.0, None, Op.add, rd=("k16",), wr=("kst1",))
+    fill(T.kx[:], -1.0, "kx")
+    for i, r in enumerate(order):
+        fill(T.kx[:, 4 * i:4 * i + 4:3], float(r), "kx")
+    vtt(cs(5), cs(0), cs(1), Op.subtract, ("c0", "c1"), ("c5",))
+    vts(cs(6), cs(5), 32.0, None, Op.add, rd=("c5",), wr=("c6",))
+    vts(cs(7), cs(5), 64.0, None, Op.add, rd=("c5",), wr=("c7",))
+    fill(T.m2t[:], 0.0, "m20", "m21", "m22", "m23")
+    for b in range(4):
+        act(T.et[:, 512 * b:512 * b + 512], T.zt[:], Act.Copy, ("zt",), ("et%d" % b,))
+        act(T.et[:, 512 * b + b:512 * b + 512:4], T.iden[:], Act.Copy, ("iden",), ("et%d" % b,), scale=0.5)
+
+    kk = ("kq", "kp", "kqo", "kpo")
+    mm(5, 128, "x", 32, "k", 0, rd=kk)
+    mm(6, 128, "x", 64, "k", 0, rd=kk)
+    for b in range(5):
+        mm(b, 128, "r", 128 * b, "k", 0, rd=kk)
+    vscan(T.rmax[:, 0:128], bank(5, 128), T.zer[:], -1e29, Op.max, Op.add, ("b5", "zer"), ("rA",))
+    vscan(T.rmax[:, 128:256], bank(6, 128), T.zer[:], -1e29, Op.max, Op.add, ("b6", "zer"), ("rB",))
+    for b in range(5):
+        vred(T.m5[:, b:b + 1], bank(b, 128), Op.max, ("b%d" % b,), ("m5%d" % b,))
+    best = [T.rmax[:, 127:128], T.rmax[:, 255:256]]
+
+    def rep(b):
+        act(T.rep[:, 32 * b:32 * b + 32], T.ones[:], Act.Copy, ("ones", "m5%d" % b), ("rep%d" % b,), scale=T.m5[:, b:b + 1])
+
+    def theta(i):
+        act(T.th[:, 160 * i:160 * i + 160], T.lneg[:, 160 * i:160 * i + 160], Act.Identity,
+            ("ln" + "AB"[i], "ab2", "r" + "AB"[i]), ("th%d" % i,), scale=tn("ab2", i), bias=best[i])
+
+    def below(i, dst, a, step):
+        v = T.rmax[:, 128 * i + a:128 * i + 128 - (step > 1):step]
+        n = len(range(a, 128 - (step > 1), step))
+        j0 = {"gg": 0, "gd": 0, "gq": 8}[dst]
+        key = "jnk%d%s" % (i, dst) if dst != "gd" else "jnk%dgg" % i
+        j0 = 128 * i if dst != "gq" else None
+        out = T.jnk[:, j0:j0 + n] if j0 is not None else T.jnk[:, 128 * i:128 * i + n]
+        key = "jnk%d" % i
+        act(out, v, Act.Sign, ("r" + "AB"[i],), (dst + str(i), key), scale=-1.0, bias=best[i], accum_out=tn(dst, i))
+
+    act(tn("ab"), T.rmax[:, 127:256:128], Act.Abs, ("rA", "rB"), ("ab",), scale=1.25 * 2.0 ** -24)
+    act(tn("ab2"), tn("ab"), Act.Identity, ("ab",), ("ab2",), bias=2.0 ** -100)
+    rep(0)
+    theta(0)
+    rep(1)
+    rep(2)
+    theta(1)
+    rep(3)
+    rep(4)
+    for i in range(2):
+        below(i, "gg", 0, 1)
+        below(i, "gq", 31, 32)
+    run("v", lambda: V.transpose(T.mrow[:], T.rep[:]), tuple("rep%d" % b for b in range(5)), ("mrow",))
+    vtt(T.cc[:, 0:160], T.mrow[:], T.th[:, 0:160], Op.is_gt, ("mrow", "th0"), ("ccA",))
+    act(T.cj[:], T.cc[:, 0:160], Act.Copy, ("ccA",), ("cj", "cn0"), accum_out=tn("cn", 0))
+    vtt(T.cc[:, 160:320], T.mrow[:], T.th[:, 160:320], Op.is_gt, ("mrow", "th1"), ("ccB",))
+    vred(tn("cn", 1), T.cc[:, 160:320], Op.add, ("ccB",), ("cn1",))
+    for i in range(2):
+        vts(tn("sel", i), tn("cn", i), 64.0, None, Op.is_lt, rd=("cn%d" % i,), wr=("sel%d" % i,))
+    for i in range(2):
+        vts(T.ot[:, i:512:4], T.rowb[:], tn("gg", i), tn("sel", i), Op.is_equal, Op.mult,
+            ("rowb", "gg%d" % i, "sel%d" % i), ("ot" + "AB"[i],))
+        vts(T.ot[:, 512 + i:528:4], T.rowb[:, 0:4], tn("gq", i), tn("sel", i), Op.is_equal, Op.mult,
+            ("rowb", "gq%d" % i, "sel%d" % i), ("ot" + "CD"[i],))
+    quant("ob", 0, 132, T.ot[:], ("otA", "otB", "otC", "otD"))
+    mm(0, 132, "tr", 0, "ob", 0)
+    mm(1, 132, "tr", 128, "ob", 0)
+    for i in range(2):
+        below(i, "gd", 15, 16)
+    act(tn("gd16"), tn("gd"), Act.Copy, ("gd0", "gd1"), ("gd16",), scale=16.0)
+    act(tn("gd64"), tn("gd"), Act.Copy, ("gd0", "gd1"), ("gd64",), scale=64.0)
+    for i in range(2):
+        act(tn("gm", i), tn("gd", i), Act.Identity, ("gd%d" % i, "gg%d" % i), ("gm%d" % i,), scale=-16.0, bias=tn("gg", i))
+    for i in range(2):
+        vts(T.mmt[:, 64 + i:96:2], T.kx[:], tn("gq", i), cs(1), Op.is_equal, Op.mult, ("kx", "gq%d" % i, "c1"), ("mm%d" % i,))
+        vts(T.mmt[:, 128 + i:160:2], T.kx[:], tn("gq", i), cs(6 + i), Op.is_equal, Op.mult,
+            ("kx", "gq%d" % i, "c%d" % (6 + i)), ("mm%d" % (2 + i),))
+    quant("mm", 0, 160, T.mmt[:], ("mm0", "mm1", "mm2", "mm3"))
+    for i in range(2):
+        vred(tn("yy", i), bank(i, 128, 132), Op.max, ("b%d" % i,), ("yy%d" % i,))
+    for i in range(2):
+        vts(T.stt[:, i:512:2], T.kst[:], tn("yy", i), None, Op.is_equal, rd=("kst0", "kst1", "yy%d" % i), wr=("st%d" % i,))
+    quant("st", 0, 128, T.stt[:], ("st0", "st1"))
+    mm(2, 128, "st", 0, "mm", 16, True, False)
+    mm(2, 128, "st", 0, "mm", 32, False, True)
+    for i in range(2):
+        vred(tn("lpv", i), bank(i, 128), Op.max, ("b%d" % i,), ("lpv%d" % i,))
+    for i in range(2):
+        vts(T.s2t[:, i:512:2], T.k16[:], tn("gm", i), None, Op.is_equal, rd=("k16", "gm%d" % i), wr=("s2%d" % i,))
+    vcp(T.invu[:], bank(2, 8), ("b2",), ("invu",))
+    pickq("sl", 0, 96, "x", 192, T.invu[:, 0:6], ("xq", "invu"), ("slq",))
+    pickp("sl", 0, 96, "x", 192, T.invu[:, 0:6], ("xp", "invu"), ("slp",))
+    at = 32 + 32 * (3 - s)
+    scatter([T.slq[:, 32 * i:32 * i + 32].bitcast(u8) for i in range(3)], T.winq[:, at:at + 32].bitcast(u8), others,
+            "so", "lb", ("slq",), 0)
+    scatter([T.slp[:, 32 * i:32 * i + 32] for i in range(3)], T.winp[:, at:at + 32], others, "so", "lb", ("slp",), 3)
+    lastw["winq"] = lastw["winp"] = [("so", 24)]
+    y2 = ("yy0", "yy1")
+    vts(tn("hia"), tn("yy"), 16.0, 16.0, Op.is_gt, Op.mult, y2, ("hia",))
+    vts(tn("hib"), tn("yy"), 0.0, 32.0 * (3 - s), Op.is_gt, Op.mult, y2, ("hib",))
+    vts(tn("ylo"), tn("yy"), 0.0, None, Op.max, rd=y2, wr=("ylo",))
+    vtt(tn("key"), tn("gd64"), tn("lpv"), Op.add, ("gd64", "lpv0", "lpv1"), ("key",))
+    vtt(tn("hi"), tn("hia"), tn("hib"), Op.add, ("hia", "hib"), ("hi",))
+    vtt(tn("lo"), tn("ylo"), tn("hia"), Op.subtract, ("ylo", "hia"), ("lo",))
+    for i in range(2):
+        vts(T.m2t[:, i:64:4], T.kc[:], tn("key", i), tn("lo", i), Op.is_equal, Op.mult, ("kc", "key", "lo"), ("m2%d" % i,))
+        vts(T.m2t[:, 2 + i:64:4], T.kc[:], tn("key", i), tn("hi", i), Op.is_equal, Op.mult, ("kc", "key", "hi"), ("m2%d" % (2 + i),))
+    quant("s2", 0, 128, T.s2t[:], ("s20", "s21"))
+    quant("m2", 0, 128, T.m2t[:], ("m20", "m21", "m22", "m23"))
+    mm(3, 128, "s2", 0, "m2", 0)
+    pickq("win", at, at + 32, "x", 192, T.invu[:, 6:8], ("xq", "invu", "winqz"), ("winqo",))
+    pickp("win", at, at + 32, "x", 192, T.invu[:, 6:8], ("xp", "invu", "winpz"), ("winpo",))
+    vcp(T.lst[:], bank(3, 16), ("b3",), ("lst",))
+    scatter([T.lst[:, 4 * r:4 * r + 4] for r in others], T.ll[:, 8 * s:8 * s + 4], others, "li", "lb", ("lst",), 0)
+    vcp(T.ll[:, 8 * s:8 * s + 4], T.lst[:, 4 * s:4 * s + 4], ("lst", "ll"), ("llo",))
+    lastw["lli"] = [("li", 12)]
+    if s < 3:
+        vts(T.nz[:], T.lst[:], 0.0, None, Op.is_gt, rd=("lst",), wr=("nz",))
+        for h in range(2):
+            vtt(T.csum[:, h:8:2], T.nz[:, h:16:4], T.nz[:, 2 + h:16:4], Op.add, ("nz",), ("csum%d" % h,))
+        higher = [r for r in others if r > s]
+        scatter([T.csum[:, 0:8]] * len(higher), T.lc[:, 8 * s:8 * s + 8], higher, "ct", "lb", ("csum0", "csum1"), 0)
+    if s > 0:
+        lastw["lc"] = [("ct", 4 * s)]
+
+    quant("e", 0, 512, T.et[:], ("et0", "et1", "et2", "et3"))
+    quant("w", 0, 512, T.wt[:], ("wt",))
+    for b in range(4):
+        mm(b, 128, "e", 128 * b, "x", 0)
+    for i in range(4):
+        mm(4 + i, 192, "w", 128 * i, "x", 0)
+    for b in range(4):
+        act(T.da[:, 32 * b:32 * b + 32], bank(b, 32), Act.Copy, ("b%d" % b,), ("da%d" % b,))
+    for i in range(4):
+        act(T.hot[:, i:768:4], bank(4 + i, 192), Act.Relu, ("b%d" % (4 + i),), ("hot%d" % i,), scale=0.0625)
+    fill(T.mt[:], 0.0, "mt0", "mt1", "mt2", "mt3")
+    fill(T.hmt[:], 0.0, "hmt0", "hmt1", "hmt2", "hmt3")
+
+    L = T.ll
+    rl = ("ll", "llo", "lli")
+    vtt(T.la16[:], L[:, 0:16], L[:, 16:32], Op.max, rl, ("la16",))
+    vtt(T.lb16[:], L[:, 0:16], L[:, 16:32], Op.min, rl, ("lb16",))
+    vtt(T.lu[:], T.la16[:, 0:8], T.la16[:, 8:16], Op.max, ("la16",), ("lu",))
+    vtt(T.lcm[:], T.la16[:, 0:2], T.la16[:, 8:10], Op.min, ("la16",), ("lcm",))
+    vtt(T.lf[:], T.lb16[:, 0:2], T.lb16[:, 8:10], Op.max, ("lb16",), ("lf",))
+    vtt(T.lg[:], T.lcm[:], T.lf[:], Op.max, ("lcm", "lf"), ("lg",))
+    vtt(T.lu[:, 2:4], T.lg[:], T.lu[:, 2:4], Op.max, ("lg",), ("lu",))
+    vts(T.off[:], T.lu[:, 0:4], 31.0, None, Op.add, rd=("lu",), wr=("off",))
+    ww = lambda c: ("win" + c, "win" + c + "o", "win" + c + "z", "off")
+    pickq("fs", 0, 64, "win", 160, T.off[:, 0:4], ww("q"), ("fsq",))
+    pickp("fs", 0, 64, "win", 160, T.off[:, 0:4], ww("p"), ("fsp",))
+    for b in range(4):
+        mm(b, 128, "e", 128 * b, "fs", 0)
+
+    def add1(b):
+        vtt(T.uu[:, 32 * b:32 * b + 32], T.da[:, 32 * b:32 * b + 32], bank(b, 32), Op.add, ("da%d" % b, "b%d" % b), ("uu%d" % b,))
+
+    def add2(b):
+        vtt(T.mt[:, b:128:4], T.uu[:, 32 * b:32 * b + 32], bank(b, 32, 64), Op.add, ("uu%d" % b, "b%d" % b), ("mt%d" % b,))
+    add1(0)
+    for b in range(1, 4):
+        add1(b)
+        add2(b - 1)
+    add2(3)
+    quant("m", 0, 128, T.mt[:], ("mt0", "mt1", "mt2", "mt3"))
+    for i in range(4):
+        mm(4 + i, 128, "w", 128 * i, "m", 0)
+    for i in range(4):
+        k = ("b%d" % (4 + i),), ("hmt%d" % i,)
+        if i % 2 == 0:
+            act(T.hmt[:, i:128:4], bank(4 + i, 32), Act.Relu, k[0], k[1], scale=0.0625)
+        else:
+            vts(T.hmt[:, i:128:4], bank(4 + i, 32), 0.0, 0.0625, Op.max, Op.mult, k[0], k[1])
+    quant("hm", 0, 128, T.hmt[:], ("hmt0", "hmt1", "hmt2", "hmt3"))
+    hat = 192 + A * s
+    bcast(T.hmq[:, 0:A].bitcast(u8), T.hwq[:, hat:hat + A].bitcast(u8), "hm", "lb", ("hmq",))
+    bcast(T.hmp[:, 0:A], T.hwp[:, hat:hat + A], "hm", "lb", ("hmp",))
+    lastw["hwq"] = lastw["hwp"] = [("hm", 96)]
+
+    fill(T.s3t[:], 0.0, "s3a", "s3b")
+    fill(T.tmt[:], 0.0, "tm0", "tm1", "tm2", "tm3", "tm4", "tm5")
+    vts(tn("thz"), tn("lpv"), 30.0, 0.0, Op.subtract, Op.max, ("lpv0", "lpv1"), ("thz",))
+    vts(tn("thy"), tn("yy"), 0.0, None, Op.is_gt, rd=y2, wr=("thy",))
+    vts(cs(3), cs(5), 0.0625, None, Op.mult, rd=("c5",), wr=("c3",))
+    vts(T.s3t[:, 0:512:2], T.k16[:], cs(1), None, Op.is_equal, rd=("k16", "c1"), wr=("s3a",))
+    vtt(tn("thr"), tn("thz"), tn("thy"), Op.mult, ("thz", "thy"), ("thr",))
+    vts(cs(4), cs(3), 2.0, None, Op.add, rd=("c3",), wr=("c4",))
+    vts(T.s3t[96:128, 1:512:2], T.k16[96:128, :], T.cst[96:128, 1:2], None, Op.is_equal, rd=("k16", "c1"), wr=("s3b",))
+    vts(T.tmt[:, 0:512:4], T.iden[:], tn("thr", 0), None, Op.mult, rd=("iden", "thr"), wr=("tm0",))
+    vts(T.tmt[:, 513:640:4], T.iden[:, 96:128], tn("thr", 1), None, Op.mult, rd=("iden", "thr"), wr=("tm1",))
+    for i in range(2):
+        vts(T.tmt[:, 640 + i:680:4], T.row[:, 0:10], cs(3 + i), tn("gm", i), Op.is_equal, Op.mult,
+            ("row", "c%d" % (3 + i), "gm%d" % i), ("tm%d" % (2 + i),))
+        vts(T.tmt[:, 642 + i:680:4], T.row[:, 0:10], cs(3 + i), tn("gd16", i), Op.is_equal, Op.mult,
+            ("row", "c%d" % (3 + i), "gd16"), ("tm%d" % (4 + i),))
+    quant("tm", 0, 172, T.tmt[:], tuple("tm%d" % i for i in range(6)))
+    quant("s3", 0, 128, T.s3t[:], ("s3a", "s3b"))
+    mm(1, 128, "s3", 0, "tm", 44)
+    mm(0, 160, "s3", 0, "tm", 0)
+    vts(T.colm[:], T.colw[:], 192.0, None, Op.subtract, rd=("colw",), wr=("colm",))
+    fill(T.rst[:], 1.0, "rst")
+    fill(T.rst[:, 0:160:16], 0.0, "rst")
+    vcp(T.gwu[:], bank(1, 116, 126), ("b1",), ("gwu",))
+    if s > 0:
+        src, key = T.lc[:, 0:8], "lc"
+        for r in range(1, s):
+            vtt(T.ctot[:], src, T.lc[:, 8 * r:8 * r + 8], Op.add, ("lc", key), ("ctot",))
+            src, key = T.ctot[:], "ctot"
+        vcp(T.cu[:], src, (key,), ("cu",))
+        act(T.crow[:], T.row[:, 0:128].indirect(T.cu[:, 0:8]), Act.Copy, ("row", "cu"), ("crow",))
+        act(T.prior[:], T.crow[:, 0:128].indirect(T.gwu[:, 0:10]), Act.Copy, ("crow", "gwu"), ("prior",))
+    vtt(T.dw[:], bank(1, 116, 126), T.colm[:, 2:12], Op.subtract, ("b1", "colm"), ("dw",))
+    pickq("hw", hat, hat + A, "hm", 128, T.colu[:, 0:2], ("hmq", "colu"), ("hwqm",))
+    pickp("hw", hat, hat + A, "hm", 128, T.colu[:, 0:2], ("hmp", "colu"), ("hwpm",))
+    quant("hw", 0, 192, T.hot[:], ("hot0", "hot1", "hot2", "hot3"), ("hwqo", "hwpo"))
+    quant("v", 0, 128, T.vt[:], ("vt",))
+    vts(T.fm[:], T.lu[:, 0:2], 0.0, 192.0 + A * s, Op.is_gt, Op.mult, ("lu",), ("fm",))
+    vtt(T.fin[:, 0:2], T.fm[:], T.colw[:, 0:2], Op.add, ("fm", "colw"), ("fin0",))
+    if s > 0:
+        vtt(T.adm[:], T.prior[:], bank(0, 160), Op.is_lt, ("prior", "b0"), ("adm",))
+    else:
+        vts(T.adm[:], bank(0, 160), 0.0, None, Op.is_gt, rd=("b0",), wr=("adm",))
+    vscan(T.scn[:], T.rst[:], T.adm[:], 0.0, Op.mult, Op.add, ("rst", "adm"), ("scn",))
+    vtt(T.admt[:], T.scn[:, 15:160:16], T.dw[:], Op.mult, ("scn", "dw"), ("admt",))
+    vtt(T.fin[:, 2:12], T.admt[:], T.colw[:, 2:12], Op.add, ("admt", "colw"), ("fin1",))
+    vcp(T.finu[:], T.fin[:], ("fin0", "fin1"), ("finu",))
+    fill(T.mgt[:, 0:192], -1.0, "mgta")
+    fill(T.mgr[:, 0:32], -1.0, "mgr0")
+    act(T.mgr[:, 32:192], T.mgt[:, 0:320].indirect(T.finu[:, 2:12]), Act.Copy, ("mgta", "mgtb", "finu"), ("mgr1",))
+    run("y", lambda: g.sync.dma_start(T.mg[0:1, 0:192], T.mgr[0:1, 0:192]), ("mgr0", "mgr1"), (), sem="dout")
+
+    hh = lambda c: ("hw" + c, "hw" + c + "m", "hw" + c + "o", "finu")
+    pickq("fo", 0, 192, "hw", 320, T.finu[:, 0:12], hh("q"), ("foq",))
+    pickp("fo", 0, 192, "hw", 320, T.finu[:, 0:12], hh("p"), ("fop",))
+    mm(2, 192, "v", 0, "fo", 0)
+    vcp(T.yo[:], bank(2, 192), ("b2",), ("yo",))
+    run("y", lambda: g.sync.dma_start(T.oc[:, 0:768], T.foq[:, 0:192].bitcast(u8)), ("foq",), (), sem="dout")
+    run("y", lambda: g.sync.dma_start(T.y[:, :], T.yo[:, :]), ("yo",), (), sem="dout")
+    for k in range(4):
+        run("s", lambda: S.dma_start(T.osc[4 * k:4 * k + 4, 0:192], T.fop[32 * k:32 * k + 4, 0:192]), ("fop",), (), sem="dout")
+    wait("g", [(n, total[n]) for n in ("qv", "qs", "qt", "qg", "dout")] + [("lb", lsum["lb"])])

@@ -20,19 +20,19 @@ def _mx(**names):
 
 SCRATCH["psum"] = ("psum", [128, 4096], F)
 _sb(I32, pidi=1, ui=1)
-_sb(F, cst=16, row=160, kc=16, kx=16, rli=40, colw=12, colm=12, lneg=320, ones=32, zer=128, rst=160, mgt=320,
-    rmax=256, m5=8, rep=160, mrow=160, th=320, jnk=256, tiny=64, tri=256,
+_sb(F, cst=16, row=160, kc=16, kx=16, rli=40, colw=12, colm=12, lneg=320, zer=160, rst=160, seg=160, mgt=320,
+    rmax=256, md=160, rep=160, mrow=160, th=320, jnk=256, tiny=64, tri=256, kab=32,
     da=128, uu=128, dw=10, crow=128, prior=160, adm=160, scn=160, admt=10, fin=12, fm=2, mgr=192, yo=192)
 _sb(B16, rowb=128, k16=256, kst=256, iden=128, et=2048, trt=1024, s3t=512, zt=512, xz=512, xt=768, wt=2048, vt=512,
-    cc=320, cj=160, ot=528, mmt=640, stt=512, s2t=512, m2t=512, tmt=688, mt=512, hmt=512, hot=768,
-    lst=16, nz=16, csum=8, ll=32, lc=24, la16=16, lb16=16, lu=8, lcm=2, lf=2, lg=2, ctot=8)
+    cc=320, cj=320, ot=528, mmt=640, stt=512, s2t=512, m2t=512, tmt=688, mt=512, hmt=512, hot=768, hot10=20,
+    lst=16, nz=16, csum=8, ll=32, lc=24, lab=32, lu=16, lcm=2, lf=2, sec=2, ctot=8)
 _sb(U16, rlu=40, colu=12, invu=8, off=4, gwu=10, cu=8, finu=12)
 _mx(e=512, tr=256, s3=128, a=128, x=192, k=128, r=640, w=512, v=128, ob=132, mm=160, st=128, s2=128, m2=128, tm=172,
     sl=96, win=160, fs=128, m=128, hm=128, hw=320, fo=192)
 
 SEMAPHORES = ["qv", "qs", "qt", "qg", "dxa", "dx", "dw", "dv", "an", "so", "li", "ct", "hm", "la", "lb", "dout"]
 _TINY = {n: 2 * i for i, n in enumerate(["ab", "ab2", "cn", "sel", "gg", "gd", "gq", "gm", "gd16", "gd64", "yy", "lpv",
-                                         "key", "hia", "hib", "hi", "ylo", "lo", "thz", "thy", "thr"])}
+                                         "key", "hib", "hi", "ylo", "yl8", "lo", "thz", "thy", "thr", "sg1", "sg2"])}
 
 
 def rank_program(g, core, T, topo):
@@ -97,6 +97,9 @@ def rank_program(g, core, T, topo):
     def act(out, in_, func, rd=(), wr=(), **kw):
         run("s", lambda: S.activation(out, in_, func, **kw), rd, wr)
 
+    def iota(out, pattern, base, *wr):
+        run("g", lambda: g.iota(out, pattern, base, 0, allow_small_or_imprecise_dtypes=True), (), wr)
+
     def quant(n, a, b, src, rd=(), wr=None):
         run("v", lambda: V.quantize_mx(T[n + "q"][:, a:b], T[n + "p"][:, a:b], src), rd, wr or (n + "q", n + "p"))
 
@@ -130,7 +133,7 @@ def rank_program(g, core, T, topo):
     lsum = {"la": 0, "lb": 0}
 
     def bcast(src, dst, sem, local, rd):
-        eng = [e for e in topo.engines(core, T.cores[others[0]])]
+        eng = topo.engines(core, T.cores[others[0]])
         wait("g", [t for k in rd for t in lastw[k]])
         g.remote_dma_fused([RemoteDMATransfer(dst_ids=[addr(r) for r in others], dma_engine_mask=msk(eng),
                                               remote_sem=T.sem[sem], srcs=[src], dsts=[dst] * len(others))],
@@ -149,124 +152,125 @@ def rank_program(g, core, T, topo):
         lsum[local] += 4 * len(tr)
 
     u8 = dt.uint8
-    small = {"allow_small_or_imprecise_dtypes": True}
+
+    def cs(j):
+        return T.cst[:, j:j + 1]
 
     run("y", lambda: g.sync.dma_start(T.xz[:, 0:128], T.x[:, 0:128]), (), ("xza",), sem="dxa")
     run("s", lambda: S.dma_start(T.xt[:, :], T.x[:, :]), (), ("xt",), sem="dx")
 
     run("g", lambda: g.iota(T.pidi[:], [[0, 1]], 0, 1), (), ("pidi",))
-    run("g", lambda: g.iota(T.row[:], [[1, 160]], 0, 0, **small), (), ("row",))
-    run("g", lambda: g.iota(T.rli[:], [[32, 5], [0, 4], [16, 2]], A, 0, **small), (), ("rli",))
-    run("g", lambda: g.iota(T.colw[:], [[16, 12]], 0, 0, **small), (), ("colw",))
-    run("g", lambda: g.iota(T.k16[:], [[0, 8], [1, 16], [0, 2]], 0, 0, **small), (), ("k16",))
-    run("g", lambda: g.iota(T.kc[:], [[128, 4], [-1, 2], [64, 2]], 32, 0, **small), (), ("kc",))
+    iota(T.row[:], [[1, 160]], 0, "row")
+    iota(T.rli[:], [[32, 5], [0, 4], [16, 2]], A, "rli")
+    iota(T.colw[:], [[16, 12]], 0, "colw")
+    iota(T.k16[:], [[0, 8], [1, 16], [0, 2]], 0, "k16")
+    iota(T.kc[:], [[128, 4], [-1, 2], [64, 2]], 32, "kc")
 
-    def cs(j):
-        return T.cst[:, j:j + 1]
-    fill(T.xz[:, 128:512], 0.0, "xzz")
     fill(T.zt[:], 0.0, "zt")
+    fill(T.xz[:, 128:512], 0.0, "xzz")
     quant("win", 0, 128, T.zt[:], ("zt",), ("winqz", "winpz"))
     quant("fs", 0, 128, T.zt[:], ("zt",))
     fill(T.ll[:], 0.0, "ll")
     vcp(cs(0), T.pidi[:], ("pidi",), ("c0",))
     run("v", lambda: V.tensor_scalar(T.ui[:], T.pidi[:], 15, None, Op.bitwise_and), ("pidi",), ("ui",))
-    fill(T.trt[:], 0.0, "trA", "trB")
+    fill(T.zer[:], 0.0, "zer")
     vcp(cs(1), T.ui[:], ("ui",), ("c1",))
     vts(T.iden[:], T.row[:, 0:128], cs(0), None, Op.is_equal, rd=("row", "c0"), wr=("iden",))
     vts(T.rlu[:], T.rli[:], cs(1), None, Op.add, rd=("rli", "c1"), wr=("rlu",))
     vts(T.colw[:], T.colw[:], cs(1), None, Op.add, rd=("c1",), wr=("colw",))
+    fill(T.trt[:], 0.0, "trA", "trB")
     vcp(T.colu[:], T.colw[:], ("colw",), ("colu",))
+    for b in range(4):
+        act(T.et[:, 512 * b:512 * b + 512], T.zt[:], Act.Copy, ("zt",), ("et%d" % b,))
+    for b in range(4):
+        act(T.et[:, 512 * b + b:512 * b + 512:4], T.iden[:], Act.Copy, ("iden",), ("et%d" % b,), scale=0.5)
 
     quant("a", 0, 128, T.xz[:], ("xza", "xzz"))
     bcast(T.aq[:, 0:A].bitcast(u8), T.kq[:, A * s:A * s + A].bitcast(u8), "an", "la", ("aq",))
     bcast(T.ap[:, 0:A], T.kp[:, A * s:A * s + A], "an", "la", ("ap",))
     lastw["kq"] = lastw["kp"] = [("an", 96)]
-    run("g", lambda: g.iota(T.mgt[:, 192:320], [[192, 4], [1, 32]], 0, 0, **small), (), ("mgtb",))
     wait("y", [("la", lsum["la"])])
     run("y", lambda: g.sync.dma_start(T.wt[:, :], T.w[:, :]), (), ("wt",), sem="dw")
     run("y", lambda: g.sync.dma_start(T.vt[:, :], T.v[:, :]), (), ("vt",), sem="dv")
 
+    def sel_g(out, in_, pattern, op, fl, base, cm, rd, wr):
+        run("g", lambda: g.affine_select(out, in_, pattern, op, fl, base, cm), rd, wr)
+    sel_g(T.lneg[:, 0:160], T.zer[:], [[1, 160]], Op.is_ge, -1.0, 0, -1, ("zer",), ("ln0",))
+    sel_g(T.lneg[:, 160:320], T.zer[:], [[1, 160]], Op.is_ge, -1.0, -32, -1, ("zer",), ("ln1",))
+    iota(T.rowb[:], [[1, 128]], 0, "rowb")
+    iota(T.tmt[:], [[0, 688]], 0, *["tm%d" % i for i in range(6)])
+    iota(T.s3t[:], [[0, 512]], 0, "s3a", "s3b")
+    iota(T.mt[:], [[0, 512]], 0, "mt0", "mt1", "mt2", "mt3")
     quant("x", 0, 192, T.xt[:], ("xt",))
     own = (A * s, A * s + A)
     pickq("k", own[0], own[1], "a", 128, T.colu[:, 0:2], ("aq", "colu"), ("kqo",))
     pickp("k", own[0], own[1], "a", 128, T.colu[:, 0:2], ("ap", "colu"), ("kpo",))
     pickq("r", 0, 640, "x", 192, T.rlu[:, 0:40], ("xq", "rlu"), ("rq",))
     pickp("r", 0, 640, "x", 192, T.rlu[:, 0:40], ("xp", "rlu"), ("rp",))
-    fill(T.ones[:], 1.0, "ones")
-    fill(T.zer[:], 0.0, "zer")
-    vts(cs(2), cs(0), 32.0, None, Op.add, rd=("c0",), wr=("c2",))
-    vts(T.lneg[:, 0:160], T.row[:], cs(0), -1.0, Op.is_lt, Op.mult, rd=("row", "c0"), wr=("lnA",))
-    vts(T.lneg[:, 160:320], T.row[:], cs(2), -1.0, Op.is_lt, Op.mult, rd=("row", "c2"), wr=("lnB",))
-    vcp(T.rowb[:], T.row[:, 0:128], ("row",), ("rowb",))
+    fill(T.md[:], 0.0, "md0", "md1", "md2", "md3", "md4")
+    fill(T.seg[:], 1.0, "seg")
+    fill(T.seg[:, 0:160:32], 0.0, "seg")
     vts(T.tri[:, 0:128], T.row[:, 0:128], cs(0), -1.0, Op.is_gt, Op.mult, rd=("row", "c0"), wr=("tri1",))
     vts(T.tri[:, 128:256], T.row[:, 0:128], cs(0), 32.0, Op.is_equal, Op.mult, rd=("row", "c0"), wr=("tri2",))
     fill(T.trt[:, 896:1024:4], -1.0, "trB2")
     vtt(T.trt[:, 0:512:4], T.tri[:, 0:128], T.tri[:, 128:256], Op.add, ("tri1", "tri2"), ("trA",))
-    fill(T.ot[:], 0.0, "otA", "otB", "otC", "otD")
+    fill(T.kx[:], -1.0, "kx")
     vcp(T.trt[96:128, 897:1024:4], T.trt[96:128, 384:512:4], ("trA",), ("trB",))
-    fill(T.mmt[:], 0.0, "mm0", "mm1", "mm2", "mm3")
+    for i, r in enumerate(order):
+        fill(T.kx[:, 4 * i:4 * i + 4:3], float(r), "kx")
     quant("tr", 0, 256, T.trt[:], ("trA", "trB", "trB2"))
     vts(T.kst[:, 0:256:2], T.k16[:, 0:256:2], 1.0, None, Op.add, rd=("k16",), wr=("kst0",))
     vts(T.kst[:, 1:256:2], T.k16[:, 1:256:2], 17.0, None, Op.add, rd=("k16",), wr=("kst1",))
-    fill(T.kx[:], -1.0, "kx")
-    for i, r in enumerate(order):
-        fill(T.kx[:, 4 * i:4 * i + 4:3], float(r), "kx")
     vtt(cs(5), cs(0), cs(1), Op.subtract, ("c0", "c1"), ("c5",))
+    vts(cs(8), cs(1), -1.0, None, Op.mult, rd=("c1",), wr=("c8",))
     vts(cs(6), cs(5), 32.0, None, Op.add, rd=("c5",), wr=("c6",))
     vts(cs(7), cs(5), 64.0, None, Op.add, rd=("c5",), wr=("c7",))
-    fill(T.m2t[:], 0.0, "m20", "m21", "m22", "m23")
-    for b in range(4):
-        act(T.et[:, 512 * b:512 * b + 512], T.zt[:], Act.Copy, ("zt",), ("et%d" % b,))
-        act(T.et[:, 512 * b + b:512 * b + 512:4], T.iden[:], Act.Copy, ("iden",), ("et%d" % b,), scale=0.5)
+    vts(cs(9), cs(6), -1.0, None, Op.mult, rd=("c6",), wr=("c9",))
+    vts(cs(10), cs(7), -1.0, None, Op.mult, rd=("c7",), wr=("c10",))
+    act(T.mmt[:, 0:512], T.zt[:], Act.Copy, ("zt",), ("mm0", "mm1", "mm2", "mm3"))
+    act(T.mmt[:, 512:640], T.zt[:, 0:128], Act.Copy, ("zt",), ("mm4",))
+    act(T.ot[:, 0:512], T.zt[:], Act.Copy, ("zt",), ("otA", "otB"))
+    act(T.ot[:, 512:528], T.zt[:, 0:16], Act.Copy, ("zt",), ("otC", "otD"))
+    act(T.m2t[:], T.zt[:], Act.Copy, ("zt",), ("m20", "m21", "m22", "m23"))
 
     kk = ("kq", "kp", "kqo", "kpo")
     mm(5, 128, "x", 32, "k", 0, rd=kk)
     mm(6, 128, "x", 64, "k", 0, rd=kk)
     for b in range(5):
         mm(b, 128, "r", 128 * b, "k", 0, rd=kk)
-    vscan(T.rmax[:, 0:128], bank(5, 128), T.zer[:], -1e29, Op.max, Op.add, ("b5", "zer"), ("rA",))
-    vscan(T.rmax[:, 128:256], bank(6, 128), T.zer[:], -1e29, Op.max, Op.add, ("b6", "zer"), ("rB",))
+    for i in range(2):
+        vscan(T.rmax[:, 128 * i:128 * i + 128], bank(5 + i, 128), T.zer[:, 0:128], -1e29, Op.max, Op.add,
+              ("b%d" % (5 + i), "zer"), ("r%d" % i,))
     for b in range(5):
-        vred(T.m5[:, b:b + 1], bank(b, 128), Op.max, ("b%d" % b,), ("m5%d" % b,))
+        vred(T.md[:, 32 * b:32 * b + 1], bank(b, 128), Op.max, ("b%d" % b,), ("md%d" % b,))
     best = [T.rmax[:, 127:128], T.rmax[:, 255:256]]
 
-    def rep(b):
-        act(T.rep[:, 32 * b:32 * b + 32], T.ones[:], Act.Copy, ("ones", "m5%d" % b), ("rep%d" % b,), scale=T.m5[:, b:b + 1])
-
-    def theta(i):
-        act(T.th[:, 160 * i:160 * i + 160], T.lneg[:, 160 * i:160 * i + 160], Act.Identity,
-            ("ln" + "AB"[i], "ab2", "r" + "AB"[i]), ("th%d" % i,), scale=tn("ab2", i), bias=best[i])
-
     def below(i, dst, a, step):
-        v = T.rmax[:, 128 * i + a:128 * i + 128 - (step > 1):step]
-        n = len(range(a, 128 - (step > 1), step))
-        j0 = {"gg": 0, "gd": 0, "gq": 8}[dst]
-        key = "jnk%d%s" % (i, dst) if dst != "gd" else "jnk%dgg" % i
-        j0 = 128 * i if dst != "gq" else None
-        out = T.jnk[:, j0:j0 + n] if j0 is not None else T.jnk[:, 128 * i:128 * i + n]
-        key = "jnk%d" % i
-        act(out, v, Act.Sign, ("r" + "AB"[i],), (dst + str(i), key), scale=-1.0, bias=best[i], accum_out=tn(dst, i))
+        end = 128 - (step > 1)
+        n = len(range(a, end, step))
+        act(T.jnk[:, 128 * i:128 * i + n], T.rmax[:, 128 * i + a:128 * i + end:step], Act.Sign, ("r%d" % i,),
+            (dst + str(i), "jnk%d" % i), scale=-1.0, bias=best[i], accum_out=tn(dst, i))
 
-    act(tn("ab"), T.rmax[:, 127:256:128], Act.Abs, ("rA", "rB"), ("ab",), scale=1.25 * 2.0 ** -24)
+    act(tn("ab"), T.rmax[:, 127:256:128], Act.Abs, ("r0", "r1"), ("ab",), scale=1.25 * 2.0 ** -24)
     act(tn("ab2"), tn("ab"), Act.Identity, ("ab",), ("ab2",), bias=2.0 ** -100)
-    rep(0)
-    theta(0)
-    rep(1)
-    rep(2)
-    theta(1)
-    rep(3)
-    rep(4)
+    for i in range(2):
+        act(T.th[:, 160 * i:160 * i + 160], T.lneg[:, 160 * i:160 * i + 160], Act.Identity,
+            ("ln%d" % i, "ab2", "r%d" % i), ("th%d" % i,), scale=tn("ab2", i), bias=best[i])
     for i in range(2):
         below(i, "gg", 0, 1)
         below(i, "gq", 31, 32)
-    run("v", lambda: V.transpose(T.mrow[:], T.rep[:]), tuple("rep%d" % b for b in range(5)), ("mrow",))
-    vtt(T.cc[:, 0:160], T.mrow[:], T.th[:, 0:160], Op.is_gt, ("mrow", "th0"), ("ccA",))
-    act(T.cj[:], T.cc[:, 0:160], Act.Copy, ("ccA",), ("cj", "cn0"), accum_out=tn("cn", 0))
-    vtt(T.cc[:, 160:320], T.mrow[:], T.th[:, 160:320], Op.is_gt, ("mrow", "th1"), ("ccB",))
-    vred(tn("cn", 1), T.cc[:, 160:320], Op.add, ("ccB",), ("cn1",))
+    for i in range(2):
+        below(i, "gd", 15, 16)
+    for i in range(2):
+        act(tn("gm", i), tn("gd", i), Act.Identity, ("gd%d" % i, "gg%d" % i), ("gm%d" % i,), scale=-16.0, bias=tn("gg", i))
+    vscan(T.rep[:], T.seg[:], T.md[:], 0.0, Op.mult, Op.add, ("seg", "md0", "md1", "md2", "md3", "md4"), ("rep",))
+    run("v", lambda: V.transpose(T.mrow[:], T.rep[:]), ("rep",), ("mrow",))
+    for i in range(2):
+        c = slice(160 * i, 160 * i + 160)
+        vtt(T.cc[:, c], T.mrow[:], T.th[:, c], Op.is_gt, ("mrow", "th%d" % i), ("cc%d" % i,))
+        act(T.cj[:, c], T.cc[:, c], Act.Copy, ("cc%d" % i,), ("cj%d" % i, "cn%d" % i), accum_out=tn("cn", i))
     for i in range(2):
         vts(tn("sel", i), tn("cn", i), 64.0, None, Op.is_lt, rd=("cn%d" % i,), wr=("sel%d" % i,))
-    for i in range(2):
         vts(T.ot[:, i:512:4], T.rowb[:], tn("gg", i), tn("sel", i), Op.is_equal, Op.mult,
             ("rowb", "gg%d" % i, "sel%d" % i), ("ot" + "AB"[i],))
         vts(T.ot[:, 512 + i:528:4], T.rowb[:, 0:4], tn("gq", i), tn("sel", i), Op.is_equal, Op.mult,
@@ -275,16 +279,16 @@ def rank_program(g, core, T, topo):
     mm(0, 132, "tr", 0, "ob", 0)
     mm(1, 132, "tr", 128, "ob", 0)
     for i in range(2):
-        below(i, "gd", 15, 16)
-    act(tn("gd16"), tn("gd"), Act.Copy, ("gd0", "gd1"), ("gd16",), scale=16.0)
+        act(T.kab[:, 16 * i:16 * i + 16], T.kx[:], Act.Abs, ("kx", "gq%d" % i), ("kab%d" % i,), scale=-1.0, bias=tn("gq", i))
+    for i in range(2):
+        kab = T.kab[:, 16 * i:16 * i + 16]
+        act(T.mmt[:, 64 + i:96:2], kab, Act.Relu, ("kab%d" % i, "c1", "c8"), ("mm%d" % i,), scale=cs(8), bias=cs(1))
+        act(T.mmt[:, 128 + i:160:2], kab, Act.Relu, ("kab%d" % i, "c%d" % (6 + i), "c%d" % (9 + i)), ("mm%d" % (2 + i),),
+            scale=cs(9 + i), bias=cs(6 + i))
     act(tn("gd64"), tn("gd"), Act.Copy, ("gd0", "gd1"), ("gd64",), scale=64.0)
     for i in range(2):
-        act(tn("gm", i), tn("gd", i), Act.Identity, ("gd%d" % i, "gg%d" % i), ("gm%d" % i,), scale=-16.0, bias=tn("gg", i))
-    for i in range(2):
-        vts(T.mmt[:, 64 + i:96:2], T.kx[:], tn("gq", i), cs(1), Op.is_equal, Op.mult, ("kx", "gq%d" % i, "c1"), ("mm%d" % i,))
-        vts(T.mmt[:, 128 + i:160:2], T.kx[:], tn("gq", i), cs(6 + i), Op.is_equal, Op.mult,
-            ("kx", "gq%d" % i, "c%d" % (6 + i)), ("mm%d" % (2 + i),))
-    quant("mm", 0, 160, T.mmt[:], ("mm0", "mm1", "mm2", "mm3"))
+        vts(T.s2t[:, i:512:2], T.k16[:], tn("gm", i), None, Op.is_equal, rd=("k16", "gm%d" % i), wr=("s2%d" % i,))
+    quant("mm", 0, 160, T.mmt[:], ("mm0", "mm1", "mm2", "mm3", "mm4"))
     for i in range(2):
         vred(tn("yy", i), bank(i, 128, 132), Op.max, ("b%d" % i,), ("yy%d" % i,))
     for i in range(2):
@@ -292,35 +296,39 @@ def rank_program(g, core, T, topo):
     quant("st", 0, 128, T.stt[:], ("st0", "st1"))
     mm(2, 128, "st", 0, "mm", 16, True, False)
     mm(2, 128, "st", 0, "mm", 32, False, True)
+    y2 = ("yy0", "yy1")
+    k3 = 16.0 * (3 - s)
+    act(tn("sg1"), tn("yy"), Act.Sign, y2, ("sg1",), bias=-16.5)
+    act(tn("sg2"), tn("yy"), Act.Sign, y2, ("sg2",), bias=-0.5)
+    act(tn("ylo"), tn("yy"), Act.Relu, y2, ("ylo",))
+    act(tn("hib"), tn("sg2"), Act.Identity, ("sg2",), ("hib",), scale=k3, bias=k3 + 8.0)
+    act(tn("yl8"), tn("ylo"), Act.Identity, ("ylo",), ("yl8",), bias=-8.0)
+    for i in range(2):
+        act(tn("lo", i), tn("sg1", i), Act.Identity, ("sg1", "yl8"), ("lo%d" % i,), scale=-8.0, bias=tn("yl8", i))
+        act(tn("hi", i), tn("sg1", i), Act.Identity, ("sg1", "hib"), ("hi%d" % i,), scale=8.0, bias=tn("hib", i))
+    quant("s2", 0, 128, T.s2t[:], ("s20", "s21"))
     for i in range(2):
         vred(tn("lpv", i), bank(i, 128), Op.max, ("b%d" % i,), ("lpv%d" % i,))
-    for i in range(2):
-        vts(T.s2t[:, i:512:2], T.k16[:], tn("gm", i), None, Op.is_equal, rd=("k16", "gm%d" % i), wr=("s2%d" % i,))
     vcp(T.invu[:], bank(2, 8), ("b2",), ("invu",))
     pickq("sl", 0, 96, "x", 192, T.invu[:, 0:6], ("xq", "invu"), ("slq",))
     pickp("sl", 0, 96, "x", 192, T.invu[:, 0:6], ("xp", "invu"), ("slp",))
     at = 32 + 32 * (3 - s)
     scatter([T.slq[:, 32 * i:32 * i + 32].bitcast(u8) for i in range(3)], T.winq[:, at:at + 32].bitcast(u8), others,
             "so", "lb", ("slq",), 0)
-    scatter([T.slp[:, 32 * i:32 * i + 32] for i in range(3)], T.winp[:, at:at + 32], others, "so", "lb", ("slp",), 3)
-    lastw["winq"] = lastw["winp"] = [("so", 24)]
-    y2 = ("yy0", "yy1")
-    vts(tn("hia"), tn("yy"), 16.0, 16.0, Op.is_gt, Op.mult, y2, ("hia",))
-    vts(tn("hib"), tn("yy"), 0.0, 32.0 * (3 - s), Op.is_gt, Op.mult, y2, ("hib",))
-    vts(tn("ylo"), tn("yy"), 0.0, None, Op.max, rd=y2, wr=("ylo",))
     vtt(tn("key"), tn("gd64"), tn("lpv"), Op.add, ("gd64", "lpv0", "lpv1"), ("key",))
-    vtt(tn("hi"), tn("hia"), tn("hib"), Op.add, ("hia", "hib"), ("hi",))
-    vtt(tn("lo"), tn("ylo"), tn("hia"), Op.subtract, ("ylo", "hia"), ("lo",))
     for i in range(2):
-        vts(T.m2t[:, i:64:4], T.kc[:], tn("key", i), tn("lo", i), Op.is_equal, Op.mult, ("kc", "key", "lo"), ("m2%d" % i,))
-        vts(T.m2t[:, 2 + i:64:4], T.kc[:], tn("key", i), tn("hi", i), Op.is_equal, Op.mult, ("kc", "key", "hi"), ("m2%d" % (2 + i),))
-    quant("s2", 0, 128, T.s2t[:], ("s20", "s21"))
+        vts(T.m2t[:, i:64:4], T.kc[:], tn("key", i), tn("lo", i), Op.is_equal, Op.mult,
+            ("kc", "key", "lo%d" % i), ("m2%d" % i,))
+        vts(T.m2t[:, 2 + i:64:4], T.kc[:], tn("key", i), tn("hi", i), Op.is_equal, Op.mult,
+            ("kc", "key", "hi%d" % i), ("m2%d" % (2 + i),))
     quant("m2", 0, 128, T.m2t[:], ("m20", "m21", "m22", "m23"))
     mm(3, 128, "s2", 0, "m2", 0)
     pickq("win", at, at + 32, "x", 192, T.invu[:, 6:8], ("xq", "invu", "winqz"), ("winqo",))
     pickp("win", at, at + 32, "x", 192, T.invu[:, 6:8], ("xp", "invu", "winpz"), ("winpo",))
     vcp(T.lst[:], bank(3, 16), ("b3",), ("lst",))
-    scatter([T.lst[:, 4 * r:4 * r + 4] for r in others], T.ll[:, 8 * s:8 * s + 4], others, "li", "lb", ("lst",), 0)
+    scatter([T.lst[:, 4 * r:4 * r + 4] for r in others], T.ll[:, 8 * s:8 * s + 4], others, "li", "lb", ("lst",), 3)
+    scatter([T.slp[:, 32 * i:32 * i + 32] for i in range(3)], T.winp[:, at:at + 32], others, "so", "lb", ("slp",), 2)
+    lastw["winq"] = lastw["winp"] = [("so", 24)]
     vcp(T.ll[:, 8 * s:8 * s + 4], T.lst[:, 4 * s:4 * s + 4], ("lst", "ll"), ("llo",))
     lastw["lli"] = [("li", 12)]
     if s < 3:
@@ -328,10 +336,13 @@ def rank_program(g, core, T, topo):
         for h in range(2):
             vtt(T.csum[:, h:8:2], T.nz[:, h:16:4], T.nz[:, 2 + h:16:4], Op.add, ("nz",), ("csum%d" % h,))
         higher = [r for r in others if r > s]
-        scatter([T.csum[:, 0:8]] * len(higher), T.lc[:, 8 * s:8 * s + 8], higher, "ct", "lb", ("csum0", "csum1"), 0)
+        scatter([T.csum[:, 0:8]] * len(higher), T.lc[:, 8 * s:8 * s + 8], higher, "ct", "lb", ("csum0", "csum1"), 1)
     if s > 0:
         lastw["lc"] = [("ct", 4 * s)]
 
+    iota(T.rst[:], [[0, 160]], 1, "rst")
+    iota(T.mgt[:, 0:192], [[0, 192]], -1, "mgta")
+    iota(T.mgt[:, 192:320], [[192, 4], [1, 32]], 0, "mgtb")
     quant("e", 0, 512, T.et[:], ("et0", "et1", "et2", "et3"))
     quant("w", 0, 512, T.wt[:], ("wt",))
     for b in range(4):
@@ -342,20 +353,39 @@ def rank_program(g, core, T, topo):
         act(T.da[:, 32 * b:32 * b + 32], bank(b, 32), Act.Copy, ("b%d" % b,), ("da%d" % b,))
     for i in range(4):
         act(T.hot[:, i:768:4], bank(4 + i, 192), Act.Relu, ("b%d" % (4 + i),), ("hot%d" % i,), scale=0.0625)
-    fill(T.mt[:], 0.0, "mt0", "mt1", "mt2", "mt3")
     fill(T.hmt[:], 0.0, "hmt0", "hmt1", "hmt2", "hmt3")
+    vts(cs(3), cs(5), 0.0625, None, Op.mult, rd=("c5",), wr=("c3",))
+    vts(T.s3t[:, 0:512:2], T.k16[:], cs(1), None, Op.is_equal, rd=("k16", "c1"), wr=("s3a",))
+    vts(cs(4), cs(3), 2.0, None, Op.add, rd=("c3",), wr=("c4",))
+    vts(T.s3t[96:128, 1:512:2], T.k16[96:128, :], T.cst[96:128, 1:2], None, Op.is_equal, rd=("k16", "c1"), wr=("s3b",))
+    for i in range(2):
+        vts(T.hot10[:, 10 * i:10 * i + 10], T.row[:, 0:10], cs(3 + i), None, Op.is_equal, rd=("row", "c%d" % (3 + i)),
+            wr=("h10%d" % i,))
+    quant("s3", 0, 128, T.s3t[:], ("s3a", "s3b"))
+    act(tn("gd16"), tn("gd"), Act.Copy, ("gd0", "gd1"), ("gd16",), scale=16.0)
+    act(tn("thz"), tn("lpv"), Act.Relu, ("lpv0", "lpv1"), ("thz",), bias=-30.0)
+    act(tn("thy"), tn("ylo"), Act.Sign, ("ylo",), ("thy",))
+    for i in range(2):
+        h10 = T.hot10[:, 10 * i:10 * i + 10]
+        act(T.tmt[:, 640 + i:680:4], h10, Act.Copy, ("h10%d" % i, "gm%d" % i), ("tm%d" % (2 + i),), scale=tn("gm", i))
+        act(T.tmt[:, 642 + i:680:4], h10, Act.Copy, ("h10%d" % i, "gd16"), ("tm%d" % (4 + i),), scale=tn("gd16", i))
+        act(tn("thr", i), tn("thz", i), Act.Copy, ("thz", "thy"), ("thr%d" % i,), scale=tn("thy", i))
+    act(T.tmt[:, 0:512:4], T.iden[:], Act.Copy, ("iden", "thr0"), ("tm0",), scale=tn("thr", 0))
+    act(T.tmt[:, 513:640:4], T.iden[:, 96:128], Act.Copy, ("iden", "thr1"), ("tm1",), scale=tn("thr", 1))
 
-    L = T.ll
+    L, X = T.ll, T.lab
     rl = ("ll", "llo", "lli")
-    vtt(T.la16[:], L[:, 0:16], L[:, 16:32], Op.max, rl, ("la16",))
-    vtt(T.lb16[:], L[:, 0:16], L[:, 16:32], Op.min, rl, ("lb16",))
-    vtt(T.lu[:], T.la16[:, 0:8], T.la16[:, 8:16], Op.max, ("la16",), ("lu",))
-    vtt(T.lcm[:], T.la16[:, 0:2], T.la16[:, 8:10], Op.min, ("la16",), ("lcm",))
-    vtt(T.lf[:], T.lb16[:, 0:2], T.lb16[:, 8:10], Op.max, ("lb16",), ("lf",))
-    vtt(T.lg[:], T.lcm[:], T.lf[:], Op.max, ("lcm", "lf"), ("lg",))
-    vtt(T.lu[:, 2:4], T.lg[:], T.lu[:, 2:4], Op.max, ("lg",), ("lu",))
-    vts(T.off[:], T.lu[:, 0:4], 31.0, None, Op.add, rd=("lu",), wr=("off",))
-    ww = lambda c: ("win" + c, "win" + c + "o", "win" + c + "z", "off")
+    vtt(X[:, 0:32:2], L[:, 0:16], L[:, 16:32], Op.max, rl, ("lab0",))
+    vtt(X[:, 1:32:2], L[:, 0:16], L[:, 16:32], Op.min, rl, ("lab1",))
+    vtt(T.lcm[:], X[:, 0:4:2], X[:, 16:20:2], Op.min, ("lab0",), ("lcm",))
+    vtt(T.lu[:], X[:, 0:16], X[:, 16:32], Op.max, ("lab0", "lab1"), ("lu",))
+    vtt(T.lf[:], T.lu[:, 1:4:2], T.lu[:, 4:8:2], Op.max, ("lu",), ("lf",))
+    vts(T.off[:, 0:2], T.lu[:, 0:4:2], 31.0, None, Op.add, rd=("lu",), wr=("off0",))
+    vtt(T.sec[:], T.lcm[:], T.lf[:], Op.max, ("lcm", "lf"), ("sec",))
+    vts(T.off[:, 2:4], T.sec[:], 31.0, None, Op.add, rd=("sec",), wr=("off1",))
+
+    def ww(c):
+        return ("win" + c, "win" + c + "o", "win" + c + "z", "off0", "off1")
     pickq("fs", 0, 64, "win", 160, T.off[:, 0:4], ww("q"), ("fsq",))
     pickp("fs", 0, 64, "win", 160, T.off[:, 0:4], ww("p"), ("fsp",))
     for b in range(4):
@@ -386,30 +416,9 @@ def rank_program(g, core, T, topo):
     bcast(T.hmp[:, 0:A], T.hwp[:, hat:hat + A], "hm", "lb", ("hmp",))
     lastw["hwq"] = lastw["hwp"] = [("hm", 96)]
 
-    fill(T.s3t[:], 0.0, "s3a", "s3b")
-    fill(T.tmt[:], 0.0, "tm0", "tm1", "tm2", "tm3", "tm4", "tm5")
-    vts(tn("thz"), tn("lpv"), 30.0, 0.0, Op.subtract, Op.max, ("lpv0", "lpv1"), ("thz",))
-    vts(tn("thy"), tn("yy"), 0.0, None, Op.is_gt, rd=y2, wr=("thy",))
-    vts(cs(3), cs(5), 0.0625, None, Op.mult, rd=("c5",), wr=("c3",))
-    vts(T.s3t[:, 0:512:2], T.k16[:], cs(1), None, Op.is_equal, rd=("k16", "c1"), wr=("s3a",))
-    vtt(tn("thr"), tn("thz"), tn("thy"), Op.mult, ("thz", "thy"), ("thr",))
-    vts(cs(4), cs(3), 2.0, None, Op.add, rd=("c3",), wr=("c4",))
-    vts(T.s3t[96:128, 1:512:2], T.k16[96:128, :], T.cst[96:128, 1:2], None, Op.is_equal, rd=("k16", "c1"), wr=("s3b",))
-    vts(T.tmt[:, 0:512:4], T.iden[:], tn("thr", 0), None, Op.mult, rd=("iden", "thr"), wr=("tm0",))
-    vts(T.tmt[:, 513:640:4], T.iden[:, 96:128], tn("thr", 1), None, Op.mult, rd=("iden", "thr"), wr=("tm1",))
-    for i in range(2):
-        vts(T.tmt[:, 640 + i:680:4], T.row[:, 0:10], cs(3 + i), tn("gm", i), Op.is_equal, Op.mult,
-            ("row", "c%d" % (3 + i), "gm%d" % i), ("tm%d" % (2 + i),))
-        vts(T.tmt[:, 642 + i:680:4], T.row[:, 0:10], cs(3 + i), tn("gd16", i), Op.is_equal, Op.mult,
-            ("row", "c%d" % (3 + i), "gd16"), ("tm%d" % (4 + i),))
     quant("tm", 0, 172, T.tmt[:], tuple("tm%d" % i for i in range(6)))
-    quant("s3", 0, 128, T.s3t[:], ("s3a", "s3b"))
     mm(1, 128, "s3", 0, "tm", 44)
     mm(0, 160, "s3", 0, "tm", 0)
-    vts(T.colm[:], T.colw[:], 192.0, None, Op.subtract, rd=("colw",), wr=("colm",))
-    fill(T.rst[:], 1.0, "rst")
-    fill(T.rst[:, 0:160:16], 0.0, "rst")
-    vcp(T.gwu[:], bank(1, 116, 126), ("b1",), ("gwu",))
     if s > 0:
         src, key = T.lc[:, 0:8], "lc"
         for r in range(1, s):
@@ -417,13 +426,14 @@ def rank_program(g, core, T, topo):
             src, key = T.ctot[:], "ctot"
         vcp(T.cu[:], src, (key,), ("cu",))
         act(T.crow[:], T.row[:, 0:128].indirect(T.cu[:, 0:8]), Act.Copy, ("row", "cu"), ("crow",))
+    vcp(T.gwu[:], bank(1, 116, 126), ("b1",), ("gwu",))
+    if s > 0:
         act(T.prior[:], T.crow[:, 0:128].indirect(T.gwu[:, 0:10]), Act.Copy, ("crow", "gwu"), ("prior",))
-    vtt(T.dw[:], bank(1, 116, 126), T.colm[:, 2:12], Op.subtract, ("b1", "colm"), ("dw",))
-    pickq("hw", hat, hat + A, "hm", 128, T.colu[:, 0:2], ("hmq", "colu"), ("hwqm",))
-    pickp("hw", hat, hat + A, "hm", 128, T.colu[:, 0:2], ("hmp", "colu"), ("hwpm",))
+    vts(T.colm[:], T.colw[:], 192.0, None, Op.subtract, rd=("colw",), wr=("colm",))
     quant("hw", 0, 192, T.hot[:], ("hot0", "hot1", "hot2", "hot3"), ("hwqo", "hwpo"))
-    quant("v", 0, 128, T.vt[:], ("vt",))
-    vts(T.fm[:], T.lu[:, 0:2], 0.0, 192.0 + A * s, Op.is_gt, Op.mult, ("lu",), ("fm",))
+    vtt(T.dw[:], bank(1, 116, 126), T.colm[:, 2:12], Op.subtract, ("b1", "colm"), ("dw",))
+    fill(T.rst[:, 0:160:16], 0.0, "rst")
+    vts(T.fm[:], T.lu[:, 0:4:2], 0.0, 192.0 + A * s, Op.is_gt, Op.mult, ("lu",), ("fm",))
     vtt(T.fin[:, 0:2], T.fm[:], T.colw[:, 0:2], Op.add, ("fm", "colw"), ("fin0",))
     if s > 0:
         vtt(T.adm[:], T.prior[:], bank(0, 160), Op.is_lt, ("prior", "b0"), ("adm",))
@@ -433,18 +443,25 @@ def rank_program(g, core, T, topo):
     vtt(T.admt[:], T.scn[:, 15:160:16], T.dw[:], Op.mult, ("scn", "dw"), ("admt",))
     vtt(T.fin[:, 2:12], T.admt[:], T.colw[:, 2:12], Op.add, ("admt", "colw"), ("fin1",))
     vcp(T.finu[:], T.fin[:], ("fin0", "fin1"), ("finu",))
-    fill(T.mgt[:, 0:192], -1.0, "mgta")
+    pickq("hw", hat, hat + A, "hm", 128, T.colu[:, 0:2], ("hmq", "colu"), ("hwqm",))
+    pickp("hw", hat, hat + A, "hm", 128, T.colu[:, 0:2], ("hmp", "colu"), ("hwpm",))
+    quant("v", 0, 128, T.vt[:], ("vt",))
     fill(T.mgr[:, 0:32], -1.0, "mgr0")
-    act(T.mgr[:, 32:192], T.mgt[:, 0:320].indirect(T.finu[:, 2:12]), Act.Copy, ("mgta", "mgtb", "finu"), ("mgr1",))
-    run("y", lambda: g.sync.dma_start(T.mg[0:1, 0:192], T.mgr[0:1, 0:192]), ("mgr0", "mgr1"), (), sem="dout")
 
-    hh = lambda c: ("hw" + c, "hw" + c + "m", "hw" + c + "o", "finu")
-    pickq("fo", 0, 192, "hw", 320, T.finu[:, 0:12], hh("q"), ("foq",))
-    pickp("fo", 0, 192, "hw", 320, T.finu[:, 0:12], hh("p"), ("fop",))
-    mm(2, 192, "v", 0, "fo", 0)
-    vcp(T.yo[:], bank(2, 192), ("b2",), ("yo",))
-    run("y", lambda: g.sync.dma_start(T.oc[:, 0:768], T.foq[:, 0:192].bitcast(u8)), ("foq",), (), sem="dout")
-    run("y", lambda: g.sync.dma_start(T.y[:, :], T.yo[:, :]), ("yo",), (), sem="dout")
+    def hh(c):
+        return ("hw" + c, "hw" + c + "m", "hw" + c + "o", "finu")
+    for i, (a, b) in enumerate([(0, 128), (128, 192)]):
+        pickq("fo", a, b, "hw", 320, T.finu[:, a // 16:b // 16], hh("q"), ("foq%d" % i,))
+        pickp("fo", a, b, "hw", 320, T.finu[:, a // 16:b // 16], hh("p"), ("fop%d" % i,))
+    mm(2, 128, "v", 0, "fo", 0, rd=("foq0", "fop0"))
+    mm(3, 128, "v", 0, "fo", 64, rd=("foq0", "fop0", "foq1", "fop1"))
+    vcp(T.yo[:, 0:128], bank(2, 128), ("b2",), ("yo0",))
+    vcp(T.yo[:, 128:192], bank(3, 64, 128), ("b3",), ("yo1",))
+    act(T.mgr[:, 32:192], T.mgt[:, 0:320].indirect(T.finu[:, 2:12]), Act.Copy, ("mgta", "mgtb", "finu"), ("mgr1",))
+    run("y", lambda: g.sync.dma_start(T.oc[:, 0:768], T.foq[:, 0:192].bitcast(u8)), ("foq0", "foq1"), (), sem="dout")
     for k in range(4):
-        run("s", lambda: S.dma_start(T.osc[4 * k:4 * k + 4, 0:192], T.fop[32 * k:32 * k + 4, 0:192]), ("fop",), (), sem="dout")
+        run("s", lambda: S.dma_start(T.osc[4 * k:4 * k + 4, 0:192], T.fop[32 * k:32 * k + 4, 0:192]), ("fop0", "fop1"), (),
+            sem="dout")
+    run("y", lambda: g.sync.dma_start(T.mg[0:1, 0:192], T.mgr[0:1, 0:192]), ("mgr0", "mgr1"), (), sem="dout")
+    run("y", lambda: g.sync.dma_start(T.y[:, :], T.yo[:, :]), ("yo0", "yo1"), (), sem="dout")
     wait("g", [(n, total[n]) for n in ("qv", "qs", "qt", "qg", "dout")] + [("lb", lsum["lb"])])

@@ -2,6 +2,7 @@ from concourse.bass import DstId, RemoteDMATransfer
 from concourse.mybir import dt, AluOpType as Op, AxisListType, ActivationFunctionType as Act
 
 A = 32
+EPS, TINY = 1.25 * 2.0 ** -24, 2.0 ** -125
 F, B16, I32, U16, CODE, PL = "float32", "bfloat16", "int32", "uint16", "float8_e4m3fn_x4", "uint8"
 
 SCRATCH = {}
@@ -19,20 +20,21 @@ def _mx(**names):
 
 
 SCRATCH["psum"] = ("psum", [128, 4096], F)
-_sb(I32, pidi=1, ui=1)
-_sb(F, cst=16, row=160, kc=16, kx=16, rli=40, colw=12, colm=12, lneg=320, zer=160, rst=160, seg=160, mgt=320,
-    rmax=256, md=160, rep=160, mrow=160, th=320, jnk=256, tiny=64, tri=256, kab=32,
-    da=128, uu=128, dw=10, crow=128, prior=160, adm=160, scn=160, admt=10, fin=12, fm=2, mgr=192, yo=192)
-_sb(B16, rowb=128, k16=256, kst=256, iden=128, et=2048, trt=1024, s3t=512, zt=512, xz=512, xt=768, wt=2048, vt=512,
-    cc=320, cj=320, ot=528, mmt=640, stt=512, s2t=512, m2t=512, tmt=688, mt=512, hmt=512, hot=768, hot10=20,
-    lst=16, nz=16, csum=8, ll=32, lc=24, lab=32, lu=16, lcm=2, lf=2, sec=2, ctot=8)
-_sb(U16, rlu=40, colu=12, invu=8, off=4, gwu=10, cu=8, finu=12)
-_mx(e=512, tr=256, s3=128, a=128, x=192, k=128, r=640, w=512, v=128, ob=132, mm=160, st=128, s2=128, m2=128, tm=172,
-    sl=96, win=160, fs=128, m=128, hm=128, hw=320, fo=192)
+_sb(I32, pidi=1, ui=2)
+_sb(F, cst=16, row=128, kc=16, kx=16, colw=12, colm=12, one=96, mk=96, tri32=32, rst=160, mgt=320,
+    rmax=256, m5=8, a5=8, rep=224, mrow=224, jnk=256, tiny=64, kab=16,
+    ss=128, dw=10, crow=128, prior=160, adm=160, scn=160, admt=10, fin=12, fm=2, mgr=192, yo=192)
+_sb(B16, rowb=128, k16=256, kst=256, iden=128, et=516, trt=1024, s3t=512, zt=512, xz=512, xt=1152, wt=2048, vt=512,
+    cc=320, cj=320, ot=536, mz=608, stt=512, s2t=512, tmt=688, mh=640, hot=768, hot10=20,
+    lst=16, nz=16, csum=8, ll=32, lc=24, lab=32, lu=16, lcm=2, lf=2, ctot=8)
+_sb(U16, colu=12, invu=8, off=4, gwu=10, cu=8, finu=12)
+_mx(e=512, tr=256, s3=128, a=128, x=288, k=192, w=512, v=128, ob=134, mm=136, st=128, s2=128, m2=128, tm=172,
+    sl=96, win=256, m=128, hm=128, hw=320, fo=192)
 
-SEMAPHORES = ["qv", "qs", "qt", "qg", "dxa", "dx", "dw", "dv", "an", "so", "li", "ct", "hm", "la", "lb", "dout"]
-_TINY = {n: 2 * i for i, n in enumerate(["ab", "ab2", "cn", "sel", "gg", "gd", "gq", "gm", "gd16", "gd64", "yy", "lpv",
-                                         "key", "hib", "hi", "ylo", "yl8", "lo", "thz", "thy", "thr", "sg1", "sg2"])}
+SEMAPHORES = ["qv", "qs", "qt", "qg", "dxa", "dx", "dx2", "dw", "dv", "dz1", "dz2", "dz3", "an", "so", "li", "ct", "hm",
+              "la", "lb", "dout"]
+_TINY = {n: 2 * i for i, n in enumerate(["cn", "gg", "gd", "gq", "gm", "gd16", "gd64", "yy", "lpv", "key", "hi", "yl8", "lo",
+                                         "thz", "thy", "thr", "sg1"])}
 
 
 def rank_program(g, core, T, topo):
@@ -94,11 +96,17 @@ def rank_program(g, core, T, topo):
     def vscan(out, d0, d1, init, op0, op1, rd=(), wr=()):
         run("v", lambda: V.tensor_tensor_scan(out, d0, d1, init, op0, op1), rd, wr)
 
+    def vtr(out, in_, rd=(), wr=()):
+        run("v", lambda: V.transpose(out, in_), rd, wr)
+
     def act(out, in_, func, rd=(), wr=(), **kw):
         run("s", lambda: S.activation(out, in_, func, **kw), rd, wr)
 
-    def iota(out, pattern, base, *wr):
-        run("g", lambda: g.iota(out, pattern, base, 0, allow_small_or_imprecise_dtypes=True), (), wr)
+    def iota(out, pattern, base, *wr, rd=()):
+        run("g", lambda: g.iota(out, pattern, base, 0, allow_small_or_imprecise_dtypes=True), rd, wr)
+
+    def select(out, in_, pattern, op, fl, base, cm, rd, wr):
+        run("g", lambda: g.affine_select(out, in_, pattern, op, fl, base, cm), rd, wr)
 
     def quant(n, a, b, src, rd=(), wr=None):
         run("v", lambda: V.quantize_mx(T[n + "q"][:, a:b], T[n + "p"][:, a:b], src), rd, wr or (n + "q", n + "p"))
@@ -106,18 +114,18 @@ def rank_program(g, core, T, topo):
     def bank(i, a, b=None):
         return T.psum[:, 512 * i:512 * i + a] if b is None else T.psum[:, 512 * i + a:512 * i + b]
 
-    def mm(i, n, ln, la, rn, ra, start=True, stop=True, rd=None):
+    def mm(i, n, ln, la, rn, ra, start=True, stop=True, rd=None, lrd=None):
         b = "b%d" % i
         run("t", lambda: P.matmul_mx(bank(i, n), T[ln + "q"][:, la:la + 128], T[ln + "p"][:, la:la + 128],
                                      T[rn + "q"][:, ra:ra + n], T[rn + "p"][:, ra:ra + n], start, stop),
-            (ln + "q", ln + "p") + (rd or (rn + "q", rn + "p")), (b,), free=() if start else (b,))
+            (lrd or (ln + "q", ln + "p")) + (rd or (rn + "q", rn + "p")), (b,), free=() if start else (b,))
 
-    def pickq(dn, c, d, sn, w, off, rd, wr):
+    def pickq(dn, c, d, sn, lo, hi, off, rd, wr):
         run("v", lambda: V.tensor_copy(T[dn + "q"][:, c:d].bitcast(dt.uint32),
-                                       T[sn + "q"][:, 0:w].bitcast(dt.uint32).indirect(off)), rd, wr)
+                                       T[sn + "q"][:, lo:hi].bitcast(dt.uint32).indirect(off)), rd, wr)
 
-    def pickp(dn, c, d, sn, w, off, rd, wr):
-        run("s", lambda: S.activation(T[dn + "p"][:, c:d], T[sn + "p"][:, 0:w].indirect(off), Act.Copy), rd, wr)
+    def pickp(dn, c, d, sn, lo, hi, off, rd, wr):
+        run("s", lambda: S.activation(T[dn + "p"][:, c:d], T[sn + "p"][:, lo:hi].indirect(off), Act.Copy), rd, wr)
 
     def tn(n, i=None):
         c = _TINY[n]
@@ -157,93 +165,95 @@ def rank_program(g, core, T, topo):
         return T.cst[:, j:j + 1]
 
     run("y", lambda: g.sync.dma_start(T.xz[:, 0:128], T.x[:, 0:128]), (), ("xza",), sem="dxa")
-    run("s", lambda: S.dma_start(T.xt[:, :], T.x[:, :]), (), ("xt",), sem="dx")
+    run("s", lambda: S.dma_start(T.xt[:, 0:768], T.x[:, :]), (), ("xt",), sem="dx")
+    run("y", lambda: g.sync.dma_start(T.xt[:, 768:1152], T.x[:, 128:512]), (), ("xt2",), sem="dx2")
 
     run("g", lambda: g.iota(T.pidi[:], [[0, 1]], 0, 1), (), ("pidi",))
-    iota(T.row[:], [[1, 160]], 0, "row")
-    iota(T.rli[:], [[32, 5], [0, 4], [16, 2]], A, "rli")
     iota(T.colw[:], [[16, 12]], 0, "colw")
+    iota(T.row[:], [[1, 128]], 0, "row")
+
+    fill(T.xz[:, 128:512], 0.0, "xzz")
+    fill(T.zt[:], 0.0, "zt")
+    fill(T.ll[:], 0.0, "ll")
+    run("v", lambda: V.tensor_scalar(T.ui[:, 0:1], T.pidi[:], 15, None, Op.bitwise_and), ("pidi",), ("ui",))
+    run("v", lambda: V.tensor_scalar(T.ui[:, 1:2], T.pidi[:], 31, None, Op.bitwise_and), ("pidi",), ("ui31",))
+    vcp(cs(0), T.pidi[:], ("pidi",), ("c0",))
+    vcp(cs(1), T.ui[:, 0:1], ("ui",), ("c1",))
+    vcp(cs(2), T.ui[:, 1:2], ("ui31",), ("c2",))
+    act(T.ot[:, 0:512], T.zt[:], Act.Copy, ("zt",), ("otA", "otB"))
+    act(T.ot[:, 512:536], T.zt[:, 0:24], Act.Copy, ("zt",), ("otC", "otD", "otZ"))
+    act(cs(8), cs(1), Act.Copy, ("c1",), ("c8",), scale=-1.0)
+    act(cs(5), cs(0), Act.Identity, ("c0", "c8"), ("c5",), bias=cs(8))
+    act(cs(3), cs(5), Act.Copy, ("c5",), ("c3",), scale=0.0625)
+    act(cs(6), cs(5), Act.Copy, ("c5",), ("c6",), bias=32.0)
+    act(cs(7), cs(5), Act.Copy, ("c5",), ("c7",), bias=64.0)
+    act(cs(4), cs(3), Act.Copy, ("c3",), ("c4",), bias=2.0)
+    act(cs(9), cs(6), Act.Copy, ("c6",), ("c9",), scale=-1.0)
+
+    quant("a", 0, 128, T.xz[:], ("xza", "xzz"))
+    at1 = 64 + A * s
+    bcast(T.aq[:, 0:A].bitcast(u8), T.kq[:, at1:at1 + A].bitcast(u8), "an", "la", ("aq",))
+    bcast(T.ap[:, 0:A], T.kp[:, at1:at1 + A], "an", "la", ("ap",))
+    lastw["kq"] = lastw["kp"] = [("an", 96)]
+    wait("y", [("la", lsum["la"])])
+    run("y", lambda: g.sync.dma_start(T.tmt[:, 0:512], T.zt[:, 0:512]), ("zt",), ("tm0",), sem="dz2")
+    run("y", lambda: g.sync.dma_start(T.tmt[:, 512:688], T.zt[:, 0:176]), ("zt",), ("tm1",), sem="dz3")
+    run("y", lambda: g.sync.dma_start(T.wt[:, :], T.w[:, :]), (), ("wt",), sem="dw")
+    run("y", lambda: g.sync.dma_start(T.mh[:, 128:512], T.zt[:, 0:384]), ("zt",), ("mhz",), sem="dz1")
+    run("y", lambda: g.sync.dma_start(T.vt[:, :], T.v[:, :]), (), ("vt",), sem="dv")
+    for i in range(2, 6):
+        lastw["tm%d" % i] = list(lastw["tm1"])
+
+    fill(T.one[:], 1.0, "one")
+    fill(T.trt[:], 0.0, "trA", "trB", "trB2")
+    vts(T.colw[:], T.colw[:], cs(1), None, Op.add, rd=("c1",), wr=("colw",))
+    vcp(T.colu[:], T.colw[:], ("colw",), ("colu",))
+    pickq("k", at1, at1 + A, "a", 0, 128, T.colu[:, 0:2], ("aq", "colu"), ("kqo",))
+    pickp("k", at1, at1 + A, "a", 0, 128, T.colu[:, 0:2], ("ap", "colu"), ("kpo",))
+    quant("x", 0, 288, T.xt[:], ("xt", "xt2"))
+    vts(T.tri32[:], T.row[:, 0:32], cs(2), None, Op.is_gt, rd=("row", "c2"), wr=("tri32",))
+    vts(T.iden[:], T.row[:], cs(0), None, Op.is_equal, rd=("row", "c0"), wr=("iden",))
+    fill(T.et[:], 0.0, "et")
+    act(T.et[:, 3:515:4], T.iden[:], Act.Copy, ("iden", "et"), ("et",), scale=0.5)
+    quant("win", 0, 128, T.zt[:], ("zt",), ("winqz", "winpz"))
+    fill(T.hot10[:], 0.0, "h100", "h101")
+    vts(T.hot10[:, 0:10], T.row[:, 0:10], cs(3), None, Op.is_equal, rd=("row", "c3"), wr=("h100",))
+    vts(T.hot10[96:128, 10:20], T.row[96:128, 0:10], T.cst[96:128, 4:5], None, Op.is_equal, rd=("row", "c4"), wr=("h101",))
+    for b in range(4):
+        quant("e", 128 * b, 128 * b + 128, T.et[:, 3 - b:515 - b], ("et",), ("eq%d" % b, "ep%d" % b))
+    act(T.mz[:, 0:512], T.zt[:], Act.Copy, ("zt",), ("mm0", "mm1", "mm2", "mm3", "mzz"))
+    act(T.mz[:, 512:608], T.zt[:, 0:96], Act.Copy, ("zt",), ("m20", "m21", "m22", "m23", "mzy"))
+    select(T.mk[:], T.one[:], [[32, 3], [0, 32]], Op.is_ge, 0.0, -96, 1, ("one",), ("mk",))
+    tp = [[-1, 128]]
+    select(T.trt[:, 0:512:4], T.trt[:, 0:512:4], tp, Op.is_ge, -1.0, 0, 1, ("trA",), ("trA",))
+    select(T.trt[:, 0:512:4], T.trt[:, 0:512:4], tp, Op.not_equal, 32.0, 0, 1, ("trA",), ("trA",))
+    tb, tq = T.trt[96:128, 897:1024:4], [[-1, 32]]
+    select(tb, tb, tq, Op.is_ge, -1.0, 0, 1, ("trA", "trB"), ("trB",))
+    select(tb, tb, tq, Op.not_equal, 32.0, 0, 1, ("trB",), ("trB",))
+    iota(T.trt[:, 896:1024:4], [[0, 32]], -1, "trB2", rd=("trB",))
+    iota(T.rowb[:], [[1, 128]], 0, "rowb")
+    for a, b in ((0, s), (s, 3), (3, 4)):
+        if b > a:
+            iota(T.kx[:, 4 * a:4 * b], [[1, b - a], [100, 2], [-100, 2]], order[a], "kx%d" % a)
+    kxs = tuple(k for k in ("kx0", "kx%d" % s, "kx3") if k in lastw)
+    iota(T.kst[:], [[0, 8], [1, 16], [16, 2]], 1, "kst")
     iota(T.k16[:], [[0, 8], [1, 16], [0, 2]], 0, "k16")
     iota(T.kc[:], [[128, 4], [-1, 2], [64, 2]], 32, "kc")
 
-    fill(T.zt[:], 0.0, "zt")
-    fill(T.xz[:, 128:512], 0.0, "xzz")
-    quant("win", 0, 128, T.zt[:], ("zt",), ("winqz", "winpz"))
-    quant("fs", 0, 128, T.zt[:], ("zt",))
-    fill(T.ll[:], 0.0, "ll")
-    vcp(cs(0), T.pidi[:], ("pidi",), ("c0",))
-    run("v", lambda: V.tensor_scalar(T.ui[:], T.pidi[:], 15, None, Op.bitwise_and), ("pidi",), ("ui",))
-    fill(T.zer[:], 0.0, "zer")
-    vcp(cs(1), T.ui[:], ("ui",), ("c1",))
-    vts(T.iden[:], T.row[:, 0:128], cs(0), None, Op.is_equal, rd=("row", "c0"), wr=("iden",))
-    vts(T.rlu[:], T.rli[:], cs(1), None, Op.add, rd=("rli", "c1"), wr=("rlu",))
-    vts(T.colw[:], T.colw[:], cs(1), None, Op.add, rd=("c1",), wr=("colw",))
-    fill(T.trt[:], 0.0, "trA", "trB")
-    vcp(T.colu[:], T.colw[:], ("colw",), ("colu",))
-    for b in range(4):
-        act(T.et[:, 512 * b:512 * b + 512], T.zt[:], Act.Copy, ("zt",), ("et%d" % b,))
-    for b in range(4):
-        act(T.et[:, 512 * b + b:512 * b + 512:4], T.iden[:], Act.Copy, ("iden",), ("et%d" % b,), scale=0.5)
-
-    quant("a", 0, 128, T.xz[:], ("xza", "xzz"))
-    bcast(T.aq[:, 0:A].bitcast(u8), T.kq[:, A * s:A * s + A].bitcast(u8), "an", "la", ("aq",))
-    bcast(T.ap[:, 0:A], T.kp[:, A * s:A * s + A], "an", "la", ("ap",))
-    lastw["kq"] = lastw["kp"] = [("an", 96)]
-    wait("y", [("la", lsum["la"])])
-    run("y", lambda: g.sync.dma_start(T.wt[:, :], T.w[:, :]), (), ("wt",), sem="dw")
-    run("y", lambda: g.sync.dma_start(T.vt[:, :], T.v[:, :]), (), ("vt",), sem="dv")
-
-    def sel_g(out, in_, pattern, op, fl, base, cm, rd, wr):
-        run("g", lambda: g.affine_select(out, in_, pattern, op, fl, base, cm), rd, wr)
-    sel_g(T.lneg[:, 0:160], T.zer[:], [[1, 160]], Op.is_ge, -1.0, 0, -1, ("zer",), ("ln0",))
-    sel_g(T.lneg[:, 160:320], T.zer[:], [[1, 160]], Op.is_ge, -1.0, -32, -1, ("zer",), ("ln1",))
-    iota(T.rowb[:], [[1, 128]], 0, "rowb")
-    iota(T.tmt[:], [[0, 688]], 0, *["tm%d" % i for i in range(6)])
-    iota(T.s3t[:], [[0, 512]], 0, "s3a", "s3b")
-    iota(T.mt[:], [[0, 512]], 0, "mt0", "mt1", "mt2", "mt3")
-    quant("x", 0, 192, T.xt[:], ("xt",))
-    own = (A * s, A * s + A)
-    pickq("k", own[0], own[1], "a", 128, T.colu[:, 0:2], ("aq", "colu"), ("kqo",))
-    pickp("k", own[0], own[1], "a", 128, T.colu[:, 0:2], ("ap", "colu"), ("kpo",))
-    pickq("r", 0, 640, "x", 192, T.rlu[:, 0:40], ("xq", "rlu"), ("rq",))
-    pickp("r", 0, 640, "x", 192, T.rlu[:, 0:40], ("xp", "rlu"), ("rp",))
-    fill(T.md[:], 0.0, "md0", "md1", "md2", "md3", "md4")
-    fill(T.seg[:], 1.0, "seg")
-    fill(T.seg[:, 0:160:32], 0.0, "seg")
-    vts(T.tri[:, 0:128], T.row[:, 0:128], cs(0), -1.0, Op.is_gt, Op.mult, rd=("row", "c0"), wr=("tri1",))
-    vts(T.tri[:, 128:256], T.row[:, 0:128], cs(0), 32.0, Op.is_equal, Op.mult, rd=("row", "c0"), wr=("tri2",))
-    fill(T.trt[:, 896:1024:4], -1.0, "trB2")
-    vtt(T.trt[:, 0:512:4], T.tri[:, 0:128], T.tri[:, 128:256], Op.add, ("tri1", "tri2"), ("trA",))
-    fill(T.kx[:], -1.0, "kx")
-    vcp(T.trt[96:128, 897:1024:4], T.trt[96:128, 384:512:4], ("trA",), ("trB",))
-    for i, r in enumerate(order):
-        fill(T.kx[:, 4 * i:4 * i + 4:3], float(r), "kx")
-    quant("tr", 0, 256, T.trt[:], ("trA", "trB", "trB2"))
-    vts(T.kst[:, 0:256:2], T.k16[:, 0:256:2], 1.0, None, Op.add, rd=("k16",), wr=("kst0",))
-    vts(T.kst[:, 1:256:2], T.k16[:, 1:256:2], 17.0, None, Op.add, rd=("k16",), wr=("kst1",))
-    vtt(cs(5), cs(0), cs(1), Op.subtract, ("c0", "c1"), ("c5",))
-    vts(cs(8), cs(1), -1.0, None, Op.mult, rd=("c1",), wr=("c8",))
-    vts(cs(6), cs(5), 32.0, None, Op.add, rd=("c5",), wr=("c6",))
-    vts(cs(7), cs(5), 64.0, None, Op.add, rd=("c5",), wr=("c7",))
-    vts(cs(9), cs(6), -1.0, None, Op.mult, rd=("c6",), wr=("c9",))
-    vts(cs(10), cs(7), -1.0, None, Op.mult, rd=("c7",), wr=("c10",))
-    act(T.mmt[:, 0:512], T.zt[:], Act.Copy, ("zt",), ("mm0", "mm1", "mm2", "mm3"))
-    act(T.mmt[:, 512:640], T.zt[:, 0:128], Act.Copy, ("zt",), ("mm4",))
-    act(T.ot[:, 0:512], T.zt[:], Act.Copy, ("zt",), ("otA", "otB"))
-    act(T.ot[:, 512:528], T.zt[:, 0:16], Act.Copy, ("zt",), ("otC", "otD"))
-    act(T.m2t[:], T.zt[:], Act.Copy, ("zt",), ("m20", "m21", "m22", "m23"))
-
     kk = ("kq", "kp", "kqo", "kpo")
-    mm(5, 128, "x", 32, "k", 0, rd=kk)
-    mm(6, 128, "x", 64, "k", 0, rd=kk)
-    for b in range(5):
-        mm(b, 128, "r", 128 * b, "k", 0, rd=kk)
-    for i in range(2):
-        vscan(T.rmax[:, 128 * i:128 * i + 128], bank(5 + i, 128), T.zer[:, 0:128], -1e29, Op.max, Op.add,
-              ("b%d" % (5 + i), "zer"), ("r%d" % i,))
-    for b in range(5):
-        vred(T.md[:, 32 * b:32 * b + 1], bank(b, 128), Op.max, ("b%d" % b,), ("md%d" % b,))
+    for j in (0, 4, 3, 2, 1):
+        mm(j, 128, "x", 32 + 32 * j, "k", 64, rd=kk)
     best = [T.rmax[:, 127:128], T.rmax[:, 255:256]]
+    top = {j: (T.m5[:, j:j + 1], "m%d" % j) for j in (2, 3, 4)}
+    top[0], top[1] = (best[0], "r0"), (best[1], "r1")
+
+    def lift(j):
+        m, k = top[j]
+        act(T.a5[:, j:j + 1], m, Act.Abs, (k,), ("a5%d" % j,), scale=EPS, bias=TINY)
+
+    def spread(j, c, mask, mk):
+        m, k = top[j]
+        act(T.rep[:, c:c + 32], mask, Act.Identity, (mk, k, "a5%d" % j), ("rep%d" % c,), scale=T.a5[:, j:j + 1], bias=m)
 
     def below(i, dst, a, step):
         end = 128 - (step > 1)
@@ -251,86 +261,120 @@ def rank_program(g, core, T, topo):
         act(T.jnk[:, 128 * i:128 * i + n], T.rmax[:, 128 * i + a:128 * i + end:step], Act.Sign, ("r%d" % i,),
             (dst + str(i), "jnk%d" % i), scale=-1.0, bias=best[i], accum_out=tn(dst, i))
 
-    act(tn("ab"), T.rmax[:, 127:256:128], Act.Abs, ("r0", "r1"), ("ab",), scale=1.25 * 2.0 ** -24)
-    act(tn("ab2"), tn("ab"), Act.Identity, ("ab",), ("ab2",), bias=2.0 ** -100)
+    def scan(i):
+        vscan(T.rmax[:, 128 * i:128 * i + 128], bank(i, 128), T.zt[:, 0:128], -1e29, Op.max, Op.add,
+              ("b%d" % i, "zt"), ("r%d" % i,))
+
+    def count(i):
+        c = slice(160 * i, 160 * i + 160)
+        act(T.cj[:, c], T.cc[:, c], Act.Copy, ("cc%d" % i,), ("cj%d" % i, "cn%d" % i), scale=1.0 / 64, accum_out=tn("cn", i))
+
+    scan(0)
+    lift(0)
+    spread(0, 0, T.tri32[:], "tri32")
+    spread(0, 160, T.one[:, 0:32], "one")
+    below(0, "gg", 0, 1)
+    for j in (4, 3, 2):
+        vred(top[j][0], bank(j, 128), Op.max, ("b%d" % j,), (top[j][1],))
+    act(T.a5[:, 2:5], T.m5[:, 2:5], Act.Abs, ("m2", "m3", "m4"), ("a52", "a53", "a54"), scale=EPS, bias=TINY)
+    for j in (4, 3):
+        spread(j, 32 * j, T.mk[:, 32 * j - 64:32 * j - 32], "mk")
+    scan(1)
+    lift(1)
+    spread(1, 192, T.tri32[:], "tri32")
+    below(1, "gg", 0, 1)
+    below(0, "gq", 31, 32)
+    below(1, "gq", 31, 32)
+    vts(T.rep[:, 64:96], T.mk[:, 0:32], T.a5[:, 2:3], top[2][0], Op.mult, Op.add, ("mk", "m2", "a52"), ("rep64",))
+    vts(T.rep[:, 32:64], T.row[:, 0:32], 0.0, best[1], Op.mult, Op.add, ("row", "r1"), ("rep32",))
+    vtr(T.mrow[:, 0:160], T.rep[:, 0:160], tuple("rep%d" % c for c in range(0, 160, 32)), ("mrow0",))
+    vts(T.cc[:, 0:160], T.mrow[:, 0:160], best[0], None, Op.is_gt, rd=("mrow0", "r0"), wr=("cc0",))
+    vtr(T.mrow[:, 160:224], T.rep[:, 160:224], ("rep160", "rep192"), ("mrow1",))
+    vts(T.cc[:, 160:320], T.mrow[:, 64:224], best[1], None, Op.is_gt, rd=("mrow0", "mrow1", "r1"), wr=("cc1",))
+    quant("tr", 0, 256, T.trt[:], ("trA", "trB", "trB2"))
+    count(0)
+    count(1)
     for i in range(2):
-        act(T.th[:, 160 * i:160 * i + 160], T.lneg[:, 160 * i:160 * i + 160], Act.Identity,
-            ("ln%d" % i, "ab2", "r%d" % i), ("th%d" % i,), scale=tn("ab2", i), bias=best[i])
-    for i in range(2):
-        below(i, "gg", 0, 1)
-        below(i, "gq", 31, 32)
+        vts(T.ot[:, i:512:4], T.rowb[:], tn("gg", i), tn("cn", i), Op.is_equal, Op.is_gt,
+            ("rowb", "gg%d" % i, "cn%d" % i), ("ot" + "AB"[i],))
+        vts(T.ot[:, 512 + i:528:4], T.rowb[:, 0:4], tn("gq", i), tn("cn", i), Op.is_equal, Op.is_gt,
+            ("rowb", "gq%d" % i, "cn%d" % i), ("ot" + "CD"[i],))
+    quant("ob", 0, 134, T.ot[:], ("otA", "otB", "otC", "otD", "otZ"))
+    mm(5, 134, "tr", 0, "ob", 0)
+    mm(6, 134, "tr", 128, "ob", 0)
+    act(T.kab[:], T.kx[:], Act.Abs, kxs + ("gq0",), ("kab",), scale=-1.0, bias=tn("gq", 0))
+    act(T.mz[:, 0:32:2], T.kab[:], Act.Relu, ("kab", "c1", "c8"), ("mm0",), scale=cs(8), bias=cs(1))
+    act(T.mz[:, 32:64:2], T.kab[:], Act.Relu, ("kab", "c6", "c9"), ("mm2",), scale=cs(9), bias=cs(6))
+    for k, c in ((1, 1), (3, 7)):
+        vts(T.mz[:, 16 * k - 15:16 * k + 16:2], T.kx[:], tn("gq", 1), cs(c), Op.is_equal, Op.mult,
+            kxs + ("gq1", "c%d" % c), ("mm%d" % k,))
+    quant("mm", 0, 136, T.mz[:, 0:544], ("mm0", "mm1", "mm2", "mm3", "mzz", "mzy"))
     for i in range(2):
         below(i, "gd", 15, 16)
     for i in range(2):
         act(tn("gm", i), tn("gd", i), Act.Identity, ("gd%d" % i, "gg%d" % i), ("gm%d" % i,), scale=-16.0, bias=tn("gg", i))
-    vscan(T.rep[:], T.seg[:], T.md[:], 0.0, Op.mult, Op.add, ("seg", "md0", "md1", "md2", "md3", "md4"), ("rep",))
-    run("v", lambda: V.transpose(T.mrow[:], T.rep[:]), ("rep",), ("mrow",))
-    for i in range(2):
-        c = slice(160 * i, 160 * i + 160)
-        vtt(T.cc[:, c], T.mrow[:], T.th[:, c], Op.is_gt, ("mrow", "th%d" % i), ("cc%d" % i,))
-        act(T.cj[:, c], T.cc[:, c], Act.Copy, ("cc%d" % i,), ("cj%d" % i, "cn%d" % i), accum_out=tn("cn", i))
-    for i in range(2):
-        vts(tn("sel", i), tn("cn", i), 64.0, None, Op.is_lt, rd=("cn%d" % i,), wr=("sel%d" % i,))
-        vts(T.ot[:, i:512:4], T.rowb[:], tn("gg", i), tn("sel", i), Op.is_equal, Op.mult,
-            ("rowb", "gg%d" % i, "sel%d" % i), ("ot" + "AB"[i],))
-        vts(T.ot[:, 512 + i:528:4], T.rowb[:, 0:4], tn("gq", i), tn("sel", i), Op.is_equal, Op.mult,
-            ("rowb", "gq%d" % i, "sel%d" % i), ("ot" + "CD"[i],))
-    quant("ob", 0, 132, T.ot[:], ("otA", "otB", "otC", "otD"))
-    mm(0, 132, "tr", 0, "ob", 0)
-    mm(1, 132, "tr", 128, "ob", 0)
-    for i in range(2):
-        act(T.kab[:, 16 * i:16 * i + 16], T.kx[:], Act.Abs, ("kx", "gq%d" % i), ("kab%d" % i,), scale=-1.0, bias=tn("gq", i))
-    for i in range(2):
-        kab = T.kab[:, 16 * i:16 * i + 16]
-        act(T.mmt[:, 64 + i:96:2], kab, Act.Relu, ("kab%d" % i, "c1", "c8"), ("mm%d" % i,), scale=cs(8), bias=cs(1))
-        act(T.mmt[:, 128 + i:160:2], kab, Act.Relu, ("kab%d" % i, "c%d" % (6 + i), "c%d" % (9 + i)), ("mm%d" % (2 + i),),
-            scale=cs(9 + i), bias=cs(6 + i))
     act(tn("gd64"), tn("gd"), Act.Copy, ("gd0", "gd1"), ("gd64",), scale=64.0)
     for i in range(2):
-        vts(T.s2t[:, i:512:2], T.k16[:], tn("gm", i), None, Op.is_equal, rd=("k16", "gm%d" % i), wr=("s2%d" % i,))
-    quant("mm", 0, 160, T.mmt[:], ("mm0", "mm1", "mm2", "mm3", "mm4"))
+        vred(tn("yy", i), bank(5 + i, 128, 133), Op.max, ("b%d" % (5 + i),), ("yy%d" % i,))
     for i in range(2):
-        vred(tn("yy", i), bank(i, 128, 132), Op.max, ("b%d" % i,), ("yy%d" % i,))
-    for i in range(2):
-        vts(T.stt[:, i:512:2], T.kst[:], tn("yy", i), None, Op.is_equal, rd=("kst0", "kst1", "yy%d" % i), wr=("st%d" % i,))
+        vts(T.stt[:, i:512:2], T.kst[:], tn("yy", i), None, Op.is_equal, rd=("kst", "yy%d" % i), wr=("st%d" % i,))
     quant("st", 0, 128, T.stt[:], ("st0", "st1"))
-    mm(2, 128, "st", 0, "mm", 16, True, False)
-    mm(2, 128, "st", 0, "mm", 32, False, True)
+    mm(7, 128, "st", 0, "mm", 0, True, False)
+    mm(7, 128, "st", 0, "mm", 8, False, True)
     y2 = ("yy0", "yy1")
-    k3 = 16.0 * (3 - s)
+    act(tn("thy"), tn("yy"), Act.Sign, y2, ("thy",))
+    for i in range(2):
+        act(T.jnk[:, 128 * i:128 * i + 128], bank(5 + i, 128), Act.Relu, ("b%d" % (5 + i), "yy%d" % i),
+            ("lpv%d" % i, "jnk%d" % i), accum_out=tn("lpv", i))
     act(tn("sg1"), tn("yy"), Act.Sign, y2, ("sg1",), bias=-16.5)
-    act(tn("sg2"), tn("yy"), Act.Sign, y2, ("sg2",), bias=-0.5)
-    act(tn("ylo"), tn("yy"), Act.Relu, y2, ("ylo",))
-    act(tn("hib"), tn("sg2"), Act.Identity, ("sg2",), ("hib",), scale=k3, bias=k3 + 8.0)
-    act(tn("yl8"), tn("ylo"), Act.Identity, ("ylo",), ("yl8",), bias=-8.0)
+    act(tn("yl8"), tn("yy"), Act.Copy, y2, ("yl8",), bias=-8.0)
+    for i in range(2):
+        act(tn("key", i), tn("lpv", i), Act.Identity, ("lpv%d" % i, "thy", "gd64"), ("key%d" % i,),
+            scale=tn("thy", i), bias=tn("gd64", i))
+    act(tn("hi"), tn("sg1"), Act.Copy, ("sg1",), ("hi",), scale=8.0, bias=32.0 * (3 - s) + 8.0)
     for i in range(2):
         act(tn("lo", i), tn("sg1", i), Act.Identity, ("sg1", "yl8"), ("lo%d" % i,), scale=-8.0, bias=tn("yl8", i))
-        act(tn("hi", i), tn("sg1", i), Act.Identity, ("sg1", "hib"), ("hi%d" % i,), scale=8.0, bias=tn("hib", i))
+    for i in range(2):
+        vts(T.s2t[:, i:512:2], T.k16[:], tn("gm", i), None, Op.is_equal, rd=("k16", "gm%d" % i), wr=("s2%d" % i,))
     quant("s2", 0, 128, T.s2t[:], ("s20", "s21"))
     for i in range(2):
-        vred(tn("lpv", i), bank(i, 128), Op.max, ("b%d" % i,), ("lpv%d" % i,))
-    vcp(T.invu[:], bank(2, 8), ("b2",), ("invu",))
-    pickq("sl", 0, 96, "x", 192, T.invu[:, 0:6], ("xq", "invu"), ("slq",))
-    pickp("sl", 0, 96, "x", 192, T.invu[:, 0:6], ("xp", "invu"), ("slp",))
-    at = 32 + 32 * (3 - s)
+        vts(T.mz[:, 546 + i:608:4], T.kc[:], tn("key", i), tn("hi", i), Op.is_equal, Op.mult,
+            ("kc", "key%d" % i, "hi"), ("m2%d" % (2 + i),))
+    for i in range(2):
+        vts(T.mz[:, 544 + i:608:4], T.kc[:], tn("key", i), tn("lo", i), Op.is_equal, Op.mult,
+            ("kc", "key%d" % i, "lo%d" % i), ("m2%d" % i,))
+    vcp(T.invu[:], bank(7, 8), ("b7",), ("invu",))
+    quant("m2", 0, 128, T.mz[:, 96:608], ("mzz", "mzy", "m20", "m21", "m22", "m23"))
+    mm(4, 128, "s2", 0, "m2", 0)
+    pickq("sl", 0, 96, "x", 0, 192, T.invu[:, 0:6], ("xq", "invu"), ("slq",))
+    pickp("sl", 0, 96, "x", 0, 192, T.invu[:, 0:6], ("xp", "invu"), ("slp",))
+    at = 128 + 32 * (3 - s)
+    vcp(T.lst[:], bank(4, 112, 128), ("b4",), ("lst",))
+    scatter([T.lst[:, 4 * r:4 * r + 4] for r in others], T.ll[:, 8 * s:8 * s + 4], others, "li", "lb", ("lst",), 3)
     scatter([T.slq[:, 32 * i:32 * i + 32].bitcast(u8) for i in range(3)], T.winq[:, at:at + 32].bitcast(u8), others,
             "so", "lb", ("slq",), 0)
-    vtt(tn("key"), tn("gd64"), tn("lpv"), Op.add, ("gd64", "lpv0", "lpv1"), ("key",))
-    for i in range(2):
-        vts(T.m2t[:, i:64:4], T.kc[:], tn("key", i), tn("lo", i), Op.is_equal, Op.mult,
-            ("kc", "key", "lo%d" % i), ("m2%d" % i,))
-        vts(T.m2t[:, 2 + i:64:4], T.kc[:], tn("key", i), tn("hi", i), Op.is_equal, Op.mult,
-            ("kc", "key", "hi%d" % i), ("m2%d" % (2 + i),))
-    quant("m2", 0, 128, T.m2t[:], ("m20", "m21", "m22", "m23"))
-    mm(3, 128, "s2", 0, "m2", 0)
-    pickq("win", at, at + 32, "x", 192, T.invu[:, 6:8], ("xq", "invu", "winqz"), ("winqo",))
-    pickp("win", at, at + 32, "x", 192, T.invu[:, 6:8], ("xp", "invu", "winpz"), ("winpo",))
-    vcp(T.lst[:], bank(3, 16), ("b3",), ("lst",))
-    scatter([T.lst[:, 4 * r:4 * r + 4] for r in others], T.ll[:, 8 * s:8 * s + 4], others, "li", "lb", ("lst",), 3)
     scatter([T.slp[:, 32 * i:32 * i + 32] for i in range(3)], T.winp[:, at:at + 32], others, "so", "lb", ("slp",), 2)
     lastw["winq"] = lastw["winp"] = [("so", 24)]
+    act(tn("gd16"), tn("gd"), Act.Copy, ("gd0", "gd1"), ("gd16",), scale=16.0)
+    act(tn("thz"), tn("lpv"), Act.Relu, ("lpv0", "lpv1"), ("thz",), bias=-30.0)
+    for i in range(2):
+        h10 = T.hot10[:, 10 * i:10 * i + 10]
+        act(T.tmt[:, 640 + i:680:4], h10, Act.Copy, ("h10%d" % i, "gm%d" % i), ("tm%d" % (2 + i),), scale=tn("gm", i))
+        act(T.tmt[:, 642 + i:680:4], h10, Act.Copy, ("h10%d" % i, "gd16"), ("tm%d" % (4 + i),), scale=tn("gd16", i))
+        act(tn("thr", i), tn("thz", i), Act.Copy, ("thz", "thy"), ("thr%d" % i,), scale=tn("thy", i))
+    act(T.tmt[:, 0:512:4], T.iden[:], Act.Copy, ("iden", "thr0"), ("tm0",), scale=tn("thr", 0))
+    act(T.tmt[:, 513:640:4], T.iden[:, 96:128], Act.Copy, ("iden", "thr1"), ("tm1",), scale=tn("thr", 1))
+    for i in range(4):
+        quant("w", 128 * i, 128 * i + 128, T.wt[:, 512 * i:512 * i + 512], ("wt",), ("wq%d" % i, "wp%d" % i))
+        mm((5, 6, 7, 4)[i], 192, "w", 128 * i, "x", 0, lrd=("wq%d" % i, "wp%d" % i))
+    pickq("win", at, at + 32, "x", 0, 192, T.invu[:, 6:8], ("xq", "invu"), ("winqo",))
+    pickp("win", at, at + 32, "x", 0, 192, T.invu[:, 6:8], ("xp", "invu"), ("winpo",))
     vcp(T.ll[:, 8 * s:8 * s + 4], T.lst[:, 4 * s:4 * s + 4], ("lst", "ll"), ("llo",))
     lastw["lli"] = [("li", 12)]
+    for b in range(4):
+        mm(b, 128, "e", 128 * b, "a", 0, True, False, lrd=("eq%d" % b, "ep%d" % b))
+    for i in (0, 2, 3):
+        act(T.hot[:, i:768:4], bank((5, 6, 7, 4)[i], 192), Act.Relu, ("b%d" % (5, 6, 7, 4)[i],), ("hot%d" % i,), scale=0.0625)
     if s < 3:
         vts(T.nz[:], T.lst[:], 0.0, None, Op.is_gt, rd=("lst",), wr=("nz",))
         for h in range(2):
@@ -339,129 +383,96 @@ def rank_program(g, core, T, topo):
         scatter([T.csum[:, 0:8]] * len(higher), T.lc[:, 8 * s:8 * s + 8], higher, "ct", "lb", ("csum0", "csum1"), 1)
     if s > 0:
         lastw["lc"] = [("ct", 4 * s)]
-
     iota(T.rst[:], [[0, 160]], 1, "rst")
     iota(T.mgt[:, 0:192], [[0, 192]], -1, "mgta")
     iota(T.mgt[:, 192:320], [[192, 4], [1, 32]], 0, "mgtb")
-    quant("e", 0, 512, T.et[:], ("et0", "et1", "et2", "et3"))
-    quant("w", 0, 512, T.wt[:], ("wt",))
-    for b in range(4):
-        mm(b, 128, "e", 128 * b, "x", 0)
-    for i in range(4):
-        mm(4 + i, 192, "w", 128 * i, "x", 0)
-    for b in range(4):
-        act(T.da[:, 32 * b:32 * b + 32], bank(b, 32), Act.Copy, ("b%d" % b,), ("da%d" % b,))
-    for i in range(4):
-        act(T.hot[:, i:768:4], bank(4 + i, 192), Act.Relu, ("b%d" % (4 + i),), ("hot%d" % i,), scale=0.0625)
-    fill(T.hmt[:], 0.0, "hmt0", "hmt1", "hmt2", "hmt3")
-    vts(cs(3), cs(5), 0.0625, None, Op.mult, rd=("c5",), wr=("c3",))
-    vts(T.s3t[:, 0:512:2], T.k16[:], cs(1), None, Op.is_equal, rd=("k16", "c1"), wr=("s3a",))
-    vts(cs(4), cs(3), 2.0, None, Op.add, rd=("c3",), wr=("c4",))
-    vts(T.s3t[96:128, 1:512:2], T.k16[96:128, :], T.cst[96:128, 1:2], None, Op.is_equal, rd=("k16", "c1"), wr=("s3b",))
+    vts(T.hot[:, 1:768:4], bank(6, 192), 0.0, 0.0625, Op.max, Op.mult, ("b6",), ("hot1",))
     for i in range(2):
-        vts(T.hot10[:, 10 * i:10 * i + 10], T.row[:, 0:10], cs(3 + i), None, Op.is_equal, rd=("row", "c%d" % (3 + i)),
-            wr=("h10%d" % i,))
-    quant("s3", 0, 128, T.s3t[:], ("s3a", "s3b"))
-    act(tn("gd16"), tn("gd"), Act.Copy, ("gd0", "gd1"), ("gd16",), scale=16.0)
-    act(tn("thz"), tn("lpv"), Act.Relu, ("lpv0", "lpv1"), ("thz",), bias=-30.0)
-    act(tn("thy"), tn("ylo"), Act.Sign, ("ylo",), ("thy",))
-    for i in range(2):
-        h10 = T.hot10[:, 10 * i:10 * i + 10]
-        act(T.tmt[:, 640 + i:680:4], h10, Act.Copy, ("h10%d" % i, "gm%d" % i), ("tm%d" % (2 + i),), scale=tn("gm", i))
-        act(T.tmt[:, 642 + i:680:4], h10, Act.Copy, ("h10%d" % i, "gd16"), ("tm%d" % (4 + i),), scale=tn("gd16", i))
-        act(tn("thr", i), tn("thz", i), Act.Copy, ("thz", "thy"), ("thr%d" % i,), scale=tn("thy", i))
-    act(T.tmt[:, 0:512:4], T.iden[:], Act.Copy, ("iden", "thr0"), ("tm0",), scale=tn("thr", 0))
-    act(T.tmt[:, 513:640:4], T.iden[:, 96:128], Act.Copy, ("iden", "thr1"), ("tm1",), scale=tn("thr", 1))
+        vts(T.s3t[:, i:512:2], T.k16[:], cs(1), None, Op.is_equal, rd=("k16", "c1"), wr=("s3%d" % i,))
+    quant("s3", 0, 128, T.s3t[:], ("s30", "s31"))
 
     L, X = T.ll, T.lab
     rl = ("ll", "llo", "lli")
     vtt(X[:, 0:32:2], L[:, 0:16], L[:, 16:32], Op.max, rl, ("lab0",))
     vtt(X[:, 1:32:2], L[:, 0:16], L[:, 16:32], Op.min, rl, ("lab1",))
-    vtt(T.lcm[:], X[:, 0:4:2], X[:, 16:20:2], Op.min, ("lab0",), ("lcm",))
     vtt(T.lu[:], X[:, 0:16], X[:, 16:32], Op.max, ("lab0", "lab1"), ("lu",))
+    vtt(T.lcm[:], X[:, 0:4:2], X[:, 16:20:2], Op.min, ("lab0",), ("lcm",))
     vtt(T.lf[:], T.lu[:, 1:4:2], T.lu[:, 4:8:2], Op.max, ("lu",), ("lf",))
-    vts(T.off[:, 0:2], T.lu[:, 0:4:2], 31.0, None, Op.add, rd=("lu",), wr=("off0",))
-    vtt(T.sec[:], T.lcm[:], T.lf[:], Op.max, ("lcm", "lf"), ("sec",))
-    vts(T.off[:, 2:4], T.sec[:], 31.0, None, Op.add, rd=("sec",), wr=("off1",))
+    vts(T.off[:, 0:2], T.lu[:, 0:4:2], 127.0, None, Op.add, rd=("lu",), wr=("off0",))
+    for h in range(2):
+        vts(T.off[:, 2 + h:3 + h], T.lcm[:, h:h + 1], T.lf[:, h:h + 1], 127.0, Op.max, Op.add, ("lcm", "lf"), ("off%d" % (1 + h),))
 
     def ww(c):
-        return ("win" + c, "win" + c + "o", "win" + c + "z", "off0", "off1")
-    pickq("fs", 0, 64, "win", 160, T.off[:, 0:4], ww("q"), ("fsq",))
-    pickp("fs", 0, 64, "win", 160, T.off[:, 0:4], ww("p"), ("fsp",))
+        return ("win" + c, "win" + c + "o", "win" + c + "z", "off0", "off1", "off2")
+    pickq("k", 0, 64, "win", 0, 256, T.off[:, 0:4], ww("q"), ("kqf",))
+    pickp("k", 0, 64, "win", 0, 256, T.off[:, 0:4], ww("p"), ("kpf",))
     for b in range(4):
-        mm(b, 128, "e", 128 * b, "fs", 0)
-
-    def add1(b):
-        vtt(T.uu[:, 32 * b:32 * b + 32], T.da[:, 32 * b:32 * b + 32], bank(b, 32), Op.add, ("da%d" % b, "b%d" % b), ("uu%d" % b,))
-
-    def add2(b):
-        vtt(T.mt[:, b:128:4], T.uu[:, 32 * b:32 * b + 32], bank(b, 32, 64), Op.add, ("uu%d" % b, "b%d" % b), ("mt%d" % b,))
-    add1(0)
-    for b in range(1, 4):
-        add1(b)
-        add2(b - 1)
-    add2(3)
-    quant("m", 0, 128, T.mt[:], ("mt0", "mt1", "mt2", "mt3"))
-    for i in range(4):
-        mm(4 + i, 128, "w", 128 * i, "m", 0)
-    for i in range(4):
-        k = ("b%d" % (4 + i),), ("hmt%d" % i,)
-        if i % 2 == 0:
-            act(T.hmt[:, i:128:4], bank(4 + i, 32), Act.Relu, k[0], k[1], scale=0.0625)
-        else:
-            vts(T.hmt[:, i:128:4], bank(4 + i, 32), 0.0, 0.0625, Op.max, Op.mult, k[0], k[1])
-    quant("hm", 0, 128, T.hmt[:], ("hmt0", "hmt1", "hmt2", "hmt3"))
-    hat = 192 + A * s
-    bcast(T.hmq[:, 0:A].bitcast(u8), T.hwq[:, hat:hat + A].bitcast(u8), "hm", "lb", ("hmq",))
-    bcast(T.hmp[:, 0:A], T.hwp[:, hat:hat + A], "hm", "lb", ("hmp",))
-    lastw["hwq"] = lastw["hwp"] = [("hm", 96)]
-
+        mm(b, 128, "e", 128 * b, "k", 0, False, True, rd=kk + ("kqf", "kpf"), lrd=("eq%d" % b, "ep%d" % b))
     quant("tm", 0, 172, T.tmt[:], tuple("tm%d" % i for i in range(6)))
-    mm(1, 128, "s3", 0, "tm", 44)
-    mm(0, 160, "s3", 0, "tm", 0)
+    mm(5, 128, "s3", 0, "tm", 44)
+    mm(4, 160, "s3", 0, "tm", 0)
+    vts(T.fm[:], T.lu[:, 0:4:2], 0.0, 192.0 + A * s, Op.is_gt, Op.mult, ("lu",), ("fm",))
+    vts(T.colm[:], T.colw[:], 192.0, None, Op.subtract, rd=("colw",), wr=("colm",))
+    fill(T.rst[:, 0:160:16], 0.0, "rst")
+    vtt(T.fin[:, 0:2], T.fm[:], T.colw[:, 0:2], Op.add, ("fm", "colw"), ("fin0",))
+    for b in range(4):
+        act(T.ss[:, 32 * b:32 * b + 32], bank(b, 32, 64), Act.Copy, ("b%d" % b,), ("ss%d" % b,))
+    for b in range(4):
+        vtt(T.mh[:, b:128:4], T.ss[:, 32 * b:32 * b + 32], bank(b, 32), Op.add, ("ss%d" % b, "b%d" % b), ("mt%d" % b,))
+    quant("m", 0, 128, T.mh[:, 0:512], ("mt0", "mt1", "mt2", "mt3", "mhz"))
+    for i in range(4):
+        mm(i, 128, "w", 128 * i, "m", 0, lrd=("wq%d" % i, "wp%d" % i))
     if s > 0:
         src, key = T.lc[:, 0:8], "lc"
         for r in range(1, s):
             vtt(T.ctot[:], src, T.lc[:, 8 * r:8 * r + 8], Op.add, ("lc", key), ("ctot",))
             src, key = T.ctot[:], "ctot"
         vcp(T.cu[:], src, (key,), ("cu",))
+    vcp(T.gwu[:], bank(5, 116, 126), ("b5",), ("gwu",))
+    vtt(T.dw[:], bank(5, 116, 126), T.colm[:, 2:12], Op.subtract, ("b5", "colm"), ("dw",))
+    for i in range(4):
+        k = ("b%d" % i,), ("hmt%d" % i,)
+        if i % 2 == 0:
+            act(T.mh[:, 512 + i:640:4], bank(i, 32), Act.Relu, k[0], k[1], scale=0.0625)
+        else:
+            vts(T.mh[:, 512 + i:640:4], bank(i, 32), 0.0, 0.0625, Op.max, Op.mult, k[0], k[1])
+    quant("hm", 0, 128, T.mh[:, 128:640], ("mhz", "hmt0", "hmt1", "hmt2", "hmt3"))
+    hat = 192 + A * s
+    bcast(T.hmq[:, 96:128].bitcast(u8), T.hwq[:, hat:hat + A].bitcast(u8), "hm", "lb", ("hmq",))
+    bcast(T.hmp[:, 96:128], T.hwp[:, hat:hat + A], "hm", "lb", ("hmp",))
+    lastw["hwq"] = lastw["hwp"] = [("hm", 96)]
+
+    if s > 0:
         act(T.crow[:], T.row[:, 0:128].indirect(T.cu[:, 0:8]), Act.Copy, ("row", "cu"), ("crow",))
-    vcp(T.gwu[:], bank(1, 116, 126), ("b1",), ("gwu",))
-    if s > 0:
         act(T.prior[:], T.crow[:, 0:128].indirect(T.gwu[:, 0:10]), Act.Copy, ("crow", "gwu"), ("prior",))
-    vts(T.colm[:], T.colw[:], 192.0, None, Op.subtract, rd=("colw",), wr=("colm",))
     quant("hw", 0, 192, T.hot[:], ("hot0", "hot1", "hot2", "hot3"), ("hwqo", "hwpo"))
-    vtt(T.dw[:], bank(1, 116, 126), T.colm[:, 2:12], Op.subtract, ("b1", "colm"), ("dw",))
-    fill(T.rst[:, 0:160:16], 0.0, "rst")
-    vts(T.fm[:], T.lu[:, 0:4:2], 0.0, 192.0 + A * s, Op.is_gt, Op.mult, ("lu",), ("fm",))
-    vtt(T.fin[:, 0:2], T.fm[:], T.colw[:, 0:2], Op.add, ("fm", "colw"), ("fin0",))
     if s > 0:
-        vtt(T.adm[:], T.prior[:], bank(0, 160), Op.is_lt, ("prior", "b0"), ("adm",))
+        vtt(T.adm[:], T.prior[:], bank(4, 160), Op.is_lt, ("prior", "b4"), ("adm",))
     else:
-        vts(T.adm[:], bank(0, 160), 0.0, None, Op.is_gt, rd=("b0",), wr=("adm",))
+        vts(T.adm[:], bank(4, 160), 0.0, None, Op.is_gt, rd=("b4",), wr=("adm",))
     vscan(T.scn[:], T.rst[:], T.adm[:], 0.0, Op.mult, Op.add, ("rst", "adm"), ("scn",))
     vtt(T.admt[:], T.scn[:, 15:160:16], T.dw[:], Op.mult, ("scn", "dw"), ("admt",))
     vtt(T.fin[:, 2:12], T.admt[:], T.colw[:, 2:12], Op.add, ("admt", "colw"), ("fin1",))
     vcp(T.finu[:], T.fin[:], ("fin0", "fin1"), ("finu",))
-    pickq("hw", hat, hat + A, "hm", 128, T.colu[:, 0:2], ("hmq", "colu"), ("hwqm",))
-    pickp("hw", hat, hat + A, "hm", 128, T.colu[:, 0:2], ("hmp", "colu"), ("hwpm",))
+    pickq("hw", hat, hat + A, "hm", 96, 128, T.colu[:, 0:2], ("hmq", "colu"), ("hwqm",))
+    pickp("hw", hat, hat + A, "hm", 96, 128, T.colu[:, 0:2], ("hmp", "colu"), ("hwpm",))
     quant("v", 0, 128, T.vt[:], ("vt",))
     fill(T.mgr[:, 0:32], -1.0, "mgr0")
 
     def hh(c):
         return ("hw" + c, "hw" + c + "m", "hw" + c + "o", "finu")
     for i, (a, b) in enumerate([(0, 128), (128, 192)]):
-        pickq("fo", a, b, "hw", 320, T.finu[:, a // 16:b // 16], hh("q"), ("foq%d" % i,))
-        pickp("fo", a, b, "hw", 320, T.finu[:, a // 16:b // 16], hh("p"), ("fop%d" % i,))
-    mm(2, 128, "v", 0, "fo", 0, rd=("foq0", "fop0"))
-    mm(3, 128, "v", 0, "fo", 64, rd=("foq0", "fop0", "foq1", "fop1"))
-    vcp(T.yo[:, 0:128], bank(2, 128), ("b2",), ("yo0",))
-    vcp(T.yo[:, 128:192], bank(3, 64, 128), ("b3",), ("yo1",))
-    act(T.mgr[:, 32:192], T.mgt[:, 0:320].indirect(T.finu[:, 2:12]), Act.Copy, ("mgta", "mgtb", "finu"), ("mgr1",))
+        pickq("fo", a, b, "hw", 0, 320, T.finu[:, a // 16:b // 16], hh("q"), ("foq%d" % i,))
+        pickp("fo", a, b, "hw", 0, 320, T.finu[:, a // 16:b // 16], hh("p"), ("fop%d" % i,))
     run("y", lambda: g.sync.dma_start(T.oc[:, 0:768], T.foq[:, 0:192].bitcast(u8)), ("foq0", "foq1"), (), sem="dout")
+    mm(6, 128, "v", 0, "fo", 0, rd=("foq0", "fop0"))
+    mm(7, 128, "v", 0, "fo", 64, rd=("foq0", "fop0", "foq1", "fop1"))
+    act(T.mgr[:, 32:192], T.mgt[:, 0:320].indirect(T.finu[:, 2:12]), Act.Copy, ("mgta", "mgtb", "finu"), ("mgr1",))
     for k in range(4):
         run("s", lambda: S.dma_start(T.osc[4 * k:4 * k + 4, 0:192], T.fop[32 * k:32 * k + 4, 0:192]), ("fop0", "fop1"), (),
             sem="dout")
-    run("y", lambda: g.sync.dma_start(T.mg[0:1, 0:192], T.mgr[0:1, 0:192]), ("mgr0", "mgr1"), (), sem="dout")
+    vcp(T.yo[:, 0:128], bank(6, 128), ("b6",), ("yo0",))
+    vcp(T.yo[:, 128:192], bank(7, 64, 128), ("b7",), ("yo1",))
     run("y", lambda: g.sync.dma_start(T.y[:, :], T.yo[:, :]), ("yo0", "yo1"), (), sem="dout")
+    run("s", lambda: S.dma_start(T.mg[0:1, 0:192], T.mgr[0:1, 0:192]), ("mgr0", "mgr1"), (), sem="dout")
     wait("g", [(n, total[n]) for n in ("qv", "qs", "qt", "qg", "dout")] + [("lb", lsum["lb"])])

@@ -3,7 +3,7 @@ from concourse.mybir import dt, AluOpType as Op, AxisListType, ActivationFunctio
 
 A = 32
 EPS, TINY = 1.25 * 2.0 ** -24, 2.0 ** -125
-F, B16, I32, U16, CODE, PL = "float32", "bfloat16", "int32", "uint16", "float8_e4m3fn_x4", "uint8"
+F, B16, U16, CODE, PL = "float32", "bfloat16", "uint16", "float8_e4m3fn_x4", "uint8"
 
 SCRATCH = {}
 
@@ -20,19 +20,19 @@ def _mx(**names):
 
 
 SCRATCH["psum"] = ("psum", [128, 4096], F)
-_sb(I32, pidi=1, ui=2)
-_sb(F, cst=16, row=128, kc=16, kx=16, colw=12, colm=12, one=96, mk=96, tri32=32, rst=160, mgt=320,
+_sb(F, cst=16, th=8, kc=16, kx=16, colw=12, colm=12, mk=96, tri32=32, rst=160, mgt=320,
     rmax=256, m5=8, a5=8, rep=224, mrow=224, jnk=256, tiny=64, kab=16,
     ss=128, dw=10, crow=128, prior=160, adm=160, scn=160, admt=10, fin=12, fm=2, mgr=192, yo=192)
-_sb(B16, rowb=128, k16=256, kst=256, iden=128, et=516, trt=1024, s3t=512, zt=512, xz=512, xt=1152, wt=2048, vt=512,
-    cc=320, cj=320, ot=536, mz=608, stt=512, s2t=512, tmt=688, mh=640, hot=768, hot10=20,
+_sb("int32", pidi=1, ui=1)
+_sb(B16, rowb=128, k16=256, kst=256, et=516, trt=640, s3t=512, zt=664, xz=512, xt=1152, wt=2048, vt=512,
+    cc=320, cj=320, ot=536, stt=512, s2t=512, tmt=688, mh=640, hot=768, hot10=20,
     lst=16, nz=16, csum=8, ll=32, lc=24, lab=32, lu=16, lcm=2, lf=2, ctot=8)
 _sb(U16, colu=12, invu=8, off=4, gwu=10, cu=8, finu=12)
-_mx(e=512, tr=256, s3=128, a=128, x=288, k=192, w=512, v=128, ob=134, mm=136, st=128, s2=128, m2=128, tm=172,
+_mx(e=512, tr=160, s3=128, a=128, x=288, k=192, w=512, v=128, ob=134, mm=136, st=128, s2=128, m2=128, tm=172,
     sl=96, win=256, m=128, hm=128, hw=320, fo=192)
 
-SEMAPHORES = ["qv", "qs", "qt", "qg", "dxa", "dx", "dx2", "dw", "dv", "dz1", "dz2", "dz3", "an", "so", "li", "ct", "hm",
-              "la", "lb", "dout"]
+SEMAPHORES = ["qv", "qs", "qt", "qg", "dxa", "dx", "dx2", "dw", "dv", "dz1", "dz2", "dz3", "dz4", "dkq", "dkp", "dzq", "dzp",
+              "an", "so", "li", "ct", "hm", "la", "lb", "dout"]
 _TINY = {n: 2 * i for i, n in enumerate(["cn", "gg", "gd", "gq", "gm", "gd16", "gd64", "yy", "lpv", "key", "hi", "yl8", "lo",
                                          "thz", "thy", "thr", "sg1"])}
 
@@ -102,11 +102,14 @@ def rank_program(g, core, T, topo):
     def act(out, in_, func, rd=(), wr=(), **kw):
         run("s", lambda: S.activation(out, in_, func, **kw), rd, wr)
 
-    def iota(out, pattern, base, *wr, rd=()):
-        run("g", lambda: g.iota(out, pattern, base, 0, allow_small_or_imprecise_dtypes=True), rd, wr)
+    def iota(out, pattern, base, *wr, rd=(), cm=0):
+        run("g", lambda: g.iota(out, pattern, base, cm, allow_small_or_imprecise_dtypes=True), rd, wr)
 
     def select(out, in_, pattern, op, fl, base, cm, rd, wr):
         run("g", lambda: g.affine_select(out, in_, pattern, op, fl, base, cm), rd, wr)
+
+    def sync(out, in_, sem, rd=(), wr=()):
+        run("y", lambda: g.sync.dma_start(out, in_), rd, wr, sem=sem)
 
     def quant(n, a, b, src, rd=(), wr=None):
         run("v", lambda: V.quantize_mx(T[n + "q"][:, a:b], T[n + "p"][:, a:b], src), rd, wr or (n + "q", n + "p"))
@@ -164,81 +167,79 @@ def rank_program(g, core, T, topo):
     def cs(j):
         return T.cst[:, j:j + 1]
 
-    run("y", lambda: g.sync.dma_start(T.xz[:, 0:128], T.x[:, 0:128]), (), ("xza",), sem="dxa")
+    D1, D2 = 64, 600
+    Z = T.zt[:, D1:D2]
+
+    sync(T.xz[:, 0:128], T.x[:, 0:128], "dxa", (), ("xza",))
     run("s", lambda: S.dma_start(T.xt[:, 0:768], T.x[:, :]), (), ("xt",), sem="dx")
-    run("y", lambda: g.sync.dma_start(T.xt[:, 768:1152], T.x[:, 128:512]), (), ("xt2",), sem="dx2")
+    sync(T.xt[:, 768:1152], T.x[:, 128:512], "dx2", (), ("xt2",))
 
     run("g", lambda: g.iota(T.pidi[:], [[0, 1]], 0, 1), (), ("pidi",))
-    iota(T.colw[:], [[16, 12]], 0, "colw")
-    iota(T.row[:], [[1, 128]], 0, "row")
+    iota(cs(0), [[0, 1]], 0, "c0", cm=1)
+    iota(T.rowb[:], [[1, 128]], 0, "rowb")
 
     fill(T.xz[:, 128:512], 0.0, "xzz")
-    fill(T.zt[:], 0.0, "zt")
+    run("v", lambda: V.tensor_scalar(T.ui[:], T.pidi[:], 31, None, Op.bitwise_and), ("pidi",), ("ui",))
+    fill(Z, 0.0, "zt")
+    vcp(cs(2), T.ui[:], ("ui",), ("c2",))
     fill(T.ll[:], 0.0, "ll")
-    run("v", lambda: V.tensor_scalar(T.ui[:, 0:1], T.pidi[:], 15, None, Op.bitwise_and), ("pidi",), ("ui",))
-    run("v", lambda: V.tensor_scalar(T.ui[:, 1:2], T.pidi[:], 31, None, Op.bitwise_and), ("pidi",), ("ui31",))
-    vcp(cs(0), T.pidi[:], ("pidi",), ("c0",))
-    vcp(cs(1), T.ui[:, 0:1], ("ui",), ("c1",))
-    vcp(cs(2), T.ui[:, 1:2], ("ui31",), ("c2",))
-    act(T.ot[:, 0:512], T.zt[:], Act.Copy, ("zt",), ("otA", "otB"))
-    act(T.ot[:, 512:536], T.zt[:, 0:24], Act.Copy, ("zt",), ("otC", "otD", "otZ"))
-    act(cs(8), cs(1), Act.Copy, ("c1",), ("c8",), scale=-1.0)
-    act(cs(5), cs(0), Act.Identity, ("c0", "c8"), ("c5",), bias=cs(8))
-    act(cs(3), cs(5), Act.Copy, ("c5",), ("c3",), scale=0.0625)
-    act(cs(6), cs(5), Act.Copy, ("c5",), ("c6",), bias=32.0)
-    act(cs(7), cs(5), Act.Copy, ("c5",), ("c7",), bias=64.0)
-    act(cs(4), cs(3), Act.Copy, ("c3",), ("c4",), bias=2.0)
-    act(cs(9), cs(6), Act.Copy, ("c6",), ("c9",), scale=-1.0)
-
     quant("a", 0, 128, T.xz[:], ("xza", "xzz"))
     at1 = 64 + A * s
     bcast(T.aq[:, 0:A].bitcast(u8), T.kq[:, at1:at1 + A].bitcast(u8), "an", "la", ("aq",))
     bcast(T.ap[:, 0:A], T.kp[:, at1:at1 + A], "an", "la", ("ap",))
     lastw["kq"] = lastw["kp"] = [("an", 96)]
+    iota(T.th[:, 0:7], [[0, 7]], 1, "th")
+    select(T.th[:, 0:7], T.th[:, 0:7], [[-16, 7]], Op.is_ge, 0.0, -16, 1, ("th",), ("th",))
+    sync(T.kq[:, at1:at1 + A].bitcast(u8), T.aq[:, 0:A].bitcast(u8), "dkq", ("aq",), ("kqo",))
+    sync(T.kp[:, at1:at1 + A], T.ap[:, 0:A], "dkp", ("ap",), ("kpo",))
     wait("y", [("la", lsum["la"])])
-    run("y", lambda: g.sync.dma_start(T.tmt[:, 0:512], T.zt[:, 0:512]), ("zt",), ("tm0",), sem="dz2")
-    run("y", lambda: g.sync.dma_start(T.tmt[:, 512:688], T.zt[:, 0:176]), ("zt",), ("tm1",), sem="dz3")
-    run("y", lambda: g.sync.dma_start(T.wt[:, :], T.w[:, :]), (), ("wt",), sem="dw")
-    run("y", lambda: g.sync.dma_start(T.mh[:, 128:512], T.zt[:, 0:384]), ("zt",), ("mhz",), sem="dz1")
-    run("y", lambda: g.sync.dma_start(T.vt[:, :], T.v[:, :]), (), ("vt",), sem="dv")
+    sync(T.ot[:, 0:536], Z, "dz4", ("zt",), ("otA", "otB", "otC", "otD", "otZ"))
+    sync(T.wt[:, :], T.w[:, :], "dw", (), ("wt",))
+    sync(T.winq[:, 96:128].bitcast(u8), T.aq[:, 96:128].bitcast(u8), "dzq", ("aq",), ("winqz",))
+    sync(T.winp[:, 96:128], T.ap[:, 96:128], "dzp", ("ap",), ("winpz",))
+    sync(T.tmt[:, 0:512], T.zt[:, D1:D1 + 512], "dz2", ("zt",), ("tm0",))
+    sync(T.tmt[:, 512:688], T.zt[:, D1:D1 + 176], "dz3", ("zt",), ("tm1",))
+    sync(T.mh[:, 128:512], T.zt[:, D1:D1 + 384], "dz1", ("zt",), ("mhz",))
+    sync(T.vt[:, :], T.v[:, :], "dv", (), ("vt",))
     for i in range(2, 6):
         lastw["tm%d" % i] = list(lastw["tm1"])
 
-    fill(T.one[:], 1.0, "one")
-    fill(T.trt[:], 0.0, "trA", "trB", "trB2")
-    vts(T.colw[:], T.colw[:], cs(1), None, Op.add, rd=("c1",), wr=("colw",))
-    vcp(T.colu[:], T.colw[:], ("colw",), ("colu",))
-    pickq("k", at1, at1 + A, "a", 0, 128, T.colu[:, 0:2], ("aq", "colu"), ("kqo",))
-    pickp("k", at1, at1 + A, "a", 0, 128, T.colu[:, 0:2], ("ap", "colu"), ("kpo",))
-    quant("x", 0, 288, T.xt[:], ("xt", "xt2"))
-    vts(T.tri32[:], T.row[:, 0:32], cs(2), None, Op.is_gt, rd=("row", "c2"), wr=("tri32",))
-    vts(T.iden[:], T.row[:], cs(0), None, Op.is_equal, rd=("row", "c0"), wr=("iden",))
     fill(T.et[:], 0.0, "et")
-    act(T.et[:, 3:515:4], T.iden[:], Act.Copy, ("iden", "et"), ("et",), scale=0.5)
-    quant("win", 0, 128, T.zt[:], ("zt",), ("winqz", "winpz"))
-    fill(T.hot10[:], 0.0, "h100", "h101")
-    vts(T.hot10[:, 0:10], T.row[:, 0:10], cs(3), None, Op.is_equal, rd=("row", "c3"), wr=("h100",))
-    vts(T.hot10[96:128, 10:20], T.row[96:128, 0:10], T.cst[96:128, 4:5], None, Op.is_equal, rd=("row", "c4"), wr=("h101",))
+    vts(T.et[:, 3:515:4], T.rowb[:], cs(0), 0.5, Op.is_equal, Op.mult, ("rowb", "c0"), ("et",))
+    quant("x", 0, 288, T.xt[:], ("xt", "xt2"))
     for b in range(4):
         quant("e", 128 * b, 128 * b + 128, T.et[:, 3 - b:515 - b], ("et",), ("eq%d" % b, "ep%d" % b))
-    act(T.mz[:, 0:512], T.zt[:], Act.Copy, ("zt",), ("mm0", "mm1", "mm2", "mm3", "mzz"))
-    act(T.mz[:, 512:608], T.zt[:, 0:96], Act.Copy, ("zt",), ("m20", "m21", "m22", "m23", "mzy"))
-    select(T.mk[:], T.one[:], [[32, 3], [0, 32]], Op.is_ge, 0.0, -96, 1, ("one",), ("mk",))
+    act(T.mk[:], T.zt[:, D1:D1 + 96], Act.Copy, ("zt",), ("mk",), bias=1.0)
+    act(T.trt[:, 0:512], T.zt[:, D1:D1 + 512], Act.Copy, ("zt",), ("trA",))
+    act(T.trt[:, 512:640], T.zt[:, D1:D1 + 128], Act.Copy, ("zt",), ("trB", "trB2"))
+    act(T.tri32[:], T.rowb[:, 0:32], Act.Sign, ("rowb", "c2"), ("tri32",), scale=-1.0, bias=cs(2))
+    act(T.tri32[:], T.tri32[:], Act.Relu, ("tri32",), ("tri32",), scale=-1.0)
+    act(T.jnk[:, 128:135], T.th[:, 0:7], Act.Copy, ("th",), ("jnk1", "c3"), accum_out=cs(3))
+    act(cs(1), cs(3), Act.Identity, ("c3", "c0"), ("c1",), scale=-16.0, bias=cs(0))
+    act(cs(6), cs(3), Act.Copy, ("c3",), ("c6",), scale=16.0, bias=32.0)
+    act(cs(7), cs(3), Act.Copy, ("c3",), ("c7",), scale=16.0, bias=64.0)
+    act(cs(8), cs(1), Act.Copy, ("c1",), ("c8",), scale=-1.0)
+    act(cs(9), cs(3), Act.Copy, ("c3",), ("c9",), scale=-16.0, bias=-32.0)
+    select(T.mk[:], T.mk[:], [[32, 3], [0, 32]], Op.is_ge, 0.0, -96, 1, ("mk",), ("mk",))
     tp = [[-1, 128]]
     select(T.trt[:, 0:512:4], T.trt[:, 0:512:4], tp, Op.is_ge, -1.0, 0, 1, ("trA",), ("trA",))
     select(T.trt[:, 0:512:4], T.trt[:, 0:512:4], tp, Op.not_equal, 32.0, 0, 1, ("trA",), ("trA",))
-    tb, tq = T.trt[96:128, 897:1024:4], [[-1, 32]]
-    select(tb, tb, tq, Op.is_ge, -1.0, 0, 1, ("trA", "trB"), ("trB",))
-    select(tb, tb, tq, Op.not_equal, 32.0, 0, 1, ("trB",), ("trB",))
-    iota(T.trt[:, 896:1024:4], [[0, 32]], -1, "trB2", rd=("trB",))
-    iota(T.rowb[:], [[1, 128]], 0, "rowb")
+    iota(T.trt[:, 512:640:4], [[0, 32]], -1, "trB2")
+    c = _TINY["yy"]
+    iota(T.tiny[:, c:c + 4], [[0, 4]], 0, "yy0", "yy1", "lpv0", "lpv1")
     for a, b in ((0, s), (s, 3), (3, 4)):
         if b > a:
             iota(T.kx[:, 4 * a:4 * b], [[1, b - a], [100, 2], [-100, 2]], order[a], "kx%d" % a)
     kxs = tuple(k for k in ("kx0", "kx%d" % s, "kx3") if k in lastw)
-    iota(T.kst[:], [[0, 8], [1, 16], [16, 2]], 1, "kst")
     iota(T.k16[:], [[0, 8], [1, 16], [0, 2]], 0, "k16")
+    iota(T.kst[:], [[0, 8], [1, 16], [16, 2]], 1, "kst")
     iota(T.kc[:], [[128, 4], [-1, 2], [64, 2]], 32, "kc")
+    h10 = ("h100", "h101")
+    iota(T.hot10[:], [[0, 20]], 1, *h10)
+    select(T.hot10[:], T.hot10[:], [[32, 2], [-16, 10]], Op.is_ge, 0.0, 0, 1, h10, h10)
+    select(T.hot10[:], T.hot10[:], [[-32, 2], [16, 10]], Op.is_ge, 0.0, 15, -1, h10, h10)
+    select(T.hot10[:, 10:20], T.hot10[:, 10:20], [[0, 10]], Op.is_ge, 0.0, -96, 1, h10, h10)
+    iota(T.colw[:], [[16, 12]], 0, "colw")
 
     kk = ("kq", "kp", "kqo", "kpo")
     for j in (0, 4, 3, 2, 1):
@@ -262,7 +263,7 @@ def rank_program(g, core, T, topo):
             (dst + str(i), "jnk%d" % i), scale=-1.0, bias=best[i], accum_out=tn(dst, i))
 
     def scan(i):
-        vscan(T.rmax[:, 128 * i:128 * i + 128], bank(i, 128), T.zt[:, 0:128], -1e29, Op.max, Op.add,
+        vscan(T.rmax[:, 128 * i:128 * i + 128], bank(i, 128), T.zt[:, D1:D1 + 128], -1e29, Op.max, Op.add,
               ("b%d" % i, "zt"), ("r%d" % i,))
 
     def count(i):
@@ -272,7 +273,6 @@ def rank_program(g, core, T, topo):
     scan(0)
     lift(0)
     spread(0, 0, T.tri32[:], "tri32")
-    spread(0, 160, T.one[:, 0:32], "one")
     below(0, "gg", 0, 1)
     for j in (4, 3, 2):
         vred(top[j][0], bank(j, 128), Op.max, ("b%d" % j,), (top[j][1],))
@@ -282,50 +282,67 @@ def rank_program(g, core, T, topo):
     scan(1)
     lift(1)
     spread(1, 192, T.tri32[:], "tri32")
+    for b in range(4):
+        mm(b, 128, "e", 128 * b, "a", 0, True, False, lrd=("eq%d" % b, "ep%d" % b))
     below(1, "gg", 0, 1)
     below(0, "gq", 31, 32)
     below(1, "gq", 31, 32)
+    vts(T.rep[:, 160:192], T.mk[:, 0:32], T.a5[:, 0:1], best[0], Op.mult, Op.add, ("mk", "r0", "a50"), ("rep160",))
     vts(T.rep[:, 64:96], T.mk[:, 0:32], T.a5[:, 2:3], top[2][0], Op.mult, Op.add, ("mk", "m2", "a52"), ("rep64",))
-    vts(T.rep[:, 32:64], T.row[:, 0:32], 0.0, best[1], Op.mult, Op.add, ("row", "r1"), ("rep32",))
+    vts(T.rep[:, 32:64], T.rowb[:, 0:32], 0.0, best[1], Op.mult, Op.add, ("rowb", "r1"), ("rep32",))
     vtr(T.mrow[:, 0:160], T.rep[:, 0:160], tuple("rep%d" % c for c in range(0, 160, 32)), ("mrow0",))
-    vts(T.cc[:, 0:160], T.mrow[:, 0:160], best[0], None, Op.is_gt, rd=("mrow0", "r0"), wr=("cc0",))
     vtr(T.mrow[:, 160:224], T.rep[:, 160:224], ("rep160", "rep192"), ("mrow1",))
+    vts(T.cc[:, 0:160], T.mrow[:, 0:160], best[0], None, Op.is_gt, rd=("mrow0", "r0"), wr=("cc0",))
     vts(T.cc[:, 160:320], T.mrow[:, 64:224], best[1], None, Op.is_gt, rd=("mrow0", "mrow1", "r1"), wr=("cc1",))
-    quant("tr", 0, 256, T.trt[:], ("trA", "trB", "trB2"))
     count(0)
     count(1)
+
+    def mzb(k, c):
+        vts(T.zt[:, 16 * k - 15:16 * k + 16:2], T.kx[:], tn("gq", 1), cs(c), Op.is_equal, Op.mult,
+            kxs + ("gq1", "c%d" % c), ("mm%d" % k,))
+
+    vcp(T.trt[96:128, 513:640:4], T.trt[96:128, 384:512:4], ("trA", "trB"), ("trB",))
+    quant("tr", 0, 160, T.trt[:], ("trA", "trB", "trB2"))
     for i in range(2):
         vts(T.ot[:, i:512:4], T.rowb[:], tn("gg", i), tn("cn", i), Op.is_equal, Op.is_gt,
             ("rowb", "gg%d" % i, "cn%d" % i), ("ot" + "AB"[i],))
         vts(T.ot[:, 512 + i:528:4], T.rowb[:, 0:4], tn("gq", i), tn("cn", i), Op.is_equal, Op.is_gt,
             ("rowb", "gq%d" % i, "cn%d" % i), ("ot" + "CD"[i],))
+        if i == 0:
+            mzb(1, 1)
     quant("ob", 0, 134, T.ot[:], ("otA", "otB", "otC", "otD", "otZ"))
     mm(5, 134, "tr", 0, "ob", 0)
-    mm(6, 134, "tr", 128, "ob", 0)
+    mm(6, 134, "tr", 32, "ob", 0)
     act(T.kab[:], T.kx[:], Act.Abs, kxs + ("gq0",), ("kab",), scale=-1.0, bias=tn("gq", 0))
-    act(T.mz[:, 0:32:2], T.kab[:], Act.Relu, ("kab", "c1", "c8"), ("mm0",), scale=cs(8), bias=cs(1))
-    act(T.mz[:, 32:64:2], T.kab[:], Act.Relu, ("kab", "c6", "c9"), ("mm2",), scale=cs(9), bias=cs(6))
-    for k, c in ((1, 1), (3, 7)):
-        vts(T.mz[:, 16 * k - 15:16 * k + 16:2], T.kx[:], tn("gq", 1), cs(c), Op.is_equal, Op.mult,
-            kxs + ("gq1", "c%d" % c), ("mm%d" % k,))
-    quant("mm", 0, 136, T.mz[:, 0:544], ("mm0", "mm1", "mm2", "mm3", "mzz", "mzy"))
-    for i in range(2):
-        below(i, "gd", 15, 16)
+    act(T.zt[:, 0:32:2], T.kab[:], Act.Relu, ("kab", "c1", "c8"), ("mm0",), scale=cs(8), bias=cs(1))
+    act(T.zt[:, 32:64:2], T.kab[:], Act.Relu, ("kab", "c6", "c9"), ("mm2",), scale=cs(9), bias=cs(6))
+    mzb(3, 7)
+    quant("mm", 0, 136, T.zt[:, 0:544], ("mm0", "mm1", "mm2", "mm3", "zt"))
+    below(0, "gd", 15, 16)
+    below(1, "gd", 15, 16)
     for i in range(2):
         act(tn("gm", i), tn("gd", i), Act.Identity, ("gd%d" % i, "gg%d" % i), ("gm%d" % i,), scale=-16.0, bias=tn("gg", i))
     act(tn("gd64"), tn("gd"), Act.Copy, ("gd0", "gd1"), ("gd64",), scale=64.0)
-    for i in range(2):
-        vred(tn("yy", i), bank(5 + i, 128, 133), Op.max, ("b%d" % (5 + i),), ("yy%d" % i,))
+    c = _TINY["yy"]
+    vred(T.tiny[:, c:c + 1], bank(5, 128, 133), Op.max, ("b5",), ("yy0",))
+    vred(T.tiny[96:128, c + 1:c + 2], T.psum[96:128, 6 * 512 + 128:6 * 512 + 133], Op.max, ("b6",), ("yy1",))
     for i in range(2):
         vts(T.stt[:, i:512:2], T.kst[:], tn("yy", i), None, Op.is_equal, rd=("kst", "yy%d" % i), wr=("st%d" % i,))
+
+    def s2(i):
+        vts(T.s2t[:, i:512:2], T.k16[:], tn("gm", i), None, Op.is_equal, rd=("k16", "gm%d" % i), wr=("s2%d" % i,))
+
+    s2(0)
     quant("st", 0, 128, T.stt[:], ("st0", "st1"))
+    s2(1)
     mm(7, 128, "st", 0, "mm", 0, True, False)
     mm(7, 128, "st", 0, "mm", 8, False, True)
     y2 = ("yy0", "yy1")
     act(tn("thy"), tn("yy"), Act.Sign, y2, ("thy",))
-    for i in range(2):
-        act(T.jnk[:, 128 * i:128 * i + 128], bank(5 + i, 128), Act.Relu, ("b%d" % (5 + i), "yy%d" % i),
-            ("lpv%d" % i, "jnk%d" % i), accum_out=tn("lpv", i))
+    c = _TINY["lpv"]
+    act(T.jnk[:, 0:128], bank(5, 128), Act.Relu, ("b5", "yy0"), ("lpv0", "jnk0"), accum_out=T.tiny[:, c:c + 1])
+    act(T.jnk[96:128, 128:256], T.psum[96:128, 6 * 512:6 * 512 + 128], Act.Relu, ("b6", "yy1"), ("lpv1", "jnk1"),
+        accum_out=T.tiny[96:128, c + 1:c + 2])
     act(tn("sg1"), tn("yy"), Act.Sign, y2, ("sg1",), bias=-16.5)
     act(tn("yl8"), tn("yy"), Act.Copy, y2, ("yl8",), bias=-8.0)
     for i in range(2):
@@ -334,17 +351,15 @@ def rank_program(g, core, T, topo):
     act(tn("hi"), tn("sg1"), Act.Copy, ("sg1",), ("hi",), scale=8.0, bias=32.0 * (3 - s) + 8.0)
     for i in range(2):
         act(tn("lo", i), tn("sg1", i), Act.Identity, ("sg1", "yl8"), ("lo%d" % i,), scale=-8.0, bias=tn("yl8", i))
-    for i in range(2):
-        vts(T.s2t[:, i:512:2], T.k16[:], tn("gm", i), None, Op.is_equal, rd=("k16", "gm%d" % i), wr=("s2%d" % i,))
     quant("s2", 0, 128, T.s2t[:], ("s20", "s21"))
     for i in range(2):
-        vts(T.mz[:, 546 + i:608:4], T.kc[:], tn("key", i), tn("hi", i), Op.is_equal, Op.mult,
+        vts(T.zt[:, D2 + 2 + i:D2 + 64:4], T.kc[:], tn("key", i), tn("hi", i), Op.is_equal, Op.mult,
             ("kc", "key%d" % i, "hi"), ("m2%d" % (2 + i),))
     for i in range(2):
-        vts(T.mz[:, 544 + i:608:4], T.kc[:], tn("key", i), tn("lo", i), Op.is_equal, Op.mult,
+        vts(T.zt[:, D2 + i:D2 + 64:4], T.kc[:], tn("key", i), tn("lo", i), Op.is_equal, Op.mult,
             ("kc", "key%d" % i, "lo%d" % i), ("m2%d" % i,))
     vcp(T.invu[:], bank(7, 8), ("b7",), ("invu",))
-    quant("m2", 0, 128, T.mz[:, 96:608], ("mzz", "mzy", "m20", "m21", "m22", "m23"))
+    quant("m2", 0, 128, T.zt[:, D2 + 64 - 512:D2 + 64], ("zt", "m20", "m21", "m22", "m23"))
     mm(4, 128, "s2", 0, "m2", 0)
     pickq("sl", 0, 96, "x", 0, 192, T.invu[:, 0:6], ("xq", "invu"), ("slq",))
     pickp("sl", 0, 96, "x", 0, 192, T.invu[:, 0:6], ("xp", "invu"), ("slp",))
@@ -355,41 +370,44 @@ def rank_program(g, core, T, topo):
             "so", "lb", ("slq",), 0)
     scatter([T.slp[:, 32 * i:32 * i + 32] for i in range(3)], T.winp[:, at:at + 32], others, "so", "lb", ("slp",), 2)
     lastw["winq"] = lastw["winp"] = [("so", 24)]
-    act(tn("gd16"), tn("gd"), Act.Copy, ("gd0", "gd1"), ("gd16",), scale=16.0)
-    act(tn("thz"), tn("lpv"), Act.Relu, ("lpv0", "lpv1"), ("thz",), bias=-30.0)
-    for i in range(2):
-        h10 = T.hot10[:, 10 * i:10 * i + 10]
-        act(T.tmt[:, 640 + i:680:4], h10, Act.Copy, ("h10%d" % i, "gm%d" % i), ("tm%d" % (2 + i),), scale=tn("gm", i))
-        act(T.tmt[:, 642 + i:680:4], h10, Act.Copy, ("h10%d" % i, "gd16"), ("tm%d" % (4 + i),), scale=tn("gd16", i))
-        act(tn("thr", i), tn("thz", i), Act.Copy, ("thz", "thy"), ("thr%d" % i,), scale=tn("thy", i))
-    act(T.tmt[:, 0:512:4], T.iden[:], Act.Copy, ("iden", "thr0"), ("tm0",), scale=tn("thr", 0))
-    act(T.tmt[:, 513:640:4], T.iden[:, 96:128], Act.Copy, ("iden", "thr1"), ("tm1",), scale=tn("thr", 1))
-    for i in range(4):
-        quant("w", 128 * i, 128 * i + 128, T.wt[:, 512 * i:512 * i + 512], ("wt",), ("wq%d" % i, "wp%d" % i))
-        mm((5, 6, 7, 4)[i], 192, "w", 128 * i, "x", 0, lrd=("wq%d" % i, "wp%d" % i))
-    pickq("win", at, at + 32, "x", 0, 192, T.invu[:, 6:8], ("xq", "invu"), ("winqo",))
-    pickp("win", at, at + 32, "x", 0, 192, T.invu[:, 6:8], ("xp", "invu"), ("winpo",))
-    vcp(T.ll[:, 8 * s:8 * s + 4], T.lst[:, 4 * s:4 * s + 4], ("lst", "ll"), ("llo",))
     lastw["lli"] = [("li", 12)]
-    for b in range(4):
-        mm(b, 128, "e", 128 * b, "a", 0, True, False, lrd=("eq%d" % b, "ep%d" % b))
-    for i in (0, 2, 3):
-        act(T.hot[:, i:768:4], bank((5, 6, 7, 4)[i], 192), Act.Relu, ("b%d" % (5, 6, 7, 4)[i],), ("hot%d" % i,), scale=0.0625)
     if s < 3:
-        vts(T.nz[:], T.lst[:], 0.0, None, Op.is_gt, rd=("lst",), wr=("nz",))
-        for h in range(2):
-            vtt(T.csum[:, h:8:2], T.nz[:, h:16:4], T.nz[:, 2 + h:16:4], Op.add, ("nz",), ("csum%d" % h,))
-        higher = [r for r in others if r > s]
-        scatter([T.csum[:, 0:8]] * len(higher), T.lc[:, 8 * s:8 * s + 8], higher, "ct", "lb", ("csum0", "csum1"), 1)
-    if s > 0:
-        lastw["lc"] = [("ct", 4 * s)]
+        act(T.nz[:], T.lst[:], Act.Sign, ("lst",), ("nz",))
+    pickp("win", at, at + 32, "x", 0, 192, T.invu[:, 6:8], ("xp", "invu"), ("winpo",))
+    act(tn("thz"), tn("lpv"), Act.Relu, ("lpv0", "lpv1"), ("thz",), scale=2.0, bias=-60.0)
+    act(tn("gd16"), tn("gd"), Act.Copy, ("gd0", "gd1"), ("gd16",), scale=16.0)
+    for i in range(2):
+        act(tn("thr", i), tn("thz", i), Act.Copy, ("thz", "thy"), ("thr%d" % i,), scale=tn("thy", i))
+    for i in range(2):
+        hj = T.hot10[:, 10 * i:10 * i + 10]
+        act(T.tmt[:, 640 + i:680:4], hj, Act.Copy, ("h10%d" % i, "gm%d" % i), ("tm%d" % (2 + i),), scale=tn("gm", i))
+        act(T.tmt[:, 642 + i:680:4], hj, Act.Copy, ("h10%d" % i, "gd16"), ("tm%d" % (4 + i),), scale=tn("gd16", i))
+    act(T.tmt[:, 0:512:4], T.et[:, 3:515:4], Act.Copy, ("et", "thr0"), ("tm0",), scale=tn("thr", 0))
+    act(T.tmt[:, 513:640:4], T.et[:, 387:515:4], Act.Copy, ("et", "thr1"), ("tm1",), scale=tn("thr", 1))
+    act(T.colw[:], T.colw[:], Act.Identity, ("colw", "c1"), ("colw",), bias=cs(1))
+    HB = (5, 6, 7, 4)
+
+    def hot(i):
+        act(T.hot[:, i:768:4], bank(HB[i], 192), Act.Relu, ("b%d" % HB[i],), ("hot%d" % i,), scale=0.0625)
+
+    for i in (0, 3, 1, 2):
+        quant("w", 128 * i, 128 * i + 128, T.wt[:, 512 * i:512 * i + 512], ("wt",), ("wq%d" % i, "wp%d" % i))
+        mm(HB[i], 192, "w", 128 * i, "x", 0, lrd=("wq%d" % i, "wp%d" % i))
+        if i == 3 and s < 3:
+            for h in range(2):
+                vtt(T.csum[:, h:8:2], T.nz[:, h:16:4], T.nz[:, 2 + h:16:4], Op.add, ("nz",), ("csum%d" % h,))
+            higher = [r for r in others if r > s]
+            scatter([T.csum[:, 0:8]] * len(higher), T.lc[:, 8 * s:8 * s + 8], higher, "ct", "lb", ("csum0", "csum1"), 1)
+    vcp(T.ll[:, 8 * s:8 * s + 4], T.lst[:, 4 * s:4 * s + 4], ("lst", "ll"), ("llo",))
+    pickq("win", at, at + 32, "x", 0, 192, T.invu[:, 6:8], ("xq", "invu"), ("winqo",))
+    hot(0)
+    hot(3)
+    act(T.colm[:], T.colw[:], Act.Copy, ("colw",), ("colm",), bias=-192.0)
     iota(T.rst[:], [[0, 160]], 1, "rst")
+    select(T.rst[:], T.rst[:], [[0, 10], [1, 16]], Op.not_equal, 0.0, 0, 0, ("rst",), ("rst",))
     iota(T.mgt[:, 0:192], [[0, 192]], -1, "mgta")
     iota(T.mgt[:, 192:320], [[192, 4], [1, 32]], 0, "mgtb")
-    vts(T.hot[:, 1:768:4], bank(6, 192), 0.0, 0.0625, Op.max, Op.mult, ("b6",), ("hot1",))
-    for i in range(2):
-        vts(T.s3t[:, i:512:2], T.k16[:], cs(1), None, Op.is_equal, rd=("k16", "c1"), wr=("s3%d" % i,))
-    quant("s3", 0, 128, T.s3t[:], ("s30", "s31"))
+    iota(T.mgr[:, 0:32], [[0, 32]], -1, "mgr0")
 
     L, X = T.ll, T.lab
     rl = ("ll", "llo", "lli")
@@ -408,13 +426,16 @@ def rank_program(g, core, T, topo):
     pickp("k", 0, 64, "win", 0, 256, T.off[:, 0:4], ww("p"), ("kpf",))
     for b in range(4):
         mm(b, 128, "e", 128 * b, "k", 0, False, True, rd=kk + ("kqf", "kpf"), lrd=("eq%d" % b, "ep%d" % b))
+    hot(1)
+    if s > 0:
+        lastw["lc"] = [("ct", 4 * s)]
+    for i in range(2):
+        vts(T.s3t[:, i:512:2], T.k16[:], cs(1), None, Op.is_equal, rd=("k16", "c1"), wr=("s3%d" % i,))
     quant("tm", 0, 172, T.tmt[:], tuple("tm%d" % i for i in range(6)))
+    quant("s3", 0, 128, T.s3t[:], ("s30", "s31"))
+    vcp(T.colu[:], T.colw[:], ("colw",), ("colu",))
     mm(5, 128, "s3", 0, "tm", 44)
     mm(4, 160, "s3", 0, "tm", 0)
-    vts(T.fm[:], T.lu[:, 0:4:2], 0.0, 192.0 + A * s, Op.is_gt, Op.mult, ("lu",), ("fm",))
-    vts(T.colm[:], T.colw[:], 192.0, None, Op.subtract, rd=("colw",), wr=("colm",))
-    fill(T.rst[:, 0:160:16], 0.0, "rst")
-    vtt(T.fin[:, 0:2], T.fm[:], T.colw[:, 0:2], Op.add, ("fm", "colw"), ("fin0",))
     for b in range(4):
         act(T.ss[:, 32 * b:32 * b + 32], bank(b, 32, 64), Act.Copy, ("b%d" % b,), ("ss%d" % b,))
     for b in range(4):
@@ -422,57 +443,59 @@ def rank_program(g, core, T, topo):
     quant("m", 0, 128, T.mh[:, 0:512], ("mt0", "mt1", "mt2", "mt3", "mhz"))
     for i in range(4):
         mm(i, 128, "w", 128 * i, "m", 0, lrd=("wq%d" % i, "wp%d" % i))
+    vcp(T.gwu[:], bank(5, 116, 126), ("b5",), ("gwu",))
     if s > 0:
         src, key = T.lc[:, 0:8], "lc"
         for r in range(1, s):
             vtt(T.ctot[:], src, T.lc[:, 8 * r:8 * r + 8], Op.add, ("lc", key), ("ctot",))
             src, key = T.ctot[:], "ctot"
         vcp(T.cu[:], src, (key,), ("cu",))
-    vcp(T.gwu[:], bank(5, 116, 126), ("b5",), ("gwu",))
+        act(T.crow[:], T.rowb[:, 0:128].indirect(T.cu[:, 0:8]), Act.Copy, ("rowb", "cu"), ("crow",))
     vtt(T.dw[:], bank(5, 116, 126), T.colm[:, 2:12], Op.subtract, ("b5", "colm"), ("dw",))
+    vts(T.hot[:, 2:768:4], bank(HB[2], 192), 0.0, 0.0625, Op.max, Op.mult, ("b%d" % HB[2],), ("hot2",))
     for i in range(4):
         k = ("b%d" % i,), ("hmt%d" % i,)
         if i % 2 == 0:
             act(T.mh[:, 512 + i:640:4], bank(i, 32), Act.Relu, k[0], k[1], scale=0.0625)
         else:
             vts(T.mh[:, 512 + i:640:4], bank(i, 32), 0.0, 0.0625, Op.max, Op.mult, k[0], k[1])
+    if s > 0:
+        act(T.prior[:], T.crow[:, 0:128].indirect(T.gwu[:, 0:10]), Act.Copy, ("crow", "gwu"), ("prior",))
     quant("hm", 0, 128, T.mh[:, 128:640], ("mhz", "hmt0", "hmt1", "hmt2", "hmt3"))
     hat = 192 + A * s
     bcast(T.hmq[:, 96:128].bitcast(u8), T.hwq[:, hat:hat + A].bitcast(u8), "hm", "lb", ("hmq",))
     bcast(T.hmp[:, 96:128], T.hwp[:, hat:hat + A], "hm", "lb", ("hmp",))
     lastw["hwq"] = lastw["hwp"] = [("hm", 96)]
+    pickp("hw", hat, hat + A, "hm", 96, 128, T.colu[:, 0:2], ("hmp", "colu"), ("hwpm",))
 
-    if s > 0:
-        act(T.crow[:], T.row[:, 0:128].indirect(T.cu[:, 0:8]), Act.Copy, ("row", "cu"), ("crow",))
-        act(T.prior[:], T.crow[:, 0:128].indirect(T.gwu[:, 0:10]), Act.Copy, ("crow", "gwu"), ("prior",))
     quant("hw", 0, 192, T.hot[:], ("hot0", "hot1", "hot2", "hot3"), ("hwqo", "hwpo"))
     if s > 0:
         vtt(T.adm[:], T.prior[:], bank(4, 160), Op.is_lt, ("prior", "b4"), ("adm",))
     else:
         vts(T.adm[:], bank(4, 160), 0.0, None, Op.is_gt, rd=("b4",), wr=("adm",))
+    vts(T.fm[:], T.lu[:, 0:4:2], 0.0, 192.0 + A * s, Op.is_gt, Op.mult, ("lu",), ("fm",))
     vscan(T.scn[:], T.rst[:], T.adm[:], 0.0, Op.mult, Op.add, ("rst", "adm"), ("scn",))
+    vtt(T.fin[:, 0:2], T.fm[:], T.colw[:, 0:2], Op.add, ("fm", "colw"), ("fin0",))
     vtt(T.admt[:], T.scn[:, 15:160:16], T.dw[:], Op.mult, ("scn", "dw"), ("admt",))
     vtt(T.fin[:, 2:12], T.admt[:], T.colw[:, 2:12], Op.add, ("admt", "colw"), ("fin1",))
-    vcp(T.finu[:], T.fin[:], ("fin0", "fin1"), ("finu",))
     pickq("hw", hat, hat + A, "hm", 96, 128, T.colu[:, 0:2], ("hmq", "colu"), ("hwqm",))
-    pickp("hw", hat, hat + A, "hm", 96, 128, T.colu[:, 0:2], ("hmp", "colu"), ("hwpm",))
+    vcp(T.finu[:], T.fin[:], ("fin0", "fin1"), ("finu",))
     quant("v", 0, 128, T.vt[:], ("vt",))
-    fill(T.mgr[:, 0:32], -1.0, "mgr0")
 
     def hh(c):
         return ("hw" + c, "hw" + c + "m", "hw" + c + "o", "finu")
     for i, (a, b) in enumerate([(0, 128), (128, 192)]):
         pickq("fo", a, b, "hw", 0, 320, T.finu[:, a // 16:b // 16], hh("q"), ("foq%d" % i,))
         pickp("fo", a, b, "hw", 0, 320, T.finu[:, a // 16:b // 16], hh("p"), ("fop%d" % i,))
-    run("y", lambda: g.sync.dma_start(T.oc[:, 0:768], T.foq[:, 0:192].bitcast(u8)), ("foq0", "foq1"), (), sem="dout")
+    sync(T.oc[:, 0:768], T.foq[:, 0:192].bitcast(u8), "dout", ("foq0", "foq1"))
+    for k in range(4):
+        sync(T.osc[4 * k:4 * k + 4, 0:192], T.fop[32 * k:32 * k + 4, 0:192], "dout", ("fop0", "fop1"))
     mm(6, 128, "v", 0, "fo", 0, rd=("foq0", "fop0"))
     mm(7, 128, "v", 0, "fo", 64, rd=("foq0", "fop0", "foq1", "fop1"))
     act(T.mgr[:, 32:192], T.mgt[:, 0:320].indirect(T.finu[:, 2:12]), Act.Copy, ("mgta", "mgtb", "finu"), ("mgr1",))
-    for k in range(4):
-        run("s", lambda: S.dma_start(T.osc[4 * k:4 * k + 4, 0:192], T.fop[32 * k:32 * k + 4, 0:192]), ("fop0", "fop1"), (),
-            sem="dout")
-    vcp(T.yo[:, 0:128], bank(6, 128), ("b6",), ("yo0",))
-    vcp(T.yo[:, 128:192], bank(7, 64, 128), ("b7",), ("yo1",))
-    run("y", lambda: g.sync.dma_start(T.y[:, :], T.yo[:, :]), ("yo0", "yo1"), (), sem="dout")
     run("s", lambda: S.dma_start(T.mg[0:1, 0:192], T.mgr[0:1, 0:192]), ("mgr0", "mgr1"), (), sem="dout")
+    vcp(T.yo[:, 0:128], bank(6, 128), ("b6",), ("yo0",))
+    sync(T.y[:, 0:128], T.yo[:, 0:128], "dout", ("yo0",))
+    vcp(T.yo[:, 128:192], bank(7, 64, 128), ("b7",), ("yo1",))
+    sync(T.y[:, 128:192], T.yo[:, 128:192], "dout", ("yo1",))
     wait("g", [(n, total[n]) for n in ("qv", "qs", "qt", "qg", "dout")] + [("lb", lsum["lb"])])

from concourse.bass import DstId, RemoteDMATransfer
from concourse.mybir import dt, AluOpType as Op, AxisListType, ActivationFunctionType as Act

A = 32
EPS, TINY = 1.25 * 2.0 ** -24, 2.0 ** -125
F, B16, U16, CODE, PL = "float32", "bfloat16", "uint16", "float8_e4m3fn_x4", "uint8"

SCRATCH = {}


def _sb(dtype, **names):
    for n, w in names.items():
        SCRATCH[n] = ("sbuf", [128, w], dtype)


def _mx(**names):
    for n, w in names.items():
        SCRATCH[n + "q"] = ("sbuf", [128, w], CODE)
        SCRATCH[n + "p"] = ("sbuf", [128, w], PL)


SCRATCH["psum"] = ("psum", [128, 4096], F)
_sb(F, cst=16, th=8, kc=16, kx=16, colw=12, colm=12, mk=96, tri32=32, rst=160, mgt=320,
    rmax=256, m5=8, a5=8, rep=224, mrow=224, jnk=256, tiny=64, kab=16,
    ss=128, dw=10, crow=128, prior=160, adm=160, scn=160, admt=10, fin=12, fm=2, mgr=192, yo=192)
_sb("int32", pidi=1, ui=1)
_sb(B16, rowb=128, k16=256, kst=256, et=516, trt=640, s3t=512, zt=664, xz=512, xt=1152, wt=2048, vt=512,
    cc=320, cj=320, ot=536, stt=512, s2t=512, tmt=688, mh=640, hot=768, hot10=20,
    lst=16, nz=16, csum=8, ll=32, lc=24, lab=32, lu=16, lcm=2, lf=2, ctot=8)
_sb(U16, colu=12, invu=8, off=4, gwu=10, cu=8, finu=12)
_mx(e=512, tr=160, s3=128, a=128, x=288, k=192, w=512, v=128, ob=134, mm=136, st=128, s2=128, m2=128, tm=172,
    sl=96, win=256, m=128, hm=128, hw=320, fo=192)

SEMAPHORES = ["qv", "qs", "qt", "qg", "dxa", "dx", "dx2", "dw", "dv", "dz1", "dz2", "dz3", "dz4", "dkq", "dkp", "dzq", "dzp",
              "an", "so", "li", "ct", "hm", "la", "lb", "dout"]
_TINY = {n: 2 * i for i, n in enumerate(["cn", "gg", "gd", "gq", "gm", "gd16", "gd64", "yy", "lpv", "key", "hi", "yl8", "lo",
                                         "thz", "thy", "thr", "sg1"])}


def rank_program(g, core, T, topo):
    s = T.rank_of(core)
    if s is None:
        return
    others = [r for r in range(4) if r != s]
    order = others + [s]
    Q = {"v": g.vector, "s": g.scalar, "t": g.tensor, "g": g, "y": g.sync}
    waited, lastw, readers, total = {q: {} for q in Q}, {}, {}, {}

    def wait(q, toks):
        need = {}
        for n, val in toks:
            need[n] = max(need.get(n, 0), val)
        for n in sorted(need):
            if waited[q].get(n, 0) < need[n]:
                Q[q].wait_ge(T.sem[n], need[n])
                waited[q][n] = need[n]

    def run(q, fn, rd=(), wr=(), sem=None, free=()):
        toks = []
        for k in rd:
            toks += lastw[k]
        for k in wr:
            if k not in free:
                toks += lastw.get(k, []) + readers.get(k, [])
        wait(q, toks)
        n, inc = (sem, 16) if sem else ("q" + q, 1)
        fn().then_inc(T.sem[n], inc)
        total[n] = total.get(n, 0) + inc
        tok = (n, total[n])
        for k in rd:
            readers.setdefault(k, []).append(tok)
        for k in wr:
            lastw[k] = [tok]
            readers[k] = []

    V, S, P = g.vector, g.scalar, g.tensor

    def vts(out, in0, s1, s2, op0, op1=None, rd=(), wr=()):
        if op1 is None:
            run("v", lambda: V.tensor_scalar(out, in0, s1, None, op0), rd, wr)
        else:
            run("v", lambda: V.tensor_scalar(out, in0, s1, s2, op0, op1), rd, wr)

    def vtt(out, a, b, op, rd=(), wr=()):
        run("v", lambda: V.tensor_tensor(out, a, b, op), rd, wr)

    def vcp(out, in_, rd=(), wr=()):
        run("v", lambda: V.tensor_copy(out, in_), rd, wr)

    def fill(ap, c, *wr):
        run("v", lambda: V.memset(ap, c), (), wr)

    def vred(out, in_, op, rd=(), wr=()):
        run("v", lambda: V.tensor_reduce(out, in_, AxisListType.X, op), rd, wr)

    def vscan(out, d0, d1, init, op0, op1, rd=(), wr=()):
        run("v", lambda: V.tensor_tensor_scan(out, d0, d1, init, op0, op1), rd, wr)

    def vtr(out, in_, rd=(), wr=()):
        run("v", lambda: V.transpose(out, in_), rd, wr)

    def act(out, in_, func, rd=(), wr=(), **kw):
        run("s", lambda: S.activation(out, in_, func, **kw), rd, wr)

    def iota(out, pattern, base, *wr, rd=(), cm=0):
        run("g", lambda: g.iota(out, pattern, base, cm, allow_small_or_imprecise_dtypes=True), rd, wr)

    def select(out, in_, pattern, op, fl, base, cm, rd, wr):
        run("g", lambda: g.affine_select(out, in_, pattern, op, fl, base, cm), rd, wr)

    def sync(out, in_, sem, rd=(), wr=()):
        run("y", lambda: g.sync.dma_start(out, in_), rd, wr, sem=sem)

    def quant(n, a, b, src, rd=(), wr=None):
        run("v", lambda: V.quantize_mx(T[n + "q"][:, a:b], T[n + "p"][:, a:b], src), rd, wr or (n + "q", n + "p"))

    def bank(i, a, b=None):
        return T.psum[:, 512 * i:512 * i + a] if b is None else T.psum[:, 512 * i + a:512 * i + b]

    def mm(i, n, ln, la, rn, ra, start=True, stop=True, rd=None, lrd=None):
        b = "b%d" % i
        run("t", lambda: P.matmul_mx(bank(i, n), T[ln + "q"][:, la:la + 128], T[ln + "p"][:, la:la + 128],
                                     T[rn + "q"][:, ra:ra + n], T[rn + "p"][:, ra:ra + n], start, stop),
            (lrd or (ln + "q", ln + "p")) + (rd or (rn + "q", rn + "p")), (b,), free=() if start else (b,))

    def pickq(dn, c, d, sn, lo, hi, off, rd, wr):
        run("v", lambda: V.tensor_copy(T[dn + "q"][:, c:d].bitcast(dt.uint32),
                                       T[sn + "q"][:, lo:hi].bitcast(dt.uint32).indirect(off)), rd, wr)

    def pickp(dn, c, d, sn, lo, hi, off, rd, wr):
        run("s", lambda: S.activation(T[dn + "p"][:, c:d], T[sn + "p"][:, lo:hi].indirect(off), Act.Copy), rd, wr)

    def tn(n, i=None):
        c = _TINY[n]
        return T.tiny[:, c:c + 2] if i is None else T.tiny[:, c + i:c + i + 1]

    def addr(r):
        rid, pid, _ = topo.addr(T.cores[r])
        return DstId(rid=rid, pnc=pid)

    def msk(es):
        return sum(1 << e for e in es)

    lsum = {"la": 0, "lb": 0}

    def bcast(src, dst, sem, local, rd):
        eng = topo.engines(core, T.cores[others[0]])
        wait("g", [t for k in rd for t in lastw[k]])
        g.remote_dma_fused([RemoteDMATransfer(dst_ids=[addr(r) for r in others], dma_engine_mask=msk(eng),
                                              remote_sem=T.sem[sem], srcs=[src], dsts=[dst] * len(others))],
                           local_sem=T.sem[local])
        lsum[local] += len(eng)

    def scatter(srcs, dst, dests, sem, local, rd, first=0):
        wait("g", [t for k in rd for t in lastw[k]])
        tr = []
        for i, (r, src) in enumerate(zip(dests, srcs)):
            eng = topo.engines(core, T.cores[r])
            j = 4 * ((first + i) % 4)
            tr.append(RemoteDMATransfer(dst_ids=[addr(r)], dma_engine_mask=msk(eng[j:j + 4]), remote_sem=T.sem[sem],
                                        src=src, dst=dst))
        g.remote_dma_fused(tr, local_sem=T.sem[local])
        lsum[local] += 4 * len(tr)

    u8 = dt.uint8

    def cs(j):
        return T.cst[:, j:j + 1]

    D1, D2 = 64, 600
    Z = T.zt[:, D1:D2]

    sync(T.xz[:, 0:128], T.x[:, 0:128], "dxa", (), ("xza",))
    run("s", lambda: S.dma_start(T.xt[:, 0:768], T.x[:, :]), (), ("xt",), sem="dx")
    sync(T.xt[:, 768:1152], T.x[:, 128:512], "dx2", (), ("xt2",))

    run("g", lambda: g.iota(T.pidi[:], [[0, 1]], 0, 1), (), ("pidi",))
    iota(cs(0), [[0, 1]], 0, "c0", cm=1)
    iota(T.rowb[:], [[1, 128]], 0, "rowb")

    fill(T.xz[:, 128:512], 0.0, "xzz")
    run("v", lambda: V.tensor_scalar(T.ui[:], T.pidi[:], 31, None, Op.bitwise_and), ("pidi",), ("ui",))
    fill(Z, 0.0, "zt")
    vcp(cs(2), T.ui[:], ("ui",), ("c2",))
    fill(T.ll[:], 0.0, "ll")
    quant("a", 0, 128, T.xz[:], ("xza", "xzz"))
    at1 = 64 + A * s
    bcast(T.aq[:, 0:A].bitcast(u8), T.kq[:, at1:at1 + A].bitcast(u8), "an", "la", ("aq",))
    bcast(T.ap[:, 0:A], T.kp[:, at1:at1 + A], "an", "la", ("ap",))
    lastw["kq"] = lastw["kp"] = [("an", 96)]
    iota(T.th[:, 0:7], [[0, 7]], 1, "th")
    select(T.th[:, 0:7], T.th[:, 0:7], [[-16, 7]], Op.is_ge, 0.0, -16, 1, ("th",), ("th",))
    sync(T.kq[:, at1:at1 + A].bitcast(u8), T.aq[:, 0:A].bitcast(u8), "dkq", ("aq",), ("kqo",))
    sync(T.kp[:, at1:at1 + A], T.ap[:, 0:A], "dkp", ("ap",), ("kpo",))
    wait("y", [("la", lsum["la"])])
    sync(T.ot[:, 0:536], Z, "dz4", ("zt",), ("otA", "otB", "otC", "otD", "otZ"))
    sync(T.wt[:, :], T.w[:, :], "dw", (), ("wt",))
    sync(T.winq[:, 96:128].bitcast(u8), T.aq[:, 96:128].bitcast(u8), "dzq", ("aq",), ("winqz",))
    sync(T.winp[:, 96:128], T.ap[:, 96:128], "dzp", ("ap",), ("winpz",))
    sync(T.tmt[:, 0:512], T.zt[:, D1:D1 + 512], "dz2", ("zt",), ("tm0",))
    sync(T.tmt[:, 512:688], T.zt[:, D1:D1 + 176], "dz3", ("zt",), ("tm1",))
    sync(T.mh[:, 128:512], T.zt[:, D1:D1 + 384], "dz1", ("zt",), ("mhz",))
    sync(T.vt[:, :], T.v[:, :], "dv", (), ("vt",))
    for i in range(2, 6):
        lastw["tm%d" % i] = list(lastw["tm1"])

    fill(T.et[:], 0.0, "et")
    vts(T.et[:, 3:515:4], T.rowb[:], cs(0), 0.5, Op.is_equal, Op.mult, ("rowb", "c0"), ("et",))
    quant("x", 0, 288, T.xt[:], ("xt", "xt2"))
    for b in range(4):
        quant("e", 128 * b, 128 * b + 128, T.et[:, 3 - b:515 - b], ("et",), ("eq%d" % b, "ep%d" % b))
    act(T.mk[:], T.zt[:, D1:D1 + 96], Act.Copy, ("zt",), ("mk",), bias=1.0)
    act(T.trt[:, 0:512], T.zt[:, D1:D1 + 512], Act.Copy, ("zt",), ("trA",))
    act(T.trt[:, 512:640], T.zt[:, D1:D1 + 128], Act.Copy, ("zt",), ("trB", "trB2"))
    act(T.tri32[:], T.rowb[:, 0:32], Act.Sign, ("rowb", "c2"), ("tri32",), scale=-1.0, bias=cs(2))
    act(T.tri32[:], T.tri32[:], Act.Relu, ("tri32",), ("tri32",), scale=-1.0)
    act(T.jnk[:, 128:135], T.th[:, 0:7], Act.Copy, ("th",), ("jnk1", "c3"), accum_out=cs(3))
    act(cs(1), cs(3), Act.Identity, ("c3", "c0"), ("c1",), scale=-16.0, bias=cs(0))
    act(cs(6), cs(3), Act.Copy, ("c3",), ("c6",), scale=16.0, bias=32.0)
    act(cs(7), cs(3), Act.Copy, ("c3",), ("c7",), scale=16.0, bias=64.0)
    act(cs(8), cs(1), Act.Copy, ("c1",), ("c8",), scale=-1.0)
    act(cs(9), cs(3), Act.Copy, ("c3",), ("c9",), scale=-16.0, bias=-32.0)
    select(T.mk[:], T.mk[:], [[32, 3], [0, 32]], Op.is_ge, 0.0, -96, 1, ("mk",), ("mk",))
    tp = [[-1, 128]]
    select(T.trt[:, 0:512:4], T.trt[:, 0:512:4], tp, Op.is_ge, -1.0, 0, 1, ("trA",), ("trA",))
    select(T.trt[:, 0:512:4], T.trt[:, 0:512:4], tp, Op.not_equal, 32.0, 0, 1, ("trA",), ("trA",))
    iota(T.trt[:, 512:640:4], [[0, 32]], -1, "trB2")
    c = _TINY["yy"]
    iota(T.tiny[:, c:c + 4], [[0, 4]], 0, "yy0", "yy1", "lpv0", "lpv1")
    for a, b in ((0, s), (s, 3), (3, 4)):
        if b > a:
            iota(T.kx[:, 4 * a:4 * b], [[1, b - a], [100, 2], [-100, 2]], order[a], "kx%d" % a)
    kxs = tuple(k for k in ("kx0", "kx%d" % s, "kx3") if k in lastw)
    iota(T.k16[:], [[0, 8], [1, 16], [0, 2]], 0, "k16")
    iota(T.kst[:], [[0, 8], [1, 16], [16, 2]], 1, "kst")
    iota(T.kc[:], [[128, 4], [-1, 2], [64, 2]], 32, "kc")
    h10 = ("h100", "h101")
    iota(T.hot10[:], [[0, 20]], 1, *h10)
    select(T.hot10[:], T.hot10[:], [[32, 2], [-16, 10]], Op.is_ge, 0.0, 0, 1, h10, h10)
    select(T.hot10[:], T.hot10[:], [[-32, 2], [16, 10]], Op.is_ge, 0.0, 15, -1, h10, h10)
    select(T.hot10[:, 10:20], T.hot10[:, 10:20], [[0, 10]], Op.is_ge, 0.0, -96, 1, h10, h10)
    iota(T.colw[:], [[16, 12]], 0, "colw")

    kk = ("kq", "kp", "kqo", "kpo")
    for j in (0, 4, 3, 2, 1):
        mm(j, 128, "x", 32 + 32 * j, "k", 64, rd=kk)
    best = [T.rmax[:, 127:128], T.rmax[:, 255:256]]
    top = {j: (T.m5[:, j:j + 1], "m%d" % j) for j in (2, 3, 4)}
    top[0], top[1] = (best[0], "r0"), (best[1], "r1")

    def lift(j):
        m, k = top[j]
        act(T.a5[:, j:j + 1], m, Act.Abs, (k,), ("a5%d" % j,), scale=EPS, bias=TINY)

    def spread(j, c, mask, mk):
        m, k = top[j]
        act(T.rep[:, c:c + 32], mask, Act.Identity, (mk, k, "a5%d" % j), ("rep%d" % c,), scale=T.a5[:, j:j + 1], bias=m)

    def below(i, dst, a, step):
        end = 128 - (step > 1)
        n = len(range(a, end, step))
        act(T.jnk[:, 128 * i:128 * i + n], T.rmax[:, 128 * i + a:128 * i + end:step], Act.Sign, ("r%d" % i,),
            (dst + str(i), "jnk%d" % i), scale=-1.0, bias=best[i], accum_out=tn(dst, i))

    def scan(i):
        vscan(T.rmax[:, 128 * i:128 * i + 128], bank(i, 128), T.zt[:, D1:D1 + 128], -1e29, Op.max, Op.add,
              ("b%d" % i, "zt"), ("r%d" % i,))

    def count(i):
        c = slice(160 * i, 160 * i + 160)
        act(T.cj[:, c], T.cc[:, c], Act.Copy, ("cc%d" % i,), ("cj%d" % i, "cn%d" % i), scale=1.0 / 64, accum_out=tn("cn", i))

    scan(0)
    lift(0)
    spread(0, 0, T.tri32[:], "tri32")
    below(0, "gg", 0, 1)
    for j in (4, 3, 2):
        vred(top[j][0], bank(j, 128), Op.max, ("b%d" % j,), (top[j][1],))
    act(T.a5[:, 2:5], T.m5[:, 2:5], Act.Abs, ("m2", "m3", "m4"), ("a52", "a53", "a54"), scale=EPS, bias=TINY)
    for j in (4, 3):
        spread(j, 32 * j, T.mk[:, 32 * j - 64:32 * j - 32], "mk")
    scan(1)
    lift(1)
    spread(1, 192, T.tri32[:], "tri32")
    for b in range(4):
        mm(b, 128, "e", 128 * b, "a", 0, True, False, lrd=("eq%d" % b, "ep%d" % b))
    below(1, "gg", 0, 1)
    below(0, "gq", 31, 32)
    below(1, "gq", 31, 32)
    vts(T.rep[:, 160:192], T.mk[:, 0:32], T.a5[:, 0:1], best[0], Op.mult, Op.add, ("mk", "r0", "a50"), ("rep160",))
    vts(T.rep[:, 64:96], T.mk[:, 0:32], T.a5[:, 2:3], top[2][0], Op.mult, Op.add, ("mk", "m2", "a52"), ("rep64",))
    vts(T.rep[:, 32:64], T.rowb[:, 0:32], 0.0, best[1], Op.mult, Op.add, ("rowb", "r1"), ("rep32",))
    vtr(T.mrow[:, 0:160], T.rep[:, 0:160], tuple("rep%d" % c for c in range(0, 160, 32)), ("mrow0",))
    vtr(T.mrow[:, 160:224], T.rep[:, 160:224], ("rep160", "rep192"), ("mrow1",))
    vts(T.cc[:, 0:160], T.mrow[:, 0:160], best[0], None, Op.is_gt, rd=("mrow0", "r0"), wr=("cc0",))
    vts(T.cc[:, 160:320], T.mrow[:, 64:224], best[1], None, Op.is_gt, rd=("mrow0", "mrow1", "r1"), wr=("cc1",))
    count(0)
    count(1)

    def mzb(k, c):
        vts(T.zt[:, 16 * k - 15:16 * k + 16:2], T.kx[:], tn("gq", 1), cs(c), Op.is_equal, Op.mult,
            kxs + ("gq1", "c%d" % c), ("mm%d" % k,))

    vcp(T.trt[96:128, 513:640:4], T.trt[96:128, 384:512:4], ("trA", "trB"), ("trB",))
    quant("tr", 0, 160, T.trt[:], ("trA", "trB", "trB2"))
    for i in range(2):
        vts(T.ot[:, i:512:4], T.rowb[:], tn("gg", i), tn("cn", i), Op.is_equal, Op.is_gt,
            ("rowb", "gg%d" % i, "cn%d" % i), ("ot" + "AB"[i],))
        vts(T.ot[:, 512 + i:528:4], T.rowb[:, 0:4], tn("gq", i), tn("cn", i), Op.is_equal, Op.is_gt,
            ("rowb", "gq%d" % i, "cn%d" % i), ("ot" + "CD"[i],))
        if i == 0:
            mzb(1, 1)
    quant("ob", 0, 134, T.ot[:], ("otA", "otB", "otC", "otD", "otZ"))
    mm(5, 134, "tr", 0, "ob", 0)
    mm(6, 134, "tr", 32, "ob", 0)
    act(T.kab[:], T.kx[:], Act.Abs, kxs + ("gq0",), ("kab",), scale=-1.0, bias=tn("gq", 0))
    act(T.zt[:, 0:32:2], T.kab[:], Act.Relu, ("kab", "c1", "c8"), ("mm0",), scale=cs(8), bias=cs(1))
    act(T.zt[:, 32:64:2], T.kab[:], Act.Relu, ("kab", "c6", "c9"), ("mm2",), scale=cs(9), bias=cs(6))
    mzb(3, 7)
    quant("mm", 0, 136, T.zt[:, 0:544], ("mm0", "mm1", "mm2", "mm3", "zt"))
    below(0, "gd", 15, 16)
    below(1, "gd", 15, 16)
    for i in range(2):
        act(tn("gm", i), tn("gd", i), Act.Identity, ("gd%d" % i, "gg%d" % i), ("gm%d" % i,), scale=-16.0, bias=tn("gg", i))
    act(tn("gd64"), tn("gd"), Act.Copy, ("gd0", "gd1"), ("gd64",), scale=64.0)
    c = _TINY["yy"]
    vred(T.tiny[:, c:c + 1], bank(5, 128, 133), Op.max, ("b5",), ("yy0",))
    vred(T.tiny[96:128, c + 1:c + 2], T.psum[96:128, 6 * 512 + 128:6 * 512 + 133], Op.max, ("b6",), ("yy1",))
    for i in range(2):
        vts(T.stt[:, i:512:2], T.kst[:], tn("yy", i), None, Op.is_equal, rd=("kst", "yy%d" % i), wr=("st%d" % i,))

    def s2(i):
        vts(T.s2t[:, i:512:2], T.k16[:], tn("gm", i), None, Op.is_equal, rd=("k16", "gm%d" % i), wr=("s2%d" % i,))

    s2(0)
    quant("st", 0, 128, T.stt[:], ("st0", "st1"))
    s2(1)
    mm(7, 128, "st", 0, "mm", 0, True, False)
    mm(7, 128, "st", 0, "mm", 8, False, True)
    y2 = ("yy0", "yy1")
    act(tn("thy"), tn("yy"), Act.Sign, y2, ("thy",))
    c = _TINY["lpv"]
    act(T.jnk[:, 0:128], bank(5, 128), Act.Relu, ("b5", "yy0"), ("lpv0", "jnk0"), accum_out=T.tiny[:, c:c + 1])
    act(T.jnk[96:128, 128:256], T.psum[96:128, 6 * 512:6 * 512 + 128], Act.Relu, ("b6", "yy1"), ("lpv1", "jnk1"),
        accum_out=T.tiny[96:128, c + 1:c + 2])
    act(tn("sg1"), tn("yy"), Act.Sign, y2, ("sg1",), bias=-16.5)
    act(tn("yl8"), tn("yy"), Act.Copy, y2, ("yl8",), bias=-8.0)
    for i in range(2):
        act(tn("key", i), tn("lpv", i), Act.Identity, ("lpv%d" % i, "thy", "gd64"), ("key%d" % i,),
            scale=tn("thy", i), bias=tn("gd64", i))
    act(tn("hi"), tn("sg1"), Act.Copy, ("sg1",), ("hi",), scale=8.0, bias=32.0 * (3 - s) + 8.0)
    for i in range(2):
        act(tn("lo", i), tn("sg1", i), Act.Identity, ("sg1", "yl8"), ("lo%d" % i,), scale=-8.0, bias=tn("yl8", i))
    quant("s2", 0, 128, T.s2t[:], ("s20", "s21"))
    for i in range(2):
        vts(T.zt[:, D2 + 2 + i:D2 + 64:4], T.kc[:], tn("key", i), tn("hi", i), Op.is_equal, Op.mult,
            ("kc", "key%d" % i, "hi"), ("m2%d" % (2 + i),))
    for i in range(2):
        vts(T.zt[:, D2 + i:D2 + 64:4], T.kc[:], tn("key", i), tn("lo", i), Op.is_equal, Op.mult,
            ("kc", "key%d" % i, "lo%d" % i), ("m2%d" % i,))
    vcp(T.invu[:], bank(7, 8), ("b7",), ("invu",))
    quant("m2", 0, 128, T.zt[:, D2 + 64 - 512:D2 + 64], ("zt", "m20", "m21", "m22", "m23"))
    mm(4, 128, "s2", 0, "m2", 0)
    pickq("sl", 0, 96, "x", 0, 192, T.invu[:, 0:6], ("xq", "invu"), ("slq",))
    pickp("sl", 0, 96, "x", 0, 192, T.invu[:, 0:6], ("xp", "invu"), ("slp",))
    at = 128 + 32 * (3 - s)
    vcp(T.lst[:], bank(4, 112, 128), ("b4",), ("lst",))
    scatter([T.lst[:, 4 * r:4 * r + 4] for r in others], T.ll[:, 8 * s:8 * s + 4], others, "li", "lb", ("lst",), 3)
    scatter([T.slq[:, 32 * i:32 * i + 32].bitcast(u8) for i in range(3)], T.winq[:, at:at + 32].bitcast(u8), others,
            "so", "lb", ("slq",), 0)
    scatter([T.slp[:, 32 * i:32 * i + 32] for i in range(3)], T.winp[:, at:at + 32], others, "so", "lb", ("slp",), 2)
    lastw["winq"] = lastw["winp"] = [("so", 24)]
    lastw["lli"] = [("li", 12)]
    if s < 3:
        act(T.nz[:], T.lst[:], Act.Sign, ("lst",), ("nz",))
    pickp("win", at, at + 32, "x", 0, 192, T.invu[:, 6:8], ("xp", "invu"), ("winpo",))
    act(tn("thz"), tn("lpv"), Act.Relu, ("lpv0", "lpv1"), ("thz",), scale=2.0, bias=-60.0)
    act(tn("gd16"), tn("gd"), Act.Copy, ("gd0", "gd1"), ("gd16",), scale=16.0)
    for i in range(2):
        act(tn("thr", i), tn("thz", i), Act.Copy, ("thz", "thy"), ("thr%d" % i,), scale=tn("thy", i))
    for i in range(2):
        hj = T.hot10[:, 10 * i:10 * i + 10]
        act(T.tmt[:, 640 + i:680:4], hj, Act.Copy, ("h10%d" % i, "gm%d" % i), ("tm%d" % (2 + i),), scale=tn("gm", i))
        act(T.tmt[:, 642 + i:680:4], hj, Act.Copy, ("h10%d" % i, "gd16"), ("tm%d" % (4 + i),), scale=tn("gd16", i))
    act(T.tmt[:, 0:512:4], T.et[:, 3:515:4], Act.Copy, ("et", "thr0"), ("tm0",), scale=tn("thr", 0))
    act(T.tmt[:, 513:640:4], T.et[:, 387:515:4], Act.Copy, ("et", "thr1"), ("tm1",), scale=tn("thr", 1))
    act(T.colw[:], T.colw[:], Act.Identity, ("colw", "c1"), ("colw",), bias=cs(1))
    HB = (5, 6, 7, 4)

    def hot(i):
        act(T.hot[:, i:768:4], bank(HB[i], 192), Act.Relu, ("b%d" % HB[i],), ("hot%d" % i,), scale=0.0625)

    for i in (0, 3, 1, 2):
        quant("w", 128 * i, 128 * i + 128, T.wt[:, 512 * i:512 * i + 512], ("wt",), ("wq%d" % i, "wp%d" % i))
        mm(HB[i], 192, "w", 128 * i, "x", 0, lrd=("wq%d" % i, "wp%d" % i))
        if i == 3 and s < 3:
            for h in range(2):
                vtt(T.csum[:, h:8:2], T.nz[:, h:16:4], T.nz[:, 2 + h:16:4], Op.add, ("nz",), ("csum%d" % h,))
            higher = [r for r in others if r > s]
            scatter([T.csum[:, 0:8]] * len(higher), T.lc[:, 8 * s:8 * s + 8], higher, "ct", "lb", ("csum0", "csum1"), 1)
    vcp(T.ll[:, 8 * s:8 * s + 4], T.lst[:, 4 * s:4 * s + 4], ("lst", "ll"), ("llo",))
    pickq("win", at, at + 32, "x", 0, 192, T.invu[:, 6:8], ("xq", "invu"), ("winqo",))
    hot(0)
    hot(3)
    act(T.colm[:], T.colw[:], Act.Copy, ("colw",), ("colm",), bias=-192.0)
    iota(T.rst[:], [[0, 160]], 1, "rst")
    select(T.rst[:], T.rst[:], [[0, 10], [1, 16]], Op.not_equal, 0.0, 0, 0, ("rst",), ("rst",))
    iota(T.mgt[:, 0:192], [[0, 192]], -1, "mgta")
    iota(T.mgt[:, 192:320], [[192, 4], [1, 32]], 0, "mgtb")
    iota(T.mgr[:, 0:32], [[0, 32]], -1, "mgr0")

    L, X = T.ll, T.lab
    rl = ("ll", "llo", "lli")
    vtt(X[:, 0:32:2], L[:, 0:16], L[:, 16:32], Op.max, rl, ("lab0",))
    vtt(X[:, 1:32:2], L[:, 0:16], L[:, 16:32], Op.min, rl, ("lab1",))
    vtt(T.lu[:], X[:, 0:16], X[:, 16:32], Op.max, ("lab0", "lab1"), ("lu",))
    vtt(T.lcm[:], X[:, 0:4:2], X[:, 16:20:2], Op.min, ("lab0",), ("lcm",))
    vtt(T.lf[:], T.lu[:, 1:4:2], T.lu[:, 4:8:2], Op.max, ("lu",), ("lf",))
    vts(T.off[:, 0:2], T.lu[:, 0:4:2], 127.0, None, Op.add, rd=("lu",), wr=("off0",))
    for h in range(2):
        vts(T.off[:, 2 + h:3 + h], T.lcm[:, h:h + 1], T.lf[:, h:h + 1], 127.0, Op.max, Op.add, ("lcm", "lf"), ("off%d" % (1 + h),))

    def ww(c):
        return ("win" + c, "win" + c + "o", "win" + c + "z", "off0", "off1", "off2")
    pickq("k", 0, 64, "win", 0, 256, T.off[:, 0:4], ww("q"), ("kqf",))
    pickp("k", 0, 64, "win", 0, 256, T.off[:, 0:4], ww("p"), ("kpf",))
    for b in range(4):
        mm(b, 128, "e", 128 * b, "k", 0, False, True, rd=kk + ("kqf", "kpf"), lrd=("eq%d" % b, "ep%d" % b))
    hot(1)
    if s > 0:
        lastw["lc"] = [("ct", 4 * s)]
    for i in range(2):
        vts(T.s3t[:, i:512:2], T.k16[:], cs(1), None, Op.is_equal, rd=("k16", "c1"), wr=("s3%d" % i,))
    quant("tm", 0, 172, T.tmt[:], tuple("tm%d" % i for i in range(6)))
    quant("s3", 0, 128, T.s3t[:], ("s30", "s31"))
    vcp(T.colu[:], T.colw[:], ("colw",), ("colu",))
    mm(5, 128, "s3", 0, "tm", 44)
    mm(4, 160, "s3", 0, "tm", 0)
    for b in range(4):
        act(T.ss[:, 32 * b:32 * b + 32], bank(b, 32, 64), Act.Copy, ("b%d" % b,), ("ss%d" % b,))
    for b in range(4):
        vtt(T.mh[:, b:128:4], T.ss[:, 32 * b:32 * b + 32], bank(b, 32), Op.add, ("ss%d" % b, "b%d" % b), ("mt%d" % b,))
    quant("m", 0, 128, T.mh[:, 0:512], ("mt0", "mt1", "mt2", "mt3", "mhz"))
    for i in range(4):
        mm(i, 128, "w", 128 * i, "m", 0, lrd=("wq%d" % i, "wp%d" % i))
    vcp(T.gwu[:], bank(5, 116, 126), ("b5",), ("gwu",))
    if s > 0:
        src, key = T.lc[:, 0:8], "lc"
        for r in range(1, s):
            vtt(T.ctot[:], src, T.lc[:, 8 * r:8 * r + 8], Op.add, ("lc", key), ("ctot",))
            src, key = T.ctot[:], "ctot"
        vcp(T.cu[:], src, (key,), ("cu",))
        act(T.crow[:], T.rowb[:, 0:128].indirect(T.cu[:, 0:8]), Act.Copy, ("rowb", "cu"), ("crow",))
    vtt(T.dw[:], bank(5, 116, 126), T.colm[:, 2:12], Op.subtract, ("b5", "colm"), ("dw",))
    vts(T.hot[:, 2:768:4], bank(HB[2], 192), 0.0, 0.0625, Op.max, Op.mult, ("b%d" % HB[2],), ("hot2",))
    for i in range(4):
        k = ("b%d" % i,), ("hmt%d" % i,)
        if i % 2 == 0:
            act(T.mh[:, 512 + i:640:4], bank(i, 32), Act.Relu, k[0], k[1], scale=0.0625)
        else:
            vts(T.mh[:, 512 + i:640:4], bank(i, 32), 0.0, 0.0625, Op.max, Op.mult, k[0], k[1])
    if s > 0:
        act(T.prior[:], T.crow[:, 0:128].indirect(T.gwu[:, 0:10]), Act.Copy, ("crow", "gwu"), ("prior",))
    quant("hm", 0, 128, T.mh[:, 128:640], ("mhz", "hmt0", "hmt1", "hmt2", "hmt3"))
    hat = 192 + A * s
    bcast(T.hmq[:, 96:128].bitcast(u8), T.hwq[:, hat:hat + A].bitcast(u8), "hm", "lb", ("hmq",))
    bcast(T.hmp[:, 96:128], T.hwp[:, hat:hat + A], "hm", "lb", ("hmp",))
    lastw["hwq"] = lastw["hwp"] = [("hm", 96)]
    pickp("hw", hat, hat + A, "hm", 96, 128, T.colu[:, 0:2], ("hmp", "colu"), ("hwpm",))

    quant("hw", 0, 192, T.hot[:], ("hot0", "hot1", "hot2", "hot3"), ("hwqo", "hwpo"))
    if s > 0:
        vtt(T.adm[:], T.prior[:], bank(4, 160), Op.is_lt, ("prior", "b4"), ("adm",))
    else:
        vts(T.adm[:], bank(4, 160), 0.0, None, Op.is_gt, rd=("b4",), wr=("adm",))
    vts(T.fm[:], T.lu[:, 0:4:2], 0.0, 192.0 + A * s, Op.is_gt, Op.mult, ("lu",), ("fm",))
    vscan(T.scn[:], T.rst[:], T.adm[:], 0.0, Op.mult, Op.add, ("rst", "adm"), ("scn",))
    vtt(T.fin[:, 0:2], T.fm[:], T.colw[:, 0:2], Op.add, ("fm", "colw"), ("fin0",))
    vtt(T.admt[:], T.scn[:, 15:160:16], T.dw[:], Op.mult, ("scn", "dw"), ("admt",))
    vtt(T.fin[:, 2:12], T.admt[:], T.colw[:, 2:12], Op.add, ("admt", "colw"), ("fin1",))
    pickq("hw", hat, hat + A, "hm", 96, 128, T.colu[:, 0:2], ("hmq", "colu"), ("hwqm",))
    vcp(T.finu[:], T.fin[:], ("fin0", "fin1"), ("finu",))
    quant("v", 0, 128, T.vt[:], ("vt",))

    def hh(c):
        return ("hw" + c, "hw" + c + "m", "hw" + c + "o", "finu")
    for i, (a, b) in enumerate([(0, 128), (128, 192)]):
        pickq("fo", a, b, "hw", 0, 320, T.finu[:, a // 16:b // 16], hh("q"), ("foq%d" % i,))
        pickp("fo", a, b, "hw", 0, 320, T.finu[:, a // 16:b // 16], hh("p"), ("fop%d" % i,))
    sync(T.oc[:, 0:768], T.foq[:, 0:192].bitcast(u8), "dout", ("foq0", "foq1"))
    for k in range(4):
        sync(T.osc[4 * k:4 * k + 4, 0:192], T.fop[32 * k:32 * k + 4, 0:192], "dout", ("fop0", "fop1"))
    mm(6, 128, "v", 0, "fo", 0, rd=("foq0", "fop0"))
    mm(7, 128, "v", 0, "fo", 64, rd=("foq0", "fop0", "foq1", "fop1"))
    act(T.mgr[:, 32:192], T.mgt[:, 0:320].indirect(T.finu[:, 2:12]), Act.Copy, ("mgta", "mgtb", "finu"), ("mgr1",))
    run("s", lambda: S.dma_start(T.mg[0:1, 0:192], T.mgr[0:1, 0:192]), ("mgr0", "mgr1"), (), sem="dout")
    vcp(T.yo[:, 0:128], bank(6, 128), ("b6",), ("yo0",))
    sync(T.y[:, 0:128], T.yo[:, 0:128], "dout", ("yo0",))
    vcp(T.yo[:, 128:192], bank(7, 64, 128), ("b7",), ("yo1",))
    sync(T.y[:, 128:192], T.yo[:, 128:192], "dout", ("yo1",))
    wait("g", [(n, total[n]) for n in ("qv", "qs", "qt", "qg", "dout")] + [("lb", lsum["lb"])])
